import numpy as np
import ml_dtypes


def mxq(x, axis, fmt="e4m3"):
    dtype, down = {"e4m3": (ml_dtypes.float8_e4m3fn, 7), "e5m2": (ml_dtypes.float8_e5m2, 14)}[fmt]
    v = np.moveaxis(np.asarray(x, np.float32).astype(ml_dtypes.bfloat16).astype(np.float64), axis, -1)
    blocks = v.reshape(v.shape[:-1] + (-1, 32))
    amax = np.abs(blocks).max(-1, keepdims=True)
    byte = np.maximum(np.where(amax > 0, np.frexp(amax)[1] - 1 + 127, 0) - down, 1)
    scale = np.exp2(byte - 127.0)
    codes = (blocks / scale).astype(np.float32).astype(dtype).astype(np.float64)
    return np.moveaxis((codes * scale).reshape(v.shape), -1, axis)


WIDE = False


def mx_kscale(k):
    if not WIDE:
        return np.ones(k)
    levels = np.array([10, -10, 5, -5, 0])
    if k % 512:
        return np.exp2(np.random.permutation(np.resize(levels, k // 32))).repeat(32)
    a = np.empty((k // 512, 16))
    for p in range(k // 512):
        a[p, :8] = np.random.permutation(np.resize(levels, 8))
        for g in range(8):
            far = levels[np.abs(levels - a[p, g]) >= 10]
            a[p, g + 8] = far[np.random.randint(len(far))]
    return np.exp2(a.ravel()).repeat(32)


def f64(x):
    return np.asarray(x).astype(np.float64)


def striped(idx):
    return np.tile(idx.reshape(-1, 16).T, (8, 1)).astype(np.uint16)


def unstriped(offs):
    return offs[:16].T.reshape(-1).astype(np.int64)


E2M1 = np.array([0.0, 0.5, 1.0, 1.5, 2.0, 3.0, 4.0, 6.0, -0.0, -0.5, -1.0, -1.5, -2.0, -3.0, -4.0, -6.0])


def pack_weight(w, fmt):
    k, n = w.shape
    w = f64(np.asarray(w, np.float32).astype(ml_dtypes.bfloat16)).reshape(k // 32, 32, n)
    amax = np.abs(w).max(1)
    if fmt == "e4m3":
        byte = np.frexp(amax)[1] - 1 + 127 - 7
    else:
        mant, ex = np.frexp(amax / 6.0)
        byte = np.where(mant > 0.5, ex, ex - 1) + 127
    byte = np.clip(np.where(amax > 0, byte, 1), 1, 254)
    scaled = (w * np.exp2(127.0 - byte)[:, None, :]).reshape(k, n).astype(np.float32)
    by_word = np.ascontiguousarray(scaled.reshape(k // 512, 128, 4, n).transpose(0, 1, 3, 2))
    if fmt == "e4m3":
        words = by_word.astype(ml_dtypes.float8_e4m3fn).view(np.uint8)
    else:
        c = by_word.astype(ml_dtypes.float4_e2m1fn).view(np.uint8) & 0xF
        words = (c[..., 0::2] | (c[..., 1::2] << 4)).reshape(k // 512, 128, 2 * n)
    return np.ascontiguousarray(words), np.ascontiguousarray(byte.astype(np.uint8).reshape(k // 512, 16, n))


def unpack_weight(words, scales, fmt):
    g, _, n = scales.shape
    words = np.ascontiguousarray(words).reshape(g, 128, n, -1)
    if fmt == "e4m3":
        vals = words.view(ml_dtypes.float8_e4m3fn).astype(np.float64)
    else:
        nib = np.empty((g, 128, n, 4), np.uint8)
        nib[..., 0::2] = words & 0xF
        nib[..., 1::2] = words >> 4
        vals = E2M1[nib]
    vals = vals * np.repeat(np.exp2(scales.astype(np.float64) - 127.0), 8, axis=1)[..., None]
    return vals.transpose(0, 1, 3, 2).reshape(g * 512, n)


def gelu(v):
    return 0.5 * v * (1.0 + np.tanh(np.sqrt(2.0 / np.pi) * (v + 0.044715 * v**3)))


K, K2, T, S, H, N, T2 = 512, 1024, 2048, 512, 1024, 512, 1024

def setup_inputs():
    n = np.random.standard_normal
    s = mx_kscale(K)[:, None]
    s2 = mx_kscale(K2)[:, None]
    u = mx_kscale(H)[:, None]
    tab_words, tab_scales = pack_weight(n((K, T)) * s, "e4m3")
    tab2_words, tab2_scales = pack_weight(n((K2, T)) * s2, "e4m3")
    w1_words, w1_scales = pack_weight(n((K, H)) / np.sqrt(K) / s, "e2m1")
    w3_words, w3_scales = pack_weight(n((K2, H)) / np.sqrt(K2) / s2, "e4m3")
    perm = np.random.permutation(T2)
    return {
        "tab_words": tab_words, "tab_scales": tab_scales,
        "tab2_words": tab2_words, "tab2_scales": tab2_scales,
        "offs": striped(np.random.permutation(T)[:S]),
        "offs2": striped(np.random.permutation(T)[:S]),
        "offs3": striped(perm[:S]), "offs4": striped(perm[S:]),
        "w1_words": w1_words, "w1_scales": w1_scales,
        "w2": (n((K2, H)) / np.sqrt(K2) / s2 * u.T).astype(np.float32),
        "w3_words": w3_words, "w3_scales": w3_scales,
        "gain": (np.exp(0.3 * n(H)) * u[:, 0]).astype(np.float32),
        "wg1": np.exp(0.3 * n((128, S))).astype(np.float32),
        "wg2": np.exp(0.3 * n((128, S))).astype(np.float32),
        "bias": (0.5 * n(H) * u[:, 0]).astype(np.float32),
        "w4": (n((H, N)) / np.sqrt(H) / u).astype(np.float32),
    }

def reference(tab_words, tab_scales, tab2_words, tab2_scales, offs, offs2, offs3, offs4,
              w1_words, w1_scales, w2, w3_words, w3_scales, gain, wg1, wg2, bias, w4):
    v = unpack_weight(tab_words, tab_scales, "e4m3")[:, unstriped(offs)]
    v2 = unpack_weight(tab2_words, tab2_scales, "e4m3")[:, unstriped(offs2)]
    h1 = f64(gain)[:, None] * np.tanh(unpack_weight(w1_words, w1_scales, "e2m1").T @ v)
    h2 = (mxq(f64(w2), 0, "e4m3").T @ v2) * (unpack_weight(w3_words, w3_scales, "e4m3").T @ v2)
    page = np.zeros((H, T2))
    page[:, unstriped(offs3)] = np.tile(f64(wg1), (H // 128, 1)) * h1
    page[:, unstriped(offs4)] = np.tile(f64(wg2), (H // 128, 1)) * h2
    z = page + f64(bias)[:, None]
    return mxq(f64(w4), 0, "e4m3").T @ mxq(z, 0, "e4m3")

@@ -1,0 +1,270 @@
+from contextlib import ExitStack
+
+import concourse.mybir as mybir
+
+K, K2, T, S, H, N, T2 = 512, 1024, 2048, 512, 1024, 512, 1024
+FLOPS = 2 * (K * H * S + 2 * K2 * H * S + H * N * T2)
+
+F32 = mybir.dt.float32
+BF16 = mybir.dt.bfloat16
+I32 = mybir.dt.int32
+U32 = mybir.dt.uint32
+U16 = mybir.dt.uint16
+U8 = mybir.dt.uint8
+FP8X4 = mybir.dt.float8_e4m3fn_x4
+FP4X4 = mybir.dt.float4_e2m1fn_x4
+ACT = mybir.ActivationFunctionType
+MULT = mybir.AluOpType.mult
+
+P = 128
+PACK = 4
+K_PASS = P * PACK
+QUAD = 32
+PAGES = H // P
+CHUNK = 256
+
+
+def tile_list_grain_boundary_segregation_kernel(
+    tc, tab_words, tab_scales, tab2_words, tab2_scales, offs, offs2, offs3, offs4,
+    w1_words, w1_scales, w2, w3_words, w3_scales, gain, wg1, wg2, bias, w4, out,
+):
+    nc = tc.nc
+    with ExitStack() as ctx:
+        lists = ctx.enter_context(tc.tile_pool(name="lists", bufs=1))
+        keep = ctx.enter_context(tc.tile_pool(name="keep", bufs=1))
+        psum = ctx.enter_context(tc.psum_pool(name="psum", bufs=1))
+
+        def held(shape, dtype, name, tag=None):
+            return keep.tile(shape, dtype, name=name, tag=tag or name, align_bytes=64)
+
+        def bank(index, name):
+            return psum.tile([P, 512], F32, name=name, tag="bank%d" % (index % 8))
+
+        def load_list(source, name):
+            tile = lists.tile([P, S // 16], U16, name=name)
+            nc.sync.dma_start(tile[:], source)
+            return tile
+
+        def load_words(source, columns, name):
+            tile = held([P, columns], I32, name)
+            nc.sync.dma_start(tile[:], source.rearrange("p c i -> p (c i)").bitcast(I32))
+            return tile
+
+        def load_scale_rows(queue, plane, first_row, source):
+            passes = source.shape[0]
+            for q in range(4):
+                rows = slice(QUAD * q + first_row, QUAD * q + first_row + 4 * passes)
+                queue.dma_start(plane[rows, :], source[:, 4 * q : 4 * q + 4, :].bitcast(I32))
+
+        def load_scale_quadrant(queue, plane, q, source):
+            rows = source[0, 4 * q : 4 * q + 4, :].bitcast(I32)
+            queue.dma_start(plane[QUAD * q : QUAD * (q + 1), :], rows.unsqueeze(0).to_broadcast([8, 4, rows.shape[1]]))
+
+        def load_site_weights(source, slots, name):
+            tile = held([P, len(slots), S], F32, name)
+            rows = source.rearrange("(q t) j -> q t j", t=PACK)[:, slots.start : slots.stop, :]
+            for q in range(4):
+                nc.sync.dma_start(tile[QUAD * q : QUAD * (q + 1)], rows)
+            return [tile[:, t, :] for t in range(len(slots))]
+
+        def load_rows(source, name, slot):
+            tile = held([P, PACK, 512], F32, name, tag="raw%d" % slot)
+            nc.sync.dma_start(tile[:], source.rearrange("(p j) c -> p j c", j=PACK))
+            return tile
+
+        def reorder_columns(dst, src, line):
+            nc.vector.tensor_copy(
+                dst.rearrange("p (b t m i) -> p b m t i", b=2, t=PACK, i=line),
+                src.rearrange("p (b m i t) -> p b m t i", b=2, t=PACK, i=line),
+            )
+
+        def quantize(grouped, columns, name):
+            codes = held([P, columns], U32, name + "_codes")
+            scales = held([P, columns], U8, name + "_scales")
+            nc.vector.quantize_mx(out=codes[:].bitcast(FP8X4), scales=scales[:], in_=grouped)
+            return codes, scales
+
+        tab_plane = held([P, T // 4], I32, "tab_plane")
+        w1_plane = held([P, H // 4], I32, "w1_plane")
+        w3_plane = held([P, H // 4], I32, "w3_plane")
+        tab2_plane = held([P, T // 4], I32, "tab2_plane")
+        warm = held([P, 8], F32, "warm")
+        nc.vector.memset(warm[:], 0.0)
+        for plane in (tab2_plane, w3_plane):
+            nc.vector.memset(plane[:], 0)
+
+        idx1 = load_list(offs, "idx1")
+        for q in range(4):
+            load_scale_quadrant(nc.scalar, tab_plane, q, tab_scales)
+        w1_sb = held([P, H // 2], I32, "w1_sb")
+        nc.sync.dma_start(w1_sb[:], w1_words[0].bitcast(I32))
+        load_scale_quadrant(nc.sync, w1_plane, 0, w1_scales)
+        tab_sb = load_words(tab_words[0], T, "tab_sb")
+        for q in range(1, 4):
+            load_scale_quadrant(nc.sync, w1_plane, q, w1_scales)
+        warm_out = held([P, 8], F32, "warm_out")
+        nc.scalar.activation(warm_out[:], warm[:], ACT.Tanh)
+        gain_sb = held([P, 2, PACK], F32, "gain_sb")
+        nc.gpsimd.dma_start(gain_sb[:], gain.rearrange("(b p t) -> p b t", b=2, t=PACK))
+        bias_sb = held([P, 2, PACK], F32, "bias_sb")
+        nc.gpsimd.dma_start(bias_sb[:], bias.rearrange("(b p t) -> p b t", b=2, t=PACK))
+        wg1_sb = load_site_weights(wg1, range(0, 1), "wg1_first")
+        idx3 = load_list(offs3, "idx3")
+        wg1_sb = wg1_sb + load_site_weights(wg1, range(1, PACK), "wg1_rest")
+        idx2 = load_list(offs2, "idx2")
+        load_scale_rows(nc.sync, tab2_plane, 0, tab2_scales)
+        load_scale_rows(nc.sync, w3_plane, 0, w3_scales)
+        tab2_sb = [load_words(tab2_words[a], T, "tab2_sb%d" % a) for a in range(2)]
+        w3_sb = [load_words(w3_words[a], H, "w3_sb%d" % a) for a in range(2)]
+        w2_raw = {}
+        for a in range(2):
+            w2_raw[a, 0] = load_rows(w2[K_PASS * a : K_PASS * (a + 1), 0:512], "w2_raw%d0" % a, a)
+        wg2_sb = load_site_weights(wg2, range(PACK), "wg2_sb")
+        idx4 = load_list(offs4, "idx4")
+        for a in range(2):
+            w2_raw[a, 1] = load_rows(w2[K_PASS * a : K_PASS * (a + 1), 512:1024], "w2_raw%d1" % a, 2 + a)
+
+        w1_ord = held([P, 2 * H], U8, "w1_ord")
+        reorder_columns(w1_ord[:].bitcast(U16), w1_sb[:].bitcast(U16), 8)
+        v_scales = held([P, S], U8, "v_scales")
+        nc.vector.tensor_copy(v_scales[:], tab_plane[:].bitcast(U8).indirect(idx1[:]))
+        w1_sc = held([P, H], U8, "w1_sc")
+        reorder_columns(w1_sc[:], w1_plane[:].bitcast(U8), 16)
+        v_words = held([P, S], U32, "v_words")
+        nc.vector.tensor_copy(v_words[:], tab_sb[:].bitcast(U32).indirect(idx1[:]))
+
+        pages = [held([P, T2], F32, "page%d" % i) for i in range(PAGES)]
+        for i in range(PAGES):
+            b, t = divmod(i, PACK)
+            cols = slice(P * i, P * (i + 1))
+            acc = bank(i, "h1_acc%d" % i)
+            nc.tensor.matmul_mx(
+                out=acc[:], lhsT=w1_ord[:, 2 * P * i : 2 * P * (i + 1)].bitcast(FP4X4), lhsT_scale=w1_sc[:, cols],
+                rhs=v_words[:].bitcast(FP8X4), rhs_scale=v_scales[:], start=True, stop=True,
+            )
+            response = held([P, S], F32, "response%d" % i, tag="left%d" % i)
+            nc.scalar.activation(response[:], acc[:], ACT.Tanh)
+            weight = held([P, S], F32, "weight%d" % i, tag="right%d" % i)
+            nc.scalar.activation(weight[:], wg1_sb[t], ACT.Copy, scale=gain_sb[:, b, t : t + 1])
+            nc.vector.tensor_tensor(pages[i][:].indirect(idx3[:]), response[:], weight[:], MULT)
+
+        v2_words = []
+        for a in range(2):
+            words = held([P, S], U32, "v2_words%d" % a)
+            nc.vector.tensor_copy(words[:], tab2_sb[a][:].bitcast(U32).indirect(idx2[:]))
+            v2_words.append(words)
+        v2_scales = held([P, S], U8, "v2_scales")
+        nc.vector.tensor_copy(v2_scales[:], tab2_plane[:].bitcast(U8).indirect(idx2[:]))
+        w3_sc = held([P, H], U8, "w3_sc")
+        reorder_columns(w3_sc[:], w3_plane[:].bitcast(U8), 16)
+        w3_ord = []
+        for a in range(2):
+            ordered = held([P, H], U32, "w3_ord%d" % a)
+            reorder_columns(ordered[:], w3_sb[a][:].bitcast(U32), 4)
+            w3_ord.append(ordered)
+
+        w2_q = {}
+        for b in range(2):
+            for a in range(2):
+                grouped = held([P, PACK * 512], BF16, "w2_grouped%d%d" % (a, b))
+                nc.scalar.copy(
+                    grouped[:].rearrange("p (t m j) -> p m t j", t=PACK, j=PACK),
+                    w2_raw[a, b][:].rearrange("p j (m t) -> p m t j", t=PACK),
+                )
+                w2_q[a, b] = quantize(grouped[:], 512, "w2_%d%d" % (a, b))
+
+        w4_q = {}
+        for a in range(2):
+            raw = load_rows(w4[K_PASS * a : K_PASS * (a + 1), :], "w4_raw%d" % a, a)
+            for g in range(2):
+                grouped = held([P, PACK * 2 * P], BF16, "w4_grouped%d%d" % (a, g), tag="right%d" % (2 * a + g))
+                nc.scalar.copy(
+                    grouped[:].rearrange("p (c i j) -> p c j i", i=4, j=PACK),
+                    raw[:, :, 2 * P * g : 2 * P * (g + 1)].rearrange("p j (c i) -> p c j i", i=4),
+                )
+                w4_q[a, g] = quantize(grouped[:], 2 * P, "w4_%d%d" % (a, g))
+
+        def product(acc, operands):
+            for a, (codes, scales) in enumerate(operands):
+                nc.tensor.matmul_mx(
+                    out=acc[:], lhsT=codes.bitcast(FP8X4), lhsT_scale=scales,
+                    rhs=v2_words[a][:].bitcast(FP8X4), rhs_scale=v2_scales[4 * a :, :],
+                    start=a == 0, stop=a == 1,
+                )
+
+        first = [held([P, PACK, S], F32, "first%d" % b, tag="raw%d" % (1 - b)) for b in range(2)]
+        second = {}
+
+        def w2_product(i):
+            b, t = divmod(i, PACK)
+            cols = slice(P * t, P * (t + 1))
+            acc = bank(i % 4, "w2_acc%d" % i)
+            product(acc, [(w2_q[a, b][0][:, cols], w2_q[a, b][1][:, cols]) for a in range(2)])
+            nc.scalar.copy(first[b][:, t, :], acc[:])
+
+        def w3_product(i):
+            cols = slice(P * i, P * (i + 1))
+            acc = bank(4 + i % 4, "w3_acc%d" % i)
+            product(acc, [(w3_ord[a][:, cols], w3_sc[4 * a :, cols]) for a in range(2)])
+            second[i] = held([P, S], F32, "second%d" % i, tag="left%d" % (i % 3))
+            nc.vector.tensor_tensor(second[i][:], acc[:], wg2_sb[i % PACK], MULT)
+
+        z = [held([P, T2, PACK], BF16, "z%d" % b) for b in range(2)]
+
+        def add_bias(i, cols):
+            b, t = divmod(i, PACK)
+            nc.scalar.activation(z[b][:, cols, t], pages[i][:, cols], ACT.Identity, bias=bias_sb[:, b, t : t + 1])
+
+        chunks = [slice(c, c + CHUNK) for c in range(0, T2, CHUNK)]
+        z_q = {}
+
+        def quantize_z(b, c):
+            z_q[b, c] = quantize(z[b][:, chunks[c], :].rearrange("p c j -> p (c j)"), CHUNK, "z%d%d" % (b, c))
+
+        w3_product(0)
+        w3_product(1)
+        for i in range(PAGES):
+            w2_product(i)
+        for i in range(PAGES):
+            nc.vector.tensor_tensor(pages[i][:].indirect(idx4[:]), first[i // PACK][:, i % PACK, :], second[i][:], MULT)
+            if i + 2 < PAGES:
+                w3_product(i + 2)
+            if i < PAGES - 1:
+                add_bias(i, slice(0, T2))
+            if i == PACK - 1:
+                for c in range(len(chunks)):
+                    quantize_z(0, c)
+
+        accs = {}
+
+        def reader_pass(b, c, g):
+            if b == 0:
+                accs[c, g] = bank(2 * c + g, "out_acc%d%d" % (c, g))
+            w_codes, w_sc = w4_q[b, g]
+            z_codes, z_sc = z_q[b, c]
+            for h in range(2):
+                n_cols = slice(P * h, P * (h + 1))
+                nc.tensor.matmul_mx(
+                    out=accs[c, g][:, CHUNK * h : CHUNK * (h + 1)], lhsT=w_codes[:, n_cols].bitcast(FP8X4),
+                    lhsT_scale=w_sc[:, n_cols], rhs=z_codes[:].bitcast(FP8X4), rhs_scale=z_sc[:],
+                    start=b == 0 and h == 0, stop=b == 1 and h == 1,
+                )
+
+        for c in range(len(chunks)):
+            for g in range(2):
+                reader_pass(0, c, g)
+        out_rows = out.rearrange("(g h p) t -> g p h t", h=2, p=P)
+        for c in range(len(chunks)):
+            add_bias(PAGES - 1, chunks[c])
+        for c in range(len(chunks)):
+            quantize_z(1, c)
+        for c in range(len(chunks)):
+            for g in range(2):
+                reader_pass(1, c, g)
+                result = held([P, 2, CHUNK], F32, "result%d%d" % (c, g), tag="right%d" % (2 * c + g))
+                flat = result[:].rearrange("p h t -> p (h t)")
+                if c == 0 or g == 1:
+                    nc.vector.tensor_copy(flat, accs[c, g][:])
+                else:
+                    nc.scalar.copy(flat, accs[c, g][:])
+                nc.sync.dma_start(out_rows[g][:, :, chunks[c]], result[:])

@@ -45,26 +45,28 @@ def tile_list_grain_boundary_segregation_kernel(
             nc.sync.dma_start(tile[:], source)
             return tile
 
+        def entries(idx, part):
+            return idx[:, part.start // 16 : part.stop // 16]
+
         def load_words(source, columns, name):
             tile = held([P, columns], I32, name)
             nc.sync.dma_start(tile[:], source.rearrange("p c i -> p (c i)").bitcast(I32))
             return tile
 
-        def load_scale_rows(queue, plane, first_row, source):
-            passes = source.shape[0]
-            for q in range(4):
-                rows = slice(QUAD * q + first_row, QUAD * q + first_row + 4 * passes)
-                queue.dma_start(plane[rows, :], source[:, 4 * q : 4 * q + 4, :].bitcast(I32))
+        def load_scale_rows(plane, source, quadrants):
+            for q in quadrants:
+                nc.sync.dma_start(plane[QUAD * q : QUAD * q + 8, :], source[:, 4 * q : 4 * q + 4, :].bitcast(I32))
 
         def load_scale_quadrant(queue, plane, q, source):
             rows = source[0, 4 * q : 4 * q + 4, :].bitcast(I32)
             queue.dma_start(plane[QUAD * q : QUAD * (q + 1), :], rows.unsqueeze(0).to_broadcast([8, 4, rows.shape[1]]))
 
-        def load_site_weights(source, slots, name):
-            tile = held([P, len(slots), S], F32, name)
+        def load_site_weights(source, slots, name, tag=None, last_queue=nc.sync):
+            tile = held([P, len(slots), S], F32, name, tag=tag)
             rows = source.rearrange("(q t) j -> q t j", t=PACK)[:, slots.start : slots.stop, :]
             for q in range(4):
-                nc.sync.dma_start(tile[QUAD * q : QUAD * (q + 1)], rows)
+                queue = last_queue if q == 3 else nc.sync
+                queue.dma_start(tile[QUAD * q : QUAD * (q + 1)], rows)
             return [tile[:, t, :] for t in range(len(slots))]
 
         def load_rows(source, name, slot):
@@ -74,8 +76,8 @@ def tile_list_grain_boundary_segregation_kernel(
 
         def reorder_columns(dst, src, line):
             nc.vector.tensor_copy(
-                dst.rearrange("p (b t m i) -> p b m t i", b=2, t=PACK, i=line),
-                src.rearrange("p (b m i t) -> p b m t i", b=2, t=PACK, i=line),
+                dst.rearrange("p (b t m i) -> p b m t i", t=PACK, m=P // line, i=line),
+                src.rearrange("p (b m i t) -> p b m t i", t=PACK, m=P // line, i=line),
             )
 
         def quantize(grouped, columns, name):
@@ -95,7 +97,7 @@ def tile_list_grain_boundary_segregation_kernel(
 
         idx1 = load_list(offs, "idx1")
         for q in range(4):
-            load_scale_quadrant(nc.scalar, tab_plane, q, tab_scales)
+            load_scale_quadrant(nc.sync, tab_plane, q, tab_scales)
         w1_sb = held([P, H // 2], I32, "w1_sb")
         nc.sync.dma_start(w1_sb[:], w1_words[0].bitcast(I32))
         load_scale_quadrant(nc.sync, w1_plane, 0, w1_scales)
@@ -104,49 +106,76 @@ def tile_list_grain_boundary_segregation_kernel(
             load_scale_quadrant(nc.sync, w1_plane, q, w1_scales)
         warm_out = held([P, 8], F32, "warm_out")
         nc.scalar.activation(warm_out[:], warm[:], ACT.Tanh)
+        idx3 = load_list(offs3, "idx3")
+        wg1_sb = load_site_weights(wg1, range(0, 1), "wg1_first", last_queue=nc.gpsimd)
         gain_sb = held([P, 2, PACK], F32, "gain_sb")
         nc.gpsimd.dma_start(gain_sb[:], gain.rearrange("(b p t) -> p b t", b=2, t=PACK))
-        bias_sb = held([P, 2, PACK], F32, "bias_sb")
-        nc.gpsimd.dma_start(bias_sb[:], bias.rearrange("(b p t) -> p b t", b=2, t=PACK))
-        wg1_sb = load_site_weights(wg1, range(0, 1), "wg1_first")
-        idx3 = load_list(offs3, "idx3")
-        wg1_sb = wg1_sb + load_site_weights(wg1, range(1, PACK), "wg1_rest")
-        idx2 = load_list(offs2, "idx2")
-        load_scale_rows(nc.sync, tab2_plane, 0, tab2_scales)
-        load_scale_rows(nc.sync, w3_plane, 0, w3_scales)
-        tab2_sb = [load_words(tab2_words[a], T, "tab2_sb%d" % a) for a in range(2)]
-        w3_sb = [load_words(w3_words[a], H, "w3_sb%d" % a) for a in range(2)]
+        wg1_sb = wg1_sb + load_site_weights(wg1, range(1, PACK), "wg1_rest", tag="site_weights")
         w2_raw = {}
-        for a in range(2):
-            w2_raw[a, 0] = load_rows(w2[K_PASS * a : K_PASS * (a + 1), 0:512], "w2_raw%d0" % a, a)
-        wg2_sb = load_site_weights(wg2, range(PACK), "wg2_sb")
+
+        def load_w2(b):
+            for a in range(2):
+                rows = w2[K_PASS * a : K_PASS * (a + 1), 512 * b : 512 * (b + 1)]
+                w2_raw[a, b] = load_rows(rows, "w2_raw%d%d" % (a, b), 2 * b + a)
+
+        load_w2(0)
+        load_scale_rows(tab2_plane, tab2_scales, range(4))
+        load_w2(1)
+        load_scale_rows(w3_plane, w3_scales, range(4))
+        idx2 = load_list(offs2, "idx2")
+        tab2_sb = [load_words(tab2_words[a], T, "tab2_sb%d" % a) for a in range(2)]
+        bias_sb = held([P, 2, PACK], F32, "bias_sb")
+        nc.sync.dma_start(bias_sb[:], bias.rearrange("(b p t) -> p b t", b=2, t=PACK))
+        w3_sb = [load_words(w3_words[a], H, "w3_sb%d" % a) for a in range(2)]
         idx4 = load_list(offs4, "idx4")
-        for a in range(2):
-            w2_raw[a, 1] = load_rows(w2[K_PASS * a : K_PASS * (a + 1), 512:1024], "w2_raw%d1" % a, 2 + a)
 
         w1_ord = held([P, 2 * H], U8, "w1_ord")
         reorder_columns(w1_ord[:].bitcast(U16), w1_sb[:].bitcast(U16), 8)
         v_scales = held([P, S], U8, "v_scales")
         nc.vector.tensor_copy(v_scales[:], tab_plane[:].bitcast(U8).indirect(idx1[:]))
         w1_sc = held([P, H], U8, "w1_sc")
-        reorder_columns(w1_sc[:], w1_plane[:].bitcast(U8), 16)
         v_words = held([P, S], U32, "v_words")
-        nc.vector.tensor_copy(v_words[:], tab_sb[:].bitcast(U32).indirect(idx1[:]))
+        halves = [slice(0, S // 2), slice(S // 2, S)]
+        for b, part in enumerate(halves):
+            cols = slice(512 * b, 512 * (b + 1))
+            reorder_columns(w1_sc[:, cols], w1_plane[:].bitcast(U8)[:, cols], 16)
+            nc.vector.tensor_copy(v_words[:, part], tab_sb[:].bitcast(U32).indirect(entries(idx1, part)))
 
         pages = [held([P, T2], F32, "page%d" % i) for i in range(PAGES)]
-        for i in range(PAGES):
-            b, t = divmod(i, PACK)
-            cols = slice(P * i, P * (i + 1))
-            acc = bank(i, "h1_acc%d" % i)
-            nc.tensor.matmul_mx(
-                out=acc[:], lhsT=w1_ord[:, 2 * P * i : 2 * P * (i + 1)].bitcast(FP4X4), lhsT_scale=w1_sc[:, cols],
-                rhs=v_words[:].bitcast(FP8X4), rhs_scale=v_scales[:], start=True, stop=True,
-            )
-            response = held([P, S], F32, "response%d" % i, tag="left%d" % i)
-            nc.scalar.activation(response[:], acc[:], ACT.Tanh)
-            weight = held([P, S], F32, "weight%d" % i, tag="right%d" % i)
-            nc.scalar.activation(weight[:], wg1_sb[t], ACT.Copy, scale=gain_sb[:, b, t : t + 1])
-            nc.vector.tensor_tensor(pages[i][:].indirect(idx3[:]), response[:], weight[:], MULT)
+
+        def bulk_page(step, parts):
+            t, b = divmod(step, 2)
+            i = PACK * b + t
+            response = held([P, S], F32, "response%d" % i, tag="left%d" % step)
+            h1 = held([P, S], F32, "h1_%d" % i, tag="right%d" % step)
+            for n, part in enumerate(parts):
+                acc = bank(step + 7 * n, "h1_acc%d_%d" % (i, n))
+                nc.tensor.matmul_mx(
+                    out=acc[:, part], lhsT=w1_ord[:, 2 * P * i : 2 * P * (i + 1)].bitcast(FP4X4),
+                    lhsT_scale=w1_sc[:, P * i : P * (i + 1)],
+                    rhs=v_words[:, part].bitcast(FP8X4), rhs_scale=v_scales[:, part], start=True, stop=True,
+                )
+                nc.scalar.activation(response[:, part], acc[:, part], ACT.Tanh)
+                nc.scalar.activation(h1[:, part], response[:, part], ACT.Copy, scale=gain_sb[:, b, t : t + 1])
+                nc.vector.tensor_tensor(pages[i][:].indirect(entries(idx3, part)), h1[:, part], wg1_sb[t][:, part], MULT)
+
+        w2_q = {}
+
+        def quantize_w2(b):
+            for a in range(2):
+                grouped = held([P, PACK * 512], BF16, "w2_grouped%d%d" % (a, b))
+                nc.scalar.copy(
+                    grouped[:].rearrange("p (t m j) -> p m t j", t=PACK, j=PACK),
+                    w2_raw[a, b][:].rearrange("p j (m t) -> p m t j", t=PACK),
+                )
+                w2_q[a, b] = quantize(grouped[:], 512, "w2_%d%d" % (a, b))
+
+        bulk_page(0, halves)
+        for i in range(1, 5):
+            bulk_page(i, [slice(0, S)])
+        quantize_w2(0)
+        for i in range(5, PAGES):
+            bulk_page(i, [slice(0, S)])
 
         v2_words = []
         for a in range(2):
@@ -163,15 +192,7 @@ def tile_list_grain_boundary_segregation_kernel(
             reorder_columns(ordered[:], w3_sb[a][:].bitcast(U32), 4)
             w3_ord.append(ordered)
 
-        w2_q = {}
-        for b in range(2):
-            for a in range(2):
-                grouped = held([P, PACK * 512], BF16, "w2_grouped%d%d" % (a, b))
-                nc.scalar.copy(
-                    grouped[:].rearrange("p (t m j) -> p m t j", t=PACK, j=PACK),
-                    w2_raw[a, b][:].rearrange("p j (m t) -> p m t j", t=PACK),
-                )
-                w2_q[a, b] = quantize(grouped[:], 512, "w2_%d%d" % (a, b))
+        quantize_w2(1)
 
         w4_q = {}
         for a in range(2):
@@ -184,6 +205,8 @@ def tile_list_grain_boundary_segregation_kernel(
                 )
                 w4_q[a, g] = quantize(grouped[:], 2 * P, "w4_%d%d" % (a, g))
 
+        wg2_sb = load_site_weights(wg2, range(PACK), "wg2_sb", tag="site_weights")
+
         def product(acc, operands):
             for a, (codes, scales) in enumerate(operands):
                 nc.tensor.matmul_mx(
@@ -195,45 +218,65 @@ def tile_list_grain_boundary_segregation_kernel(
         first = [held([P, PACK, S], F32, "first%d" % b, tag="raw%d" % (1 - b)) for b in range(2)]
         second = {}
 
-        def w2_product(i):
-            b, t = divmod(i, PACK)
-            cols = slice(P * t, P * (t + 1))
-            acc = bank(i % 4, "w2_acc%d" % i)
-            product(acc, [(w2_q[a, b][0][:, cols], w2_q[a, b][1][:, cols]) for a in range(2)])
-            nc.scalar.copy(first[b][:, t, :], acc[:])
+        order = [0, 1, 2, 6, 3, 4, 5, 7]
 
-        def w3_product(i):
+        def w2_product(step):
+            b, t = divmod(order[step], PACK)
+            cols = slice(P * t, P * (t + 1))
+            acc = bank(step % 4, "w2_acc%d" % step)
+            product(acc, [(w2_q[a, b][0][:, cols], w2_q[a, b][1][:, cols]) for a in range(2)])
+            nc.scalar.copy(first[step // PACK][:, step % PACK, :], acc[:])
+
+        def w3_product(step):
+            i = order[step]
             cols = slice(P * i, P * (i + 1))
-            acc = bank(4 + i % 4, "w3_acc%d" % i)
+            acc = bank(4 + step % 4, "w3_acc%d" % i)
             product(acc, [(w3_ord[a][:, cols], w3_sc[4 * a :, cols]) for a in range(2)])
-            second[i] = held([P, S], F32, "second%d" % i, tag="left%d" % (i % 3))
-            nc.vector.tensor_tensor(second[i][:], acc[:], wg2_sb[i % PACK], MULT)
+            return acc
+
+        def weigh(step, acc, part, tag):
+            weighed = held([P, part.stop - part.start], F32, "second%d_%d" % (step, part.start), tag=tag)
+            nc.vector.tensor_tensor(weighed[:], acc[:, part], wg2_sb[order[step] % PACK][:, part], MULT)
+            return weighed
+
+        def scatter(step, part, weighed):
+            window = pages[order[step]][:].indirect(entries(idx4, part))
+            nc.vector.tensor_tensor(window, first[step // PACK][:, step % PACK, part], weighed[:], MULT)
 
         z = [held([P, T2, PACK], BF16, "z%d" % b) for b in range(2)]
-
-        def add_bias(i, cols):
-            b, t = divmod(i, PACK)
-            nc.scalar.activation(z[b][:, cols, t], pages[i][:, cols], ACT.Identity, bias=bias_sb[:, b, t : t + 1])
-
         chunks = [slice(c, c + CHUNK) for c in range(0, T2, CHUNK)]
         z_q = {}
 
         def quantize_z(b, c):
             z_q[b, c] = quantize(z[b][:, chunks[c], :].rearrange("p c j -> p (c j)"), CHUNK, "z%d%d" % (b, c))
 
-        w3_product(0)
-        w3_product(1)
-        for i in range(PAGES):
-            w2_product(i)
-        for i in range(PAGES):
-            nc.vector.tensor_tensor(pages[i][:].indirect(idx4[:]), first[i // PACK][:, i % PACK, :], second[i][:], MULT)
-            if i + 2 < PAGES:
-                w3_product(i + 2)
-            if i < PAGES - 1:
-                add_bias(i, slice(0, T2))
-            if i == PACK - 1:
-                for c in range(len(chunks)):
-                    quantize_z(0, c)
+        whole = slice(0, S)
+        last = PAGES - 1
+        early, late = slice(0, S // 4), slice(S // 4, S)
+        for step in range(2):
+            second[step] = weigh(step, w3_product(step), whole, "left%d" % step)
+        for step in range(PAGES):
+            w2_product(step)
+        for step, i in enumerate(order[:last]):
+            b, t = divmod(i, PACK)
+            scatter(step, whole, second[step])
+            nc.scalar.activation(z[b][:, :, t], pages[i][:], ACT.Identity, bias=bias_sb[:, b, t : t + 1])
+            if step + 2 < last:
+                second[step + 2] = weigh(step + 2, w3_product(step + 2), whole, "left%d" % ((step + 2) % 3))
+            if step + 2 == last:
+                last_acc = w3_product(last)
+                second[last] = weigh(last, last_acc, early, "left%d" % (last % 3))
+        scatter(last, early, second[last])
+        z0_codes = held([P, T2], U32, "z0_codes", tag="left%d" % (last % 3))
+        z0_scales = held([P, T2], U8, "z0_scales")
+        for cols in (slice(0, T2 // 2), slice(T2 // 2, T2)):
+            nc.vector.quantize_mx(
+                out=z0_codes[:, cols].bitcast(FP8X4), scales=z0_scales[:, cols],
+                in_=z[0][:, cols, :].rearrange("p c j -> p (c j)"),
+            )
+        for c in range(len(chunks)):
+            z_q[0, c] = (z0_codes[:, chunks[c]], z0_scales[:, chunks[c]])
+        scatter(last, late, weigh(last, last_acc, late, "z0"))
 
         accs = {}
 
@@ -246,7 +289,7 @@ def tile_list_grain_boundary_segregation_kernel(
                 n_cols = slice(P * h, P * (h + 1))
                 nc.tensor.matmul_mx(
                     out=accs[c, g][:, CHUNK * h : CHUNK * (h + 1)], lhsT=w_codes[:, n_cols].bitcast(FP8X4),
-                    lhsT_scale=w_sc[:, n_cols], rhs=z_codes[:].bitcast(FP8X4), rhs_scale=z_sc[:],
+                    lhsT_scale=w_sc[:, n_cols], rhs=z_codes[:, :].bitcast(FP8X4), rhs_scale=z_sc[:, :],
                     start=b == 0 and h == 0, stop=b == 1 and h == 1,
                 )
 
@@ -254,16 +297,21 @@ def tile_list_grain_boundary_segregation_kernel(
             for g in range(2):
                 reader_pass(0, c, g)
         out_rows = out.rearrange("(g h p) t -> g p h t", h=2, p=P)
+
+        def last_bias(c):
+            nc.vector.tensor_scalar_add(z[1][:, chunks[c], PACK - 1], pages[-1][:, chunks[c]], bias_sb[:, 1, PACK - 1 : PACK])
+
+        last_bias(0)
         for c in range(len(chunks)):
-            add_bias(PAGES - 1, chunks[c])
-        for c in range(len(chunks)):
+            if c + 1 < len(chunks):
+                last_bias(c + 1)
             quantize_z(1, c)
         for c in range(len(chunks)):
             for g in range(2):
                 reader_pass(1, c, g)
                 result = held([P, 2, CHUNK], F32, "result%d%d" % (c, g), tag="right%d" % (2 * c + g))
                 flat = result[:].rearrange("p h t -> p (h t)")
-                if c == 0 or g == 1:
+                if c > 0 and g == 1:
                     nc.vector.tensor_copy(flat, accs[c, g][:])
                 else:
                     nc.scalar.copy(flat, accs[c, g][:])

@@ -90,8 +90,6 @@ def tile_list_grain_boundary_segregation_kernel(
         w1_plane = held([P, H // 4], I32, "w1_plane")
         w3_plane = held([P, H // 4], I32, "w3_plane")
         tab2_plane = held([P, T // 4], I32, "tab2_plane")
-        warm = held([P, 8], F32, "warm")
-        nc.vector.memset(warm[:], 0.0)
         for plane in (tab2_plane, w3_plane):
             nc.vector.memset(plane[:], 0)
 
@@ -104,13 +102,11 @@ def tile_list_grain_boundary_segregation_kernel(
         tab_sb = load_words(tab_words[0], T, "tab_sb")
         for q in range(1, 4):
             load_scale_quadrant(nc.sync, w1_plane, q, w1_scales)
-        warm_out = held([P, 8], F32, "warm_out")
-        nc.scalar.activation(warm_out[:], warm[:], ACT.Tanh)
         idx3 = load_list(offs3, "idx3")
         wg1_sb = load_site_weights(wg1, range(0, 1), "wg1_first", last_queue=nc.gpsimd)
         gain_sb = held([P, 2, PACK], F32, "gain_sb")
         nc.gpsimd.dma_start(gain_sb[:], gain.rearrange("(b p t) -> p b t", b=2, t=PACK))
-        wg1_sb = wg1_sb + load_site_weights(wg1, range(1, PACK), "wg1_rest", tag="site_weights")
+        wg1_sb = wg1_sb + load_site_weights(wg1, range(1, PACK), "wg1_rest")
         w2_raw = {}
 
         def load_w2(b):
@@ -171,11 +167,9 @@ def tile_list_grain_boundary_segregation_kernel(
                 w2_q[a, b] = quantize(grouped[:], 512, "w2_%d%d" % (a, b))
 
         bulk_page(0, halves)
-        for i in range(1, 5):
-            bulk_page(i, [slice(0, S)])
+        for step in range(1, PAGES):
+            bulk_page(step, [slice(0, S)])
         quantize_w2(0)
-        for i in range(5, PAGES):
-            bulk_page(i, [slice(0, S)])
 
         v2_words = []
         for a in range(2):
@@ -205,7 +199,7 @@ def tile_list_grain_boundary_segregation_kernel(
                 )
                 w4_q[a, g] = quantize(grouped[:], 2 * P, "w4_%d%d" % (a, g))
 
-        wg2_sb = load_site_weights(wg2, range(PACK), "wg2_sb", tag="site_weights")
+        wg2_sb = load_site_weights(wg2, range(PACK), "wg2_sb")
 
         def product(acc, operands):
             for a, (codes, scales) in enumerate(operands):
@@ -298,20 +292,19 @@ def tile_list_grain_boundary_segregation_kernel(
                 reader_pass(0, c, g)
         out_rows = out.rearrange("(g h p) t -> g p h t", h=2, p=P)
 
-        def last_bias(c):
-            nc.vector.tensor_scalar_add(z[1][:, chunks[c], PACK - 1], pages[-1][:, chunks[c]], bias_sb[:, 1, PACK - 1 : PACK])
-
-        last_bias(0)
+        last_bias = bias_sb[:, 1, PACK - 1 : PACK]
+        for cols in chunks[:2]:
+            nc.vector.tensor_scalar_add(z[1][:, cols, PACK - 1], pages[-1][:, cols], last_bias)
+        for cols in chunks[2:]:
+            nc.scalar.activation(z[1][:, cols, PACK - 1], pages[-1][:, cols], ACT.Identity, bias=last_bias)
         for c in range(len(chunks)):
-            if c + 1 < len(chunks):
-                last_bias(c + 1)
             quantize_z(1, c)
         for c in range(len(chunks)):
             for g in range(2):
                 reader_pass(1, c, g)
                 result = held([P, 2, CHUNK], F32, "result%d%d" % (c, g), tag="right%d" % (2 * c + g))
                 flat = result[:].rearrange("p h t -> p (h t)")
-                if c > 0 and g == 1:
+                if g == 1:
                     nc.vector.tensor_copy(flat, accs[c, g][:])
                 else:
                     nc.scalar.copy(flat, accs[c, g][:])

@@ -116,32 +116,38 @@ def tile_list_grain_boundary_segregation_kernel(
 
         load_w2(0)
         load_scale_rows(tab2_plane, tab2_scales, range(4))
-        load_w2(1)
         load_scale_rows(w3_plane, w3_scales, range(4))
         idx2 = load_list(offs2, "idx2")
         tab2_sb = [load_words(tab2_words[a], T, "tab2_sb%d" % a) for a in range(2)]
+        w3_sb = [load_words(w3_words[a], H, "w3_sb%d" % a) for a in range(2)]
+        load_w2(1)
         bias_sb = held([P, 2, PACK], F32, "bias_sb")
         nc.sync.dma_start(bias_sb[:], bias.rearrange("(b p t) -> p b t", b=2, t=PACK))
-        w3_sb = [load_words(w3_words[a], H, "w3_sb%d" % a) for a in range(2)]
         idx4 = load_list(offs4, "idx4")
 
         w1_ord = held([P, 2 * H], U8, "w1_ord")
-        reorder_columns(w1_ord[:].bitcast(U16), w1_sb[:].bitcast(U16), 8)
         v_scales = held([P, S], U8, "v_scales")
-        nc.vector.tensor_copy(v_scales[:], tab_plane[:].bitcast(U8).indirect(idx1[:]))
         w1_sc = held([P, H], U8, "w1_sc")
         v_words = held([P, S], U32, "v_words")
         halves = [slice(0, S // 2), slice(S // 2, S)]
-        for b, part in enumerate(halves):
-            cols = slice(512 * b, 512 * (b + 1))
-            reorder_columns(w1_sc[:, cols], w1_plane[:].bitcast(U8)[:, cols], 16)
-            nc.vector.tensor_copy(v_words[:, part], tab_sb[:].bitcast(U32).indirect(entries(idx1, part)))
 
-        pages = [held([P, T2], F32, "page%d" % i) for i in range(PAGES)]
+        def order_w1(b):
+            cols = slice(512 * b, 512 * (b + 1))
+            reorder_columns(w1_ord[:].bitcast(U16)[:, cols], w1_sb[:].bitcast(U16)[:, cols], 8)
+            reorder_columns(w1_sc[:, cols], w1_plane[:].bitcast(U8)[:, cols], 16)
+
+        nc.vector.tensor_copy(v_scales[:], tab_plane[:].bitcast(U8).indirect(idx1[:]))
+        order_w1(0)
+        for part in halves:
+            nc.vector.tensor_copy(v_words[:, part], tab_sb[:].bitcast(U32).indirect(entries(idx1, part)))
+        order_w1(1)
+
+        pages = {}
 
         def bulk_page(step, parts):
             t, b = divmod(step, 2)
             i = PACK * b + t
+            pages[i] = held([P, T2], F32, "page%d" % i, tag="tab2_sb%d" % b if step >= 6 else None)
             response = held([P, S], F32, "response%d" % i, tag="left%d" % step)
             h1 = held([P, S], F32, "h1_%d" % i, tag="right%d" % step)
             for n, part in enumerate(parts):
@@ -153,7 +159,8 @@ def tile_list_grain_boundary_segregation_kernel(
                 )
                 nc.scalar.activation(response[:, part], acc[:, part], ACT.Tanh)
                 nc.scalar.activation(h1[:, part], response[:, part], ACT.Copy, scale=gain_sb[:, b, t : t + 1])
-                nc.vector.tensor_tensor(pages[i][:].indirect(entries(idx3, part)), h1[:, part], wg1_sb[t][:, part], MULT)
+                nc.gpsimd.tensor_tensor(response[:, part], h1[:, part], wg1_sb[t][:, part], MULT)
+                nc.vector.tensor_copy(pages[i][:].indirect(entries(idx3, part)), response[:, part])
 
         w2_q = {}
 
@@ -166,121 +173,118 @@ def tile_list_grain_boundary_segregation_kernel(
                 )
                 w2_q[a, b] = quantize(grouped[:], 512, "w2_%d%d" % (a, b))
 
+        whole = slice(0, S)
         bulk_page(0, halves)
-        for step in range(1, PAGES):
-            bulk_page(step, [slice(0, S)])
+        for step in range(1, 4):
+            bulk_page(step, [whole])
         quantize_w2(0)
+        for step in range(4, 6):
+            bulk_page(step, [whole])
 
-        v2_words = []
-        for a in range(2):
-            words = held([P, S], U32, "v2_words%d" % a)
-            nc.vector.tensor_copy(words[:], tab2_sb[a][:].bitcast(U32).indirect(idx2[:]))
-            v2_words.append(words)
         v2_scales = held([P, S], U8, "v2_scales")
         nc.vector.tensor_copy(v2_scales[:], tab2_plane[:].bitcast(U8).indirect(idx2[:]))
         w3_sc = held([P, H], U8, "w3_sc")
         reorder_columns(w3_sc[:], w3_plane[:].bitcast(U8), 16)
-        w3_ord = []
+        w3_ord = held([P, 2 * H], U32, "w3_ord")
         for a in range(2):
-            ordered = held([P, H], U32, "w3_ord%d" % a)
-            reorder_columns(ordered[:], w3_sb[a][:].bitcast(U32), 4)
-            w3_ord.append(ordered)
+            reorder_columns(w3_ord[:, H * a : H * (a + 1)], w3_sb[a][:].bitcast(U32), 4)
 
         quantize_w2(1)
 
         w4_q = {}
         for a in range(2):
             raw = load_rows(w4[K_PASS * a : K_PASS * (a + 1), :], "w4_raw%d" % a, a)
-            for g in range(2):
-                grouped = held([P, PACK * 2 * P], BF16, "w4_grouped%d%d" % (a, g), tag="right%d" % (2 * a + g))
-                nc.scalar.copy(
-                    grouped[:].rearrange("p (c i j) -> p c j i", i=4, j=PACK),
-                    raw[:, :, 2 * P * g : 2 * P * (g + 1)].rearrange("p j (c i) -> p c j i", i=4),
-                )
-                w4_q[a, g] = quantize(grouped[:], 2 * P, "w4_%d%d" % (a, g))
+            grouped = held([P, PACK * 512], BF16, "w4_grouped%d" % a)
+            nc.scalar.copy(
+                grouped[:].rearrange("p (c i j) -> p c j i", i=4, j=PACK),
+                raw[:].rearrange("p j (c i) -> p c j i", i=4),
+            )
+            w4_q[a] = quantize(grouped[:], 512, "w4_%d" % a)
 
         wg2_sb = load_site_weights(wg2, range(PACK), "wg2_sb")
+
+        v2_words = held([P, 2 * S], U32, "v2_words", tag="raw1")
+        for a in range(2):
+            nc.vector.tensor_copy(v2_words[:, S * a : S * (a + 1)], tab2_sb[a][:].bitcast(U32).indirect(idx2[:]))
+
+        for step in range(6, PAGES):
+            bulk_page(step, [whole])
 
         def product(acc, operands):
             for a, (codes, scales) in enumerate(operands):
                 nc.tensor.matmul_mx(
                     out=acc[:], lhsT=codes.bitcast(FP8X4), lhsT_scale=scales,
-                    rhs=v2_words[a][:].bitcast(FP8X4), rhs_scale=v2_scales[4 * a :, :],
+                    rhs=v2_words[:, S * a : S * (a + 1)].bitcast(FP8X4), rhs_scale=v2_scales[4 * a :, :],
                     start=a == 0, stop=a == 1,
                 )
 
-        first = [held([P, PACK, S], F32, "first%d" % b, tag="raw%d" % (1 - b)) for b in range(2)]
-        second = {}
-
-        order = [0, 1, 2, 6, 3, 4, 5, 7]
-
-        def w2_product(step):
-            b, t = divmod(order[step], PACK)
+        first = [held([P, PACK, S], F32, "first%d" % b, tag="raw%d" % (2 + b)) for b in range(2)]
+        second = [held([P, PACK, S], F32, "second%d" % b, tag=("raw0", "tab_sb")[b]) for b in range(2)]
+        last = PAGES - 1
+        order = [0, 6, 1, 2, 3, 4, 5, 7]
+        weighed = []
+        for step, i in enumerate(order):
+            b, t = divmod(i, PACK)
             cols = slice(P * t, P * (t + 1))
-            acc = bank(step % 4, "w2_acc%d" % step)
+            acc = bank(2 * step, "w2_acc%d" % i)
             product(acc, [(w2_q[a, b][0][:, cols], w2_q[a, b][1][:, cols]) for a in range(2)])
-            nc.scalar.copy(first[step // PACK][:, step % PACK, :], acc[:])
-
-        def w3_product(step):
-            i = order[step]
+            nc.scalar.copy(first[b][:, t, :], acc[:])
             cols = slice(P * i, P * (i + 1))
-            acc = bank(4 + step % 4, "w3_acc%d" % i)
-            product(acc, [(w3_ord[a][:, cols], w3_sc[4 * a :, cols]) for a in range(2)])
-            return acc
+            acc = bank(2 * step + 1, "w3_acc%d" % i)
+            product(acc, [(w3_ord[:, H * a + P * i : H * a + P * (i + 1)], w3_sc[4 * a :, cols]) for a in range(2)])
+            nc.scalar.copy(second[b][:, t, :], acc[:])
+            h2 = held([P, S], F32, "h2_%d" % i, tag="h2_%d" % (step % 2))
+            nc.gpsimd.tensor_tensor(h2[:], first[b][:, t, :], second[b][:, t, :], MULT)
+            if step == last:
+                late_product = (h2, wg2_sb[t])
+                continue
+            ready = held([P, S], F32, "ready%d" % i, tag="right%d" % step)
+            nc.gpsimd.tensor_tensor(ready[:], h2[:], wg2_sb[t], MULT)
+            weighed.append(ready)
 
-        def weigh(step, acc, part, tag):
-            weighed = held([P, part.stop - part.start], F32, "second%d_%d" % (step, part.start), tag=tag)
-            nc.vector.tensor_tensor(weighed[:], acc[:, part], wg2_sb[order[step] % PACK][:, part], MULT)
-            return weighed
-
-        def scatter(step, part, weighed):
-            window = pages[order[step]][:].indirect(entries(idx4, part))
-            nc.vector.tensor_tensor(window, first[step // PACK][:, step % PACK, part], weighed[:], MULT)
-
-        z = [held([P, T2, PACK], BF16, "z%d" % b) for b in range(2)]
+        pairs = held([P, 2, T2, 2], BF16, "pairs", tag="w3_ord")
+        z0 = [held([P, T2 // 2, PACK], BF16, "z0_%d" % n) for n in range(2)]
+        z1 = held([P, T2, PACK], BF16, "z1")
         chunks = [slice(c, c + CHUNK) for c in range(0, T2, CHUNK)]
         z_q = {}
 
-        def quantize_z(b, c):
-            z_q[b, c] = quantize(z[b][:, chunks[c], :].rearrange("p c j -> p (c j)"), CHUNK, "z%d%d" % (b, c))
+        def quantize_z0(n, tag):
+            codes = held([P, T2 // 2], U32, "z0_codes%d" % n, tag=tag)
+            scales = held([P, T2 // 2], U8, "z0_scales%d" % n)
+            nc.vector.quantize_mx(
+                out=codes[:].bitcast(FP8X4), scales=scales[:], in_=z0[n][:].rearrange("p c j -> p (c j)"),
+            )
+            for c in range(2):
+                z_q[0, 2 * n + c] = (codes[:, chunks[c]], scales[:, chunks[c]])
 
-        whole = slice(0, S)
-        last = PAGES - 1
-        early, late = slice(0, S // 4), slice(S // 4, S)
-        for step in range(2):
-            second[step] = weigh(step, w3_product(step), whole, "left%d" % step)
-        for step in range(PAGES):
-            w2_product(step)
         for step, i in enumerate(order[:last]):
             b, t = divmod(i, PACK)
-            scatter(step, whole, second[step])
-            nc.scalar.activation(z[b][:, :, t], pages[i][:], ACT.Identity, bias=bias_sb[:, b, t : t + 1])
-            if step + 2 < last:
-                second[step + 2] = weigh(step + 2, w3_product(step + 2), whole, "left%d" % ((step + 2) % 3))
-            if step + 2 == last:
-                last_acc = w3_product(last)
-                second[last] = weigh(last, last_acc, early, "left%d" % (last % 3))
-        scatter(last, early, second[last])
-        z0_codes = held([P, T2], U32, "z0_codes", tag="left%d" % (last % 3))
-        z0_scales = held([P, T2], U8, "z0_scales")
-        for cols in (slice(0, T2 // 2), slice(T2 // 2, T2)):
-            nc.vector.quantize_mx(
-                out=z0_codes[:, cols].bitcast(FP8X4), scales=z0_scales[:, cols],
-                in_=z[0][:, cols, :].rearrange("p c j -> p (c j)"),
-            )
-        for c in range(len(chunks)):
-            z_q[0, c] = (z0_codes[:, chunks[c]], z0_scales[:, chunks[c]])
-        scatter(last, late, weigh(last, last_acc, late, "z0"))
+            nc.vector.tensor_copy(pages[i][:].indirect(idx4[:]), weighed[step][:])
+            target = pairs[:, t // 2, :, t % 2] if b == 0 else z1[:, :, t]
+            nc.scalar.activation(target, pages[i][:], ACT.Identity, bias=bias_sb[:, b, t : t + 1])
+            if i == PACK - 1:
+                words = pairs[:].rearrange("p u c e -> p (u c e)").bitcast(U32).rearrange("p (u n c i) -> p n c u i", i=4, n=2, u=2)
+                for n in range(2):
+                    nc.scalar.copy(
+                        z0[n][:].rearrange("p c j -> p (c j)").bitcast(U32).rearrange("p (c i u) -> p c u i", i=4, u=2),
+                        words[:, n],
+                    )
+            if step >= last - 2:
+                quantize_z0(step - (last - 2), "right%d" % step)
+            if step == last - 2:
+                ready = held([P, S], F32, "ready_last", tag="z0_0")
+                nc.gpsimd.tensor_tensor(ready[:], late_product[0][:], late_product[1], MULT)
+        nc.vector.tensor_copy(pages[last][:].indirect(idx4[:]), ready[:])
 
         accs = {}
 
         def reader_pass(b, c, g):
             if b == 0:
                 accs[c, g] = bank(2 * c + g, "out_acc%d%d" % (c, g))
-            w_codes, w_sc = w4_q[b, g]
+            w_codes, w_sc = w4_q[b]
             z_codes, z_sc = z_q[b, c]
             for h in range(2):
-                n_cols = slice(P * h, P * (h + 1))
+                n_cols = slice(P * (2 * g + h), P * (2 * g + h + 1))
                 nc.tensor.matmul_mx(
                     out=accs[c, g][:, CHUNK * h : CHUNK * (h + 1)], lhsT=w_codes[:, n_cols].bitcast(FP8X4),
                     lhsT_scale=w_sc[:, n_cols], rhs=z_codes[:, :].bitcast(FP8X4), rhs_scale=z_sc[:, :],
@@ -293,18 +297,25 @@ def tile_list_grain_boundary_segregation_kernel(
         out_rows = out.rearrange("(g h p) t -> g p h t", h=2, p=P)
 
         last_bias = bias_sb[:, 1, PACK - 1 : PACK]
-        for cols in chunks[:2]:
-            nc.vector.tensor_scalar_add(z[1][:, cols, PACK - 1], pages[-1][:, cols], last_bias)
-        for cols in chunks[2:]:
-            nc.scalar.activation(z[1][:, cols, PACK - 1], pages[-1][:, cols], ACT.Identity, bias=last_bias)
+
+        def last_z(c):
+            cols = chunks[c]
+            if c < 3:
+                nc.vector.tensor_scalar_add(z1[:, cols, PACK - 1], pages[last][:, cols], last_bias)
+            else:
+                nc.scalar.activation(z1[:, cols, PACK - 1], pages[last][:, cols], ACT.Identity, bias=last_bias)
+
+        last_z(0)
         for c in range(len(chunks)):
-            quantize_z(1, c)
+            if c + 1 < len(chunks):
+                last_z(c + 1)
+            z_q[1, c] = quantize(z1[:, chunks[c], :].rearrange("p c j -> p (c j)"), CHUNK, "z1%d" % c)
         for c in range(len(chunks)):
             for g in range(2):
                 reader_pass(1, c, g)
-                result = held([P, 2, CHUNK], F32, "result%d%d" % (c, g), tag="right%d" % (2 * c + g))
+                result = held([P, 2, CHUNK], F32, "result%d%d" % (c, g), tag="left%d" % (2 * c + g))
                 flat = result[:].rearrange("p h t -> p (h t)")
-                if g == 1:
+                if g == 1 and c >= 1:
                     nc.vector.tensor_copy(flat, accs[c, g][:])
                 else:
                     nc.scalar.copy(flat, accs[c, g][:])

@@ -15,6 +15,7 @@ FP8X4 = mybir.dt.float8_e4m3fn_x4
 FP4X4 = mybir.dt.float4_e2m1fn_x4
 ACT = mybir.ActivationFunctionType
 MULT = mybir.AluOpType.mult
+ADD = mybir.AluOpType.add
 
 P = 128
 PACK = 4
@@ -61,27 +62,47 @@ def tile_list_grain_boundary_segregation_kernel(
             rows = source[0, 4 * q : 4 * q + 4, :].bitcast(I32)
             queue.dma_start(plane[QUAD * q : QUAD * (q + 1), :], rows.unsqueeze(0).to_broadcast([8, 4, rows.shape[1]]))
 
-        def load_site_weights(source, slots, name, tag=None, last_queue=nc.sync):
-            tile = held([P, len(slots), S], F32, name, tag=tag)
-            rows = source.rearrange("(q t) j -> q t j", t=PACK)[:, slots.start : slots.stop, :]
+        def load_first_site_weights(source, name):
+            tile = held([P, S], F32, name)
+            rows = source.rearrange("(m t e) j -> t m e j", t=PACK, e=2)[0]
             for q in range(4):
-                queue = last_queue if q == 3 else nc.sync
-                queue.dma_start(tile[QUAD * q : QUAD * (q + 1)], rows)
+                nc.sync.dma_start(tile[QUAD * q : QUAD * (q + 1)], rows)
+            return [tile[:]]
+
+        def load_site_weights(source, slots, name):
+            tile = held([P, len(slots), S], F32, name)
+            rows = source.rearrange("(m t e) j -> e m t j", t=PACK, e=2)
+            for q in range(4):
+                for e in range(2):
+                    nc.sync.dma_start(tile[QUAD * q + e : QUAD * (q + 1) : 2], rows[e][:, slots.start : slots.stop, :])
             return [tile[:, t, :] for t in range(len(slots))]
+
+        def load_row_values(queue, source, name):
+            tile = held([P, 2, 8], F32, name)
+            runs = source.rearrange("(b m x) -> m b x", b=2, x=8)
+            for e in range(2):
+                queue.dma_start(tile[e:P:2, :, 0:7], runs[:, :, e : e + 7])
+            return [[tile[:, b, 2 * t : 2 * t + 1] for t in range(PACK)] for b in range(2)]
 
         def load_rows(source, name, slot):
             tile = held([P, PACK, 512], F32, name, tag="raw%d" % slot)
             nc.sync.dma_start(tile[:], source.rearrange("(p j) c -> p j c", j=PACK))
             return tile
 
-        def reorder_columns(dst, src, line):
+        def reorder_pairs(dst, src, line):
             nc.vector.tensor_copy(
-                dst.rearrange("p (b t m i) -> p b m t i", t=PACK, m=P // line, i=line),
-                src.rearrange("p (b m i t) -> p b m t i", t=PACK, m=P // line, i=line),
+                dst.rearrange("p (b t m i) -> p b m t i", t=PACK, m=P // 2 // line, i=line),
+                src.rearrange("p (b m i t) -> p b m t i", t=PACK, m=P // 2 // line, i=line),
             )
 
-        def quantize(grouped, columns, name):
-            codes = held([P, columns], U32, name + "_codes")
+        def reorder_words(dst, src):
+            nc.vector.tensor_copy(
+                dst.rearrange("p (b t m e) -> p b t m e", t=PACK, m=P // 2, e=2),
+                src.rearrange("p (b m t e) -> p b t m e", t=PACK, m=P // 2, e=2),
+            )
+
+        def quantize(grouped, columns, name, tag=None):
+            codes = held([P, columns], U32, name + "_codes", tag=tag)
             scales = held([P, columns], U8, name + "_scales")
             nc.vector.quantize_mx(out=codes[:].bitcast(FP8X4), scales=scales[:], in_=grouped)
             return codes, scales
@@ -90,8 +111,6 @@ def tile_list_grain_boundary_segregation_kernel(
         w1_plane = held([P, H // 4], I32, "w1_plane")
         w3_plane = held([P, H // 4], I32, "w3_plane")
         tab2_plane = held([P, T // 4], I32, "tab2_plane")
-        for plane in (tab2_plane, w3_plane):
-            nc.vector.memset(plane[:], 0)
 
         idx1 = load_list(offs, "idx1")
         for q in range(4):
@@ -101,11 +120,12 @@ def tile_list_grain_boundary_segregation_kernel(
         load_scale_quadrant(nc.sync, w1_plane, 0, w1_scales)
         tab_sb = load_words(tab_words[0], T, "tab_sb")
         for q in range(1, 4):
-            load_scale_quadrant(nc.sync, w1_plane, q, w1_scales)
+            load_scale_quadrant(nc.gpsimd, w1_plane, q, w1_scales)
+        for plane in (tab2_plane, w3_plane):
+            nc.gpsimd.memset(plane[:], 0)
         idx3 = load_list(offs3, "idx3")
-        wg1_sb = load_site_weights(wg1, range(0, 1), "wg1_first", last_queue=nc.gpsimd)
-        gain_sb = held([P, 2, PACK], F32, "gain_sb")
-        nc.gpsimd.dma_start(gain_sb[:], gain.rearrange("(b p t) -> p b t", b=2, t=PACK))
+        wg1_sb = load_first_site_weights(wg1, "wg1_first")
+        gain_sb = load_row_values(nc.sync, gain, "gain_sb")
         wg1_sb = wg1_sb + load_site_weights(wg1, range(1, PACK), "wg1_rest")
         w2_raw = {}
 
@@ -115,15 +135,7 @@ def tile_list_grain_boundary_segregation_kernel(
                 w2_raw[a, b] = load_rows(rows, "w2_raw%d%d" % (a, b), 2 * b + a)
 
         load_w2(0)
-        load_scale_rows(tab2_plane, tab2_scales, range(4))
-        load_scale_rows(w3_plane, w3_scales, range(4))
-        idx2 = load_list(offs2, "idx2")
-        tab2_sb = [load_words(tab2_words[a], T, "tab2_sb%d" % a) for a in range(2)]
-        w3_sb = [load_words(w3_words[a], H, "w3_sb%d" % a) for a in range(2)]
         load_w2(1)
-        bias_sb = held([P, 2, PACK], F32, "bias_sb")
-        nc.sync.dma_start(bias_sb[:], bias.rearrange("(b p t) -> p b t", b=2, t=PACK))
-        idx4 = load_list(offs4, "idx4")
 
         w1_ord = held([P, 2 * H], U8, "w1_ord")
         v_scales = held([P, S], U8, "v_scales")
@@ -132,9 +144,9 @@ def tile_list_grain_boundary_segregation_kernel(
         halves = [slice(0, S // 2), slice(S // 2, S)]
 
         def order_w1(b):
-            cols = slice(512 * b, 512 * (b + 1))
-            reorder_columns(w1_ord[:].bitcast(U16)[:, cols], w1_sb[:].bitcast(U16)[:, cols], 8)
-            reorder_columns(w1_sc[:, cols], w1_plane[:].bitcast(U8)[:, cols], 16)
+            cols = slice(256 * b, 256 * (b + 1))
+            reorder_pairs(w1_ord[:].bitcast(U32)[:, cols], w1_sb[:].bitcast(U32)[:, cols], 4)
+            reorder_pairs(w1_sc[:].bitcast(U16)[:, cols], w1_plane[:].bitcast(U16)[:, cols], 8)
 
         nc.vector.tensor_copy(v_scales[:], tab_plane[:].bitcast(U8).indirect(idx1[:]))
         order_w1(0)
@@ -143,13 +155,17 @@ def tile_list_grain_boundary_segregation_kernel(
         order_w1(1)
 
         pages = {}
+        late_tags = {5: "tab2_sb0", 6: "tab2_sb1", 7: "tab2_plane"}
 
         def bulk_page(step, parts):
             t, b = divmod(step, 2)
             i = PACK * b + t
-            pages[i] = held([P, T2], F32, "page%d" % i, tag="tab2_sb%d" % b if step >= 6 else None)
+            pages[i] = held([P, T2], F32, "page%d" % i, tag=late_tags.get(step))
             response = held([P, S], F32, "response%d" % i, tag="left%d" % step)
-            h1 = held([P, S], F32, "h1_%d" % i, tag="right%d" % step)
+            weight = held([P, S], F32, "weight%d" % i, tag="right%d" % step)
+            gain_col = gain_sb[b][t]
+            rest = parts[-1]
+            nc.gpsimd.tensor_scalar(weight[:, rest], wg1_sb[t][:, rest], gain_col, 0.0, MULT, ADD)
             for n, part in enumerate(parts):
                 acc = bank(step + 7 * n, "h1_acc%d_%d" % (i, n))
                 nc.tensor.matmul_mx(
@@ -158,9 +174,13 @@ def tile_list_grain_boundary_segregation_kernel(
                     rhs=v_words[:, part].bitcast(FP8X4), rhs_scale=v_scales[:, part], start=True, stop=True,
                 )
                 nc.scalar.activation(response[:, part], acc[:, part], ACT.Tanh)
-                nc.scalar.activation(h1[:, part], response[:, part], ACT.Copy, scale=gain_sb[:, b, t : t + 1])
-                nc.gpsimd.tensor_tensor(response[:, part], h1[:, part], wg1_sb[t][:, part], MULT)
-                nc.vector.tensor_copy(pages[i][:].indirect(entries(idx3, part)), response[:, part])
+                if part is rest:
+                    nc.gpsimd.tensor_tensor(weight[:, part], response[:, part], weight[:, part], MULT)
+                else:
+                    nc.vector.scalar_tensor_tensor(
+                        weight[:, part], response[:, part], gain_col, wg1_sb[t][:, part], MULT, MULT,
+                    )
+                nc.vector.tensor_copy(pages[i][:].indirect(entries(idx3, part)), weight[:, part])
 
         w2_q = {}
 
@@ -168,8 +188,8 @@ def tile_list_grain_boundary_segregation_kernel(
             for a in range(2):
                 grouped = held([P, PACK * 512], BF16, "w2_grouped%d%d" % (a, b))
                 nc.scalar.copy(
-                    grouped[:].rearrange("p (t m j) -> p m t j", t=PACK, j=PACK),
-                    w2_raw[a, b][:].rearrange("p j (m t) -> p m t j", t=PACK),
+                    grouped[:].rearrange("p (t m e j) -> p m t e j", t=PACK, e=2, j=PACK),
+                    w2_raw[a, b][:].rearrange("p j (m t e) -> p m t e j", t=PACK, e=2),
                 )
                 w2_q[a, b] = quantize(grouped[:], 512, "w2_%d%d" % (a, b))
 
@@ -178,36 +198,46 @@ def tile_list_grain_boundary_segregation_kernel(
         for step in range(1, 4):
             bulk_page(step, [whole])
         quantize_w2(0)
-        for step in range(4, 6):
-            bulk_page(step, [whole])
-
-        v2_scales = held([P, S], U8, "v2_scales")
-        nc.vector.tensor_copy(v2_scales[:], tab2_plane[:].bitcast(U8).indirect(idx2[:]))
-        w3_sc = held([P, H], U8, "w3_sc")
-        reorder_columns(w3_sc[:], w3_plane[:].bitcast(U8), 16)
-        w3_ord = held([P, 2 * H], U32, "w3_ord")
-        for a in range(2):
-            reorder_columns(w3_ord[:, H * a : H * (a + 1)], w3_sb[a][:].bitcast(U32), 4)
+        bulk_page(4, [whole])
 
         quantize_w2(1)
 
-        w4_q = {}
+        w4_grouped = []
         for a in range(2):
-            raw = load_rows(w4[K_PASS * a : K_PASS * (a + 1), :], "w4_raw%d" % a, a)
+            raw = held([P, PACK, N], F32, "w4_raw%d" % a, tag="raw%d" % a)
+            rows = w4[K_PASS * a : K_PASS * (a + 1), :].rearrange("(m t e) c -> e m t c", t=PACK, e=2)
+            for e in range(2):
+                nc.sync.dma_start(raw[e:P:2], rows[e])
             grouped = held([P, PACK * 512], BF16, "w4_grouped%d" % a)
             nc.scalar.copy(
                 grouped[:].rearrange("p (c i j) -> p c j i", i=4, j=PACK),
                 raw[:].rearrange("p j (c i) -> p c j i", i=4),
             )
-            w4_q[a] = quantize(grouped[:], 512, "w4_%d" % a)
+            w4_grouped.append(grouped)
 
+        load_scale_rows(w3_plane, w3_scales, range(4))
+        load_scale_rows(tab2_plane, tab2_scales, range(4))
+        w3_sb = [load_words(w3_words[a], H, "w3_sb%d" % a) for a in range(2)]
+        tab2_sb = [load_words(tab2_words[a], T, "tab2_sb%d" % a) for a in range(2)]
+        idx2 = load_list(offs2, "idx2")
         wg2_sb = load_site_weights(wg2, range(PACK), "wg2_sb")
+        idx4 = load_list(offs4, "idx4")
+        bias_sb = load_row_values(nc.sync, bias, "bias_sb")
 
+        w3_sc = held([P, H], U8, "w3_sc")
+        reorder_pairs(w3_sc[:].bitcast(U16), w3_plane[:].bitcast(U16), 8)
+        w3_ord = held([P, 2 * H], U32, "w3_ord")
+        for a in range(2):
+            reorder_words(w3_ord[:, H * a : H * (a + 1)], w3_sb[a][:].bitcast(U32))
+
+        w4_q = {1: quantize(w4_grouped[1][:], 512, "w4_1")}
         v2_words = held([P, 2 * S], U32, "v2_words", tag="raw1")
         for a in range(2):
             nc.vector.tensor_copy(v2_words[:, S * a : S * (a + 1)], tab2_sb[a][:].bitcast(U32).indirect(idx2[:]))
+        v2_scales = held([P, S], U8, "v2_scales")
+        nc.vector.tensor_copy(v2_scales[:], tab2_plane[:].bitcast(U8).indirect(idx2[:]))
 
-        for step in range(6, PAGES):
+        for step in range(5, PAGES):
             bulk_page(step, [whole])
 
         def product(acc, operands):
@@ -222,6 +252,7 @@ def tile_list_grain_boundary_segregation_kernel(
         second = [held([P, PACK, S], F32, "second%d" % b, tag=("raw0", "tab_sb")[b]) for b in range(2)]
         last = PAGES - 1
         order = [0, 6, 1, 2, 3, 4, 5, 7]
+        early, late = slice(0, S - 64), slice(S - 64, S)
         weighed = []
         for step, i in enumerate(order):
             b, t = divmod(i, PACK)
@@ -233,19 +264,18 @@ def tile_list_grain_boundary_segregation_kernel(
             acc = bank(2 * step + 1, "w3_acc%d" % i)
             product(acc, [(w3_ord[:, H * a + P * i : H * a + P * (i + 1)], w3_sc[4 * a :, cols]) for a in range(2)])
             nc.scalar.copy(second[b][:, t, :], acc[:])
+            part = early if step == last else whole
             h2 = held([P, S], F32, "h2_%d" % i, tag="h2_%d" % (step % 2))
-            nc.gpsimd.tensor_tensor(h2[:], first[b][:, t, :], second[b][:, t, :], MULT)
-            if step == last:
-                late_product = (h2, wg2_sb[t])
-                continue
-            ready = held([P, S], F32, "ready%d" % i, tag="right%d" % step)
-            nc.gpsimd.tensor_tensor(ready[:], h2[:], wg2_sb[t], MULT)
+            nc.gpsimd.tensor_tensor(h2[:, part], first[b][:, t, part], second[b][:, t, part], MULT)
+            ready = held([P, S], F32, "ready%d" % i, tag="left%d" % step)
+            nc.gpsimd.tensor_tensor(ready[:, part], h2[:, part], wg2_sb[t][:, part], MULT)
             weighed.append(ready)
 
         pairs = held([P, 2, T2, 2], BF16, "pairs", tag="w3_ord")
         z0 = [held([P, T2 // 2, PACK], BF16, "z0_%d" % n) for n in range(2)]
-        z1 = held([P, T2, PACK], BF16, "z1")
-        chunks = [slice(c, c + CHUNK) for c in range(0, T2, CHUNK)]
+        z1 = held([P, T2, PACK], BF16, "z1", tag="raw1")
+        edges = [0, CHUNK // 2] + list(range(CHUNK, T2 + 1, CHUNK))
+        chunks = [slice(lo, hi) for lo, hi in zip(edges, edges[1:])]
         z_q = {}
 
         def quantize_z0(n, tag):
@@ -254,14 +284,16 @@ def tile_list_grain_boundary_segregation_kernel(
             nc.vector.quantize_mx(
                 out=codes[:].bitcast(FP8X4), scales=scales[:], in_=z0[n][:].rearrange("p c j -> p (c j)"),
             )
-            for c in range(2):
-                z_q[0, 2 * n + c] = (codes[:, chunks[c]], scales[:, chunks[c]])
+            for c, cols in enumerate(chunks):
+                if cols.start // (T2 // 2) == n:
+                    own = slice(cols.start - n * T2 // 2, cols.stop - n * T2 // 2)
+                    z_q[0, c] = (codes[:, own], scales[:, own])
 
         for step, i in enumerate(order[:last]):
             b, t = divmod(i, PACK)
             nc.vector.tensor_copy(pages[i][:].indirect(idx4[:]), weighed[step][:])
             target = pairs[:, t // 2, :, t % 2] if b == 0 else z1[:, :, t]
-            nc.scalar.activation(target, pages[i][:], ACT.Identity, bias=bias_sb[:, b, t : t + 1])
+            nc.scalar.activation(target, pages[i][:], ACT.Identity, bias=bias_sb[b][t])
             if i == PACK - 1:
                 words = pairs[:].rearrange("p u c e -> p (u c e)").bitcast(U32).rearrange("p (u n c i) -> p n c u i", i=4, n=2, u=2)
                 for n in range(2):
@@ -269,54 +301,64 @@ def tile_list_grain_boundary_segregation_kernel(
                         z0[n][:].rearrange("p c j -> p (c j)").bitcast(U32).rearrange("p (c i u) -> p c u i", i=4, u=2),
                         words[:, n],
                     )
-            if step >= last - 2:
-                quantize_z0(step - (last - 2), "right%d" % step)
-            if step == last - 2:
-                ready = held([P, S], F32, "ready_last", tag="z0_0")
-                nc.gpsimd.tensor_tensor(ready[:], late_product[0][:], late_product[1], MULT)
-        nc.vector.tensor_copy(pages[last][:].indirect(idx4[:]), ready[:])
+        quantize_z0(0, "left%d" % (last - 2))
+        h2 = held([P, late.stop - late.start], F32, "h2_late", tag="z0_0")
+        nc.vector.tensor_tensor(h2[:], first[1][:, PACK - 1, late], second[1][:, PACK - 1, late], MULT)
+        quantize_z0(1, None)
+        nc.vector.tensor_tensor(weighed[last][:, late], h2[:], wg2_sb[PACK - 1][:, late], MULT)
+        w4_q[0] = quantize(w4_grouped[0][:], 512, "w4_0", tag="left%d" % (last - 1))
+        nc.vector.tensor_copy(pages[last][:].indirect(idx4[:]), weighed[last][:])
 
         accs = {}
 
-        def reader_pass(b, c, g):
+        def groups(c):
+            width = chunks[c].stop - chunks[c].start
+            tiles = 512 // width
+            return [range(n, n + tiles) for n in range(0, N // P, tiles)], width
+
+        def reader_pass(b, c, tiles, width):
             if b == 0:
-                accs[c, g] = bank(2 * c + g, "out_acc%d%d" % (c, g))
+                accs[c, tiles[0]] = bank(len(accs), "out_acc%d%d" % (c, tiles[0]))
             w_codes, w_sc = w4_q[b]
             z_codes, z_sc = z_q[b, c]
-            for h in range(2):
-                n_cols = slice(P * (2 * g + h), P * (2 * g + h + 1))
+            for h, n in enumerate(tiles):
+                n_cols = slice(P * n, P * (n + 1))
                 nc.tensor.matmul_mx(
-                    out=accs[c, g][:, CHUNK * h : CHUNK * (h + 1)], lhsT=w_codes[:, n_cols].bitcast(FP8X4),
+                    out=accs[c, tiles[0]][:, width * h : width * (h + 1)], lhsT=w_codes[:, n_cols].bitcast(FP8X4),
                     lhsT_scale=w_sc[:, n_cols], rhs=z_codes[:, :].bitcast(FP8X4), rhs_scale=z_sc[:, :],
-                    start=b == 0 and h == 0, stop=b == 1 and h == 1,
+                    start=b == 0 and n == tiles[0], stop=b == 1 and n == tiles[-1],
                 )
 
         for c in range(len(chunks)):
-            for g in range(2):
-                reader_pass(0, c, g)
-        out_rows = out.rearrange("(g h p) t -> g p h t", h=2, p=P)
+            sets, width = groups(c)
+            for tiles in sets:
+                reader_pass(0, c, tiles, width)
+        out_rows = out.rearrange("(n p) t -> p n t", p=P)
 
-        last_bias = bias_sb[:, 1, PACK - 1 : PACK]
+        last_bias = bias_sb[1][PACK - 1]
 
         def last_z(c):
             cols = chunks[c]
-            if c < 3:
+            if c + 1 < len(chunks):
                 nc.vector.tensor_scalar_add(z1[:, cols, PACK - 1], pages[last][:, cols], last_bias)
             else:
                 nc.scalar.activation(z1[:, cols, PACK - 1], pages[last][:, cols], ACT.Identity, bias=last_bias)
 
         last_z(0)
-        for c in range(len(chunks)):
+        for c, cols in enumerate(chunks):
             if c + 1 < len(chunks):
                 last_z(c + 1)
-            z_q[1, c] = quantize(z1[:, chunks[c], :].rearrange("p c j -> p (c j)"), CHUNK, "z1%d" % c)
+            z_q[1, c] = quantize(z1[:, cols, :].rearrange("p c j -> p (c j)"), cols.stop - cols.start, "z1%d" % c)
+        stores = 0
         for c in range(len(chunks)):
-            for g in range(2):
-                reader_pass(1, c, g)
-                result = held([P, 2, CHUNK], F32, "result%d%d" % (c, g), tag="left%d" % (2 * c + g))
+            sets, width = groups(c)
+            for tiles in sets:
+                reader_pass(1, c, tiles, width)
+                result = held([P, len(tiles), width], F32, "result%d" % stores, tag="right%d" % stores)
                 flat = result[:].rearrange("p h t -> p (h t)")
-                if g == 1 and c >= 1:
-                    nc.vector.tensor_copy(flat, accs[c, g][:])
+                if stores >= 3 and stores % 2 == 1:
+                    nc.vector.tensor_copy(flat, accs[c, tiles[0]][:])
                 else:
-                    nc.scalar.copy(flat, accs[c, g][:])
-                nc.sync.dma_start(out_rows[g][:, :, chunks[c]], result[:])
+                    nc.scalar.copy(flat, accs[c, tiles[0]][:])
+                nc.sync.dma_start(out_rows[:, tiles[0] : tiles[-1] + 1, chunks[c]], result[:])
+                stores = stores + 1

@@ -202,19 +202,6 @@ def tile_list_grain_boundary_segregation_kernel(
 
         quantize_w2(1)
 
-        w4_grouped = []
-        for a in range(2):
-            raw = held([P, PACK, N], F32, "w4_raw%d" % a, tag="raw%d" % a)
-            rows = w4[K_PASS * a : K_PASS * (a + 1), :].rearrange("(m t e) c -> e m t c", t=PACK, e=2)
-            for e in range(2):
-                nc.sync.dma_start(raw[e:P:2], rows[e])
-            grouped = held([P, PACK * 512], BF16, "w4_grouped%d" % a)
-            nc.scalar.copy(
-                grouped[:].rearrange("p (c i j) -> p c j i", i=4, j=PACK),
-                raw[:].rearrange("p j (c i) -> p c j i", i=4),
-            )
-            w4_grouped.append(grouped)
-
         load_scale_rows(w3_plane, w3_scales, range(4))
         load_scale_rows(tab2_plane, tab2_scales, range(4))
         w3_sb = [load_words(w3_words[a], H, "w3_sb%d" % a) for a in range(2)]
@@ -223,6 +210,13 @@ def tile_list_grain_boundary_segregation_kernel(
         wg2_sb = load_site_weights(wg2, range(PACK), "wg2_sb")
         idx4 = load_list(offs4, "idx4")
         bias_sb = load_row_values(nc.sync, bias, "bias_sb")
+        w4_raw = []
+        for a in range(2):
+            raw = held([P, PACK, N], F32, "w4_raw%d" % a)
+            rows = w4[K_PASS * a : K_PASS * (a + 1), :].rearrange("(m t e) c -> e m t c", t=PACK, e=2)
+            for e in range(2):
+                nc.sync.dma_start(raw[e:P:2], rows[e])
+            w4_raw.append(raw)
 
         w3_sc = held([P, H], U8, "w3_sc")
         reorder_pairs(w3_sc[:].bitcast(U16), w3_plane[:].bitcast(U16), 8)
@@ -230,7 +224,6 @@ def tile_list_grain_boundary_segregation_kernel(
         for a in range(2):
             reorder_words(w3_ord[:, H * a : H * (a + 1)], w3_sb[a][:].bitcast(U32))
 
-        w4_q = {1: quantize(w4_grouped[1][:], 512, "w4_1")}
         v2_words = held([P, 2 * S], U32, "v2_words", tag="raw1")
         for a in range(2):
             nc.vector.tensor_copy(v2_words[:, S * a : S * (a + 1)], tab2_sb[a][:].bitcast(U32).indirect(idx2[:]))
@@ -271,6 +264,16 @@ def tile_list_grain_boundary_segregation_kernel(
             nc.gpsimd.tensor_tensor(ready[:, part], h2[:, part], wg2_sb[t][:, part], MULT)
             weighed.append(ready)
 
+        w4_grouped = []
+        for a in range(2):
+            grouped = held([P, PACK * N], BF16, "w4_grouped%d" % a, tag="w2_grouped%d0" % a)
+            nc.scalar.copy(
+                grouped[:].rearrange("p (c i j) -> p c j i", i=4, j=PACK),
+                w4_raw[a][:].rearrange("p j (c i) -> p c j i", i=4),
+            )
+            w4_grouped.append(grouped)
+        w4_q = {}
+
         pairs = held([P, 2, T2, 2], BF16, "pairs", tag="w3_ord")
         z0 = [held([P, T2 // 2, PACK], BF16, "z0_%d" % n) for n in range(2)]
         z1 = held([P, T2, PACK], BF16, "z1", tag="raw1")
@@ -301,6 +304,8 @@ def tile_list_grain_boundary_segregation_kernel(
                         z0[n][:].rearrange("p c j -> p (c j)").bitcast(U32).rearrange("p (c i u) -> p c u i", i=4, u=2),
                         words[:, n],
                     )
+            if step == last - 3:
+                w4_q[1] = quantize(w4_grouped[1][:], N, "w4_1", tag="left%d" % step)
         quantize_z0(0, "left%d" % (last - 2))
         h2 = held([P, late.stop - late.start], F32, "h2_late", tag="z0_0")
         nc.vector.tensor_tensor(h2[:], first[1][:, PACK - 1, late], second[1][:, PACK - 1, late], MULT)

@@ -21,8 +21,9 @@ P = 128
 PACK = 4
 K_PASS = P * PACK
 QUAD = 32
-PAGES = H // P
+BANK = 512
 CHUNK = 256
+QUADRANTS = (0, 2, 1, 3)
 
 
 def tile_list_grain_boundary_segregation_kernel(
@@ -33,13 +34,17 @@ def tile_list_grain_boundary_segregation_kernel(
     with ExitStack() as ctx:
         lists = ctx.enter_context(tc.tile_pool(name="lists", bufs=1))
         keep = ctx.enter_context(tc.tile_pool(name="keep", bufs=1))
+        shared = ctx.enter_context(tc.tile_pool(name="shared", bufs=1))
         psum = ctx.enter_context(tc.psum_pool(name="psum", bufs=1))
 
         def held(shape, dtype, name, tag=None):
             return keep.tile(shape, dtype, name=name, tag=tag or name, align_bytes=64)
 
+        def placed(shape, dtype, name, kib):
+            return shared.tile(shape, dtype, name=name, align_bytes=64, offset=1024 * kib)
+
         def bank(index, name):
-            return psum.tile([P, 512], F32, name=name, tag="bank%d" % (index % 8))
+            return psum.tile([P, BANK], F32, name=name, tag="bank%d" % (index % 8))
 
         def load_list(source, name):
             tile = lists.tile([P, S // 16], U16, name=name)
@@ -49,44 +54,55 @@ def tile_list_grain_boundary_segregation_kernel(
         def entries(idx, part):
             return idx[:, part.start // 16 : part.stop // 16]
 
-        def load_words(source, columns, name):
-            tile = held([P, columns], I32, name)
+        def load_words(source, tile):
             nc.sync.dma_start(tile[:], source.rearrange("p c i -> p (c i)").bitcast(I32))
             return tile
 
-        def load_scale_rows(plane, source, quadrants):
-            for q in quadrants:
-                nc.sync.dma_start(plane[QUAD * q : QUAD * q + 8, :], source[:, 4 * q : 4 * q + 4, :].bitcast(I32))
+        def load_scale_rows(queue, plane, source, q):
+            rows = 4 * source.shape[0]
+            queue.dma_start(plane[QUAD * q : QUAD * q + rows, :], source[:, 4 * q : 4 * q + 4, :].bitcast(I32))
 
-        def load_scale_quadrant(queue, plane, q, source):
-            rows = source[0, 4 * q : 4 * q + 4, :].bitcast(I32)
-            queue.dma_start(plane[QUAD * q : QUAD * (q + 1), :], rows.unsqueeze(0).to_broadcast([8, 4, rows.shape[1]]))
-
-        def load_first_site_weights(source, name):
+        def load_site_slot(source, t, name):
             tile = held([P, S], F32, name)
-            rows = source.rearrange("(m t e) j -> t m e j", t=PACK, e=2)[0]
-            for q in range(4):
+            rows = source.rearrange("(m t e) j -> t m e j", t=PACK, e=2)[t]
+            for q in QUADRANTS:
                 nc.sync.dma_start(tile[QUAD * q : QUAD * (q + 1)], rows)
             return [tile[:]]
 
-        def load_site_weights(source, slots, name):
+        def load_site_slots(source, slots, name):
             tile = held([P, len(slots), S], F32, name)
             rows = source.rearrange("(m t e) j -> e m t j", t=PACK, e=2)
-            for q in range(4):
-                for e in range(2):
+            for e in range(2):
+                for q in QUADRANTS:
                     nc.sync.dma_start(tile[QUAD * q + e : QUAD * (q + 1) : 2], rows[e][:, slots.start : slots.stop, :])
-            return [tile[:, t, :] for t in range(len(slots))]
+            return [tile[:, n, :] for n in range(len(slots))]
 
-        def load_row_values(queue, source, name):
+        def load_row_values(source, name):
             tile = held([P, 2, 8], F32, name)
             runs = source.rearrange("(b m x) -> m b x", b=2, x=8)
             for e in range(2):
-                queue.dma_start(tile[e:P:2, :, 0:7], runs[:, :, e : e + 7])
+                nc.sync.dma_start(tile[e:P:2, :, 0:7], runs[:, :, e : e + 7])
             return [[tile[:, b, 2 * t : 2 * t + 1] for t in range(PACK)] for b in range(2)]
 
-        def load_rows(source, name, slot):
-            tile = held([P, PACK, 512], F32, name, tag="raw%d" % slot)
-            nc.sync.dma_start(tile[:], source.rearrange("(p j) c -> p j c", j=PACK))
+        def load_w2(b):
+            tiles = []
+            for a in range(2):
+                tile = placed([P, PACK, 512], F32, "w2_raw%d%d" % (a, b), 8 * (2 * b + a))
+                rows = w2[K_PASS * a : K_PASS * (a + 1), 512 * b : 512 * (b + 1)]
+                nc.sync.dma_start(tile[:], rows.rearrange("(p j) c -> p j c", j=PACK))
+                tiles.append(tile)
+            return tiles
+
+        def load_w3(b):
+            tile = held([P, 2, 512], I32, "w3_sb%d" % b)
+            words = w3_words[:, :, 512 * b : 512 * (b + 1), :].rearrange("a p c i -> p a (c i)")
+            nc.sync.dma_start(tile[:], words.bitcast(I32))
+            return tile
+
+        def load_w4(a, tile):
+            rows = w4[K_PASS * a : K_PASS * (a + 1), :].rearrange("(m t e) c -> e m t c", t=PACK, e=2)
+            for e in range(2):
+                nc.sync.dma_start(tile[e:P:2], rows[e])
             return tile
 
         def reorder_pairs(dst, src, line):
@@ -95,14 +111,11 @@ def tile_list_grain_boundary_segregation_kernel(
                 src.rearrange("p (b m i t) -> p b m t i", t=PACK, m=P // 2 // line, i=line),
             )
 
-        def reorder_words(dst, src):
-            nc.vector.tensor_copy(
-                dst.rearrange("p (b t m e) -> p b t m e", t=PACK, m=P // 2, e=2),
-                src.rearrange("p (b m t e) -> p b t m e", t=PACK, m=P // 2, e=2),
-            )
-
-        def quantize(grouped, columns, name, tag=None):
-            codes = held([P, columns], U32, name + "_codes", tag=tag)
+        def quantize(grouped, columns, name, tag=None, kib=None):
+            if kib is None:
+                codes = held([P, columns], U32, name + "_codes", tag=tag)
+            else:
+                codes = placed([P, columns], U32, name + "_codes", kib)
             scales = held([P, columns], U8, name + "_scales")
             nc.vector.quantize_mx(out=codes[:].bitcast(FP8X4), scales=scales[:], in_=grouped)
             return codes, scales
@@ -111,255 +124,248 @@ def tile_list_grain_boundary_segregation_kernel(
         w1_plane = held([P, H // 4], I32, "w1_plane")
         w3_plane = held([P, H // 4], I32, "w3_plane")
         tab2_plane = held([P, T // 4], I32, "tab2_plane")
+        nc.vector.memset(tab_plane[:], 0)
+        nc.gpsimd.memset(w1_plane[:], 0)
 
         idx1 = load_list(offs, "idx1")
-        for q in range(4):
-            load_scale_quadrant(nc.sync, tab_plane, q, tab_scales)
+        tab_sb = load_words(tab_words[0], held([P, T], I32, "tab_sb"))
         w1_sb = held([P, H // 2], I32, "w1_sb")
         nc.sync.dma_start(w1_sb[:], w1_words[0].bitcast(I32))
-        load_scale_quadrant(nc.sync, w1_plane, 0, w1_scales)
-        tab_sb = load_words(tab_words[0], T, "tab_sb")
-        for q in range(1, 4):
-            load_scale_quadrant(nc.gpsimd, w1_plane, q, w1_scales)
+        for q in QUADRANTS:
+            load_scale_rows(nc.sync, tab_plane, tab_scales, q)
+        for q in QUADRANTS[:2]:
+            load_scale_rows(nc.sync, w1_plane, w1_scales, q)
+        for q in QUADRANTS[2:]:
+            load_scale_rows(nc.gpsimd, w1_plane, w1_scales, q)
         for plane in (tab2_plane, w3_plane):
             nc.gpsimd.memset(plane[:], 0)
         idx3 = load_list(offs3, "idx3")
-        wg1_sb = load_first_site_weights(wg1, "wg1_first")
-        gain_sb = load_row_values(nc.sync, gain, "gain_sb")
-        wg1_sb = wg1_sb + load_site_weights(wg1, range(1, PACK), "wg1_rest")
-        w2_raw = {}
-
-        def load_w2(b):
-            for a in range(2):
-                rows = w2[K_PASS * a : K_PASS * (a + 1), 512 * b : 512 * (b + 1)]
-                w2_raw[a, b] = load_rows(rows, "w2_raw%d%d" % (a, b), 2 * b + a)
-
-        load_w2(0)
-        load_w2(1)
+        wg1_sb = load_site_slot(wg1, 0, "wg1_0")
+        gain_sb = load_row_values(gain, "gain_sb")
+        wg1_sb = wg1_sb + load_site_slot(wg1, 1, "wg1_1")
+        w2_raw = [load_w2(0)]
+        wg1_sb = wg1_sb + load_site_slots(wg1, range(2, PACK), "wg1_rest")
+        w2_raw.append(load_w2(1))
+        for q in QUADRANTS:
+            load_scale_rows(nc.sync, w3_plane, w3_scales, q)
+        w3_sb = [load_w3(b) for b in range(2)]
+        for q in QUADRANTS:
+            load_scale_rows(nc.sync, tab2_plane, tab2_scales, q)
+        tab2_sb = [
+            load_words(tab2_words[0], held([P, T], I32, "tab2_sb0")),
+            load_words(tab2_words[1], placed([P, T], I32, "tab2_sb1", 32)),
+        ]
+        idx2 = load_list(offs2, "idx2")
+        w4_raw = [load_w4(0, placed([P, PACK, N], F32, "w4_raw0", 0))]
+        wg2_sb = load_site_slot(wg2, 0, "wg2_0") + load_site_slots(wg2, range(1, PACK), "wg2_rest")
+        idx4 = load_list(offs4, "idx4")
+        bias_sb = load_row_values(bias, "bias_sb")
+        w4_raw.append(load_w4(1, held([P, PACK, N], F32, "w4_raw1")))
 
         w1_ord = held([P, 2 * H], U8, "w1_ord")
-        v_scales = held([P, S], U8, "v_scales")
         w1_sc = held([P, H], U8, "w1_sc")
+        v_scales = held([P, S], U8, "v_scales")
         v_words = held([P, S], U32, "v_words")
         halves = [slice(0, S // 2), slice(S // 2, S)]
+        whole = slice(0, S)
 
         def order_w1(b):
             cols = slice(256 * b, 256 * (b + 1))
             reorder_pairs(w1_ord[:].bitcast(U32)[:, cols], w1_sb[:].bitcast(U32)[:, cols], 4)
             reorder_pairs(w1_sc[:].bitcast(U16)[:, cols], w1_plane[:].bitcast(U16)[:, cols], 8)
 
-        nc.vector.tensor_copy(v_scales[:], tab_plane[:].bitcast(U8).indirect(idx1[:]))
-        order_w1(0)
-        for part in halves:
+        def gather_v(part):
             nc.vector.tensor_copy(v_words[:, part], tab_sb[:].bitcast(U32).indirect(entries(idx1, part)))
+            nc.vector.tensor_copy(v_scales[:, part], tab_plane[:].bitcast(U8).indirect(entries(idx1, part)))
+
+        gather_v(halves[0])
+        order_w1(0)
+        gather_v(halves[1])
         order_w1(1)
 
-        pages = {}
-        late_tags = {5: "tab2_sb0", 6: "tab2_sb1", 7: "tab2_plane"}
+        bulk_order = [(0, 0), (1, 0), (0, 1), (0, 2), (1, 2), (0, 3), (1, 1), (1, 3)]
+        cover, last = bulk_order[-2:]
+        pages, response, weight = {}, {}, {}
 
-        def bulk_page(step, parts):
-            t, b = divmod(step, 2)
+        def respond(step, page, part, index):
+            b, t = page
             i = PACK * b + t
-            pages[i] = held([P, T2], F32, "page%d" % i, tag=late_tags.get(step))
-            response = held([P, S], F32, "response%d" % i, tag="left%d" % step)
-            weight = held([P, S], F32, "weight%d" % i, tag="right%d" % step)
-            gain_col = gain_sb[b][t]
-            rest = parts[-1]
-            nc.gpsimd.tensor_scalar(weight[:, rest], wg1_sb[t][:, rest], gain_col, 0.0, MULT, ADD)
-            for n, part in enumerate(parts):
-                acc = bank(step + 7 * n, "h1_acc%d_%d" % (i, n))
-                nc.tensor.matmul_mx(
-                    out=acc[:, part], lhsT=w1_ord[:, 2 * P * i : 2 * P * (i + 1)].bitcast(FP4X4),
-                    lhsT_scale=w1_sc[:, P * i : P * (i + 1)],
-                    rhs=v_words[:, part].bitcast(FP8X4), rhs_scale=v_scales[:, part], start=True, stop=True,
+            acc = bank(index, "h1_acc%d_%d" % (i, part.start))
+            nc.tensor.matmul_mx(
+                out=acc[:, part], lhsT=w1_ord[:, 2 * P * i : 2 * P * (i + 1)].bitcast(FP4X4),
+                lhsT_scale=w1_sc[:, P * i : P * (i + 1)],
+                rhs=v_words[:, part].bitcast(FP8X4), rhs_scale=v_scales[:, part], start=True, stop=True,
+            )
+            nc.scalar.activation(response[page][:, part], acc[:, part], ACT.Tanh)
+
+        def weigh(page, part):
+            b, t = page
+            nc.gpsimd.tensor_scalar(weight[page][:, part], wg1_sb[t][:, part], gain_sb[b][t], 0.0, MULT, ADD)
+            if page != last:
+                nc.gpsimd.tensor_tensor(weight[page][:, part], response[page][:, part], weight[page][:, part], MULT)
+
+        def place_bulk(page, part):
+            nc.vector.tensor_copy(pages[page][:].indirect(entries(idx3, part)), weight[page][:, part])
+
+        for step, page in enumerate(bulk_order):
+            name = "%d%d" % page
+            response[page] = held([P, S], F32, "response" + name)
+            if page != cover:
+                pages[page] = held([P, T2], F32, "page" + name)
+            weight[page] = held([P, S], F32, "weight" + name)
+            if step == 0:
+                respond(step, page, halves[0], 0)
+                nc.vector.scalar_tensor_tensor(
+                    weight[page][:, halves[0]], response[page][:, halves[0]], gain_sb[0][0], wg1_sb[0][:, halves[0]],
+                    MULT, MULT,
                 )
-                nc.scalar.activation(response[:, part], acc[:, part], ACT.Tanh)
-                if part is rest:
-                    nc.gpsimd.tensor_tensor(weight[:, part], response[:, part], weight[:, part], MULT)
-                else:
-                    nc.vector.scalar_tensor_tensor(
-                        weight[:, part], response[:, part], gain_col, wg1_sb[t][:, part], MULT, MULT,
-                    )
-                nc.vector.tensor_copy(pages[i][:].indirect(entries(idx3, part)), weight[:, part])
+                place_bulk(page, halves[0])
+                respond(step, page, halves[1], 7)
+                weigh(page, halves[1])
+                place_bulk(page, halves[1])
+            else:
+                respond(step, page, whole, step)
+                weigh(page, whole)
+                if page not in (cover, last):
+                    place_bulk(page, whole)
 
-        w2_q = {}
-
-        def quantize_w2(b):
+        w2_grouped = []
+        for b in range(2):
+            grouped = held([P, 2, PACK * 512], BF16, "w2_grouped%d" % b)
             for a in range(2):
-                grouped = held([P, PACK * 512], BF16, "w2_grouped%d%d" % (a, b))
                 nc.scalar.copy(
-                    grouped[:].rearrange("p (t m e j) -> p m t e j", t=PACK, e=2, j=PACK),
-                    w2_raw[a, b][:].rearrange("p j (m t e) -> p m t e j", t=PACK, e=2),
+                    grouped[:, a, :].rearrange("p (t m e j) -> p m t e j", t=PACK, e=2, j=PACK),
+                    w2_raw[b][a][:].rearrange("p j (m t e) -> p m t e j", t=PACK, e=2),
                 )
-                w2_q[a, b] = quantize(grouped[:], 512, "w2_%d%d" % (a, b))
+            w2_grouped.append(grouped)
 
-        whole = slice(0, S)
-        bulk_page(0, halves)
-        for step in range(1, 4):
-            bulk_page(step, [whole])
-        quantize_w2(0)
-        bulk_page(4, [whole])
+        def order_w3(b, tag):
+            ordered = held([P, 2 * 512], U32, "w3_ord%d" % b, tag=tag)
+            nc.vector.tensor_copy(
+                ordered[:].rearrange("p (a t m e) -> p a t m e", t=PACK, m=P // 2, e=2),
+                w3_sb[b][:].bitcast(U32).rearrange("p a (m t e) -> p a t m e", t=PACK, e=2),
+            )
+            return ordered
 
-        quantize_w2(1)
+        def quantize_w2(b, tag=None, kib=None):
+            return quantize(w2_grouped[b][:].rearrange("p a c -> p (a c)"), 2 * 512, "w2_%d" % b, tag=tag, kib=kib)
 
-        load_scale_rows(w3_plane, w3_scales, range(4))
-        load_scale_rows(tab2_plane, tab2_scales, range(4))
-        w3_sb = [load_words(w3_words[a], H, "w3_sb%d" % a) for a in range(2)]
-        tab2_sb = [load_words(tab2_words[a], T, "tab2_sb%d" % a) for a in range(2)]
-        idx2 = load_list(offs2, "idx2")
-        wg2_sb = load_site_weights(wg2, range(PACK), "wg2_sb")
-        idx4 = load_list(offs4, "idx4")
-        bias_sb = load_row_values(nc.sync, bias, "bias_sb")
-        w4_raw = []
-        for a in range(2):
-            raw = held([P, PACK, N], F32, "w4_raw%d" % a)
-            rows = w4[K_PASS * a : K_PASS * (a + 1), :].rearrange("(m t e) c -> e m t c", t=PACK, e=2)
-            for e in range(2):
-                nc.sync.dma_start(raw[e:P:2], rows[e])
-            w4_raw.append(raw)
-
+        w2_q = [quantize_w2(0, "response%d%d" % bulk_order[-3])]
         w3_sc = held([P, H], U8, "w3_sc")
         reorder_pairs(w3_sc[:].bitcast(U16), w3_plane[:].bitcast(U16), 8)
-        w3_ord = held([P, 2 * H], U32, "w3_ord")
-        for a in range(2):
-            reorder_words(w3_ord[:, H * a : H * (a + 1)], w3_sb[a][:].bitcast(U32))
-
-        v2_words = held([P, 2 * S], U32, "v2_words", tag="raw1")
+        w3_ord = [order_w3(0, None)]
+        v2_scales = held([P, S], U8, "v2_scales", tag="response%d%d" % bulk_order[-4])
+        nc.vector.tensor_copy(v2_scales[:], tab2_plane[:].bitcast(U8).indirect(idx2[:]))
+        v2_words = held([P, 2 * S], U32, "v2_words", tag="w2_grouped0")
         for a in range(2):
             nc.vector.tensor_copy(v2_words[:, S * a : S * (a + 1)], tab2_sb[a][:].bitcast(U32).indirect(idx2[:]))
-        v2_scales = held([P, S], U8, "v2_scales")
-        nc.vector.tensor_copy(v2_scales[:], tab2_plane[:].bitcast(U8).indirect(idx2[:]))
+        w3_ord.append(order_w3(1, "tab2_plane"))
+        w2_q.append(quantize_w2(1, kib=32))
+        w4_grouped = [held([P, N, PACK], BF16, "w4_grouped0")]
+        nc.scalar.copy(
+            w4_grouped[0][:].rearrange("p (c i) j -> p c j i", i=4), w4_raw[0][:].rearrange("p j (c i) -> p c j i", i=4),
+        )
+        w4_q = [quantize(w4_grouped[0][:].rearrange("p c j -> p (c j)"), N, "w4_0", kib=36)]
+        pages[cover] = held([P, T2], F32, "page_cover", tag="tab2_sb0")
+        place_bulk(cover, whole)
 
-        for step in range(5, PAGES):
-            bulk_page(step, [whole])
+        sums = placed([P, 4, PACK, S], F32, "sums", 0)
+        first = [sums[:, b] for b in range(2)]
+        second = [sums[:, 2 + b] for b in range(2)]
+        boundary_order = [(0, 0), (0, 1), (0, 2), (0, 3), (1, 2), (1, 0), (1, 1), (1, 3)]
 
-        def product(acc, operands):
-            for a, (codes, scales) in enumerate(operands):
-                nc.tensor.matmul_mx(
-                    out=acc[:], lhsT=codes.bitcast(FP8X4), lhsT_scale=scales,
-                    rhs=v2_words[:, S * a : S * (a + 1)].bitcast(FP8X4), rhs_scale=v2_scales[4 * a :, :],
-                    start=a == 0, stop=a == 1,
+        def boundary_product(step):
+            b, t = boundary_order[step]
+            accs = [bank(2 * step + n, "bnd_acc%d%d%d" % (b, t, n)) for n in range(2)]
+            for a in range(2):
+                cols = slice(512 * a + P * t, 512 * a + P * (t + 1))
+                own = slice(512 * b + P * t, 512 * b + P * (t + 1))
+                operands = [(w2_q[b][0][:, cols], w2_q[b][1][:, cols]), (w3_ord[b][:, cols], w3_sc[4 * a :, own])]
+                for acc, (codes, scales) in zip(accs, operands):
+                    nc.tensor.matmul_mx(
+                        out=acc[:], lhsT=codes.bitcast(FP8X4), lhsT_scale=scales,
+                        rhs=v2_words[:, S * a : S * (a + 1)].bitcast(FP8X4), rhs_scale=v2_scales[4 * a :, :],
+                        start=a == 0, stop=a == 1,
+                    )
+            nc.scalar.copy(first[b][:, t, :], accs[0][:])
+            nc.scalar.copy(second[b][:, t, :], accs[1][:])
+            weighed = held([P, S], F32, "weighed%d" % step, tag="weighed%d" % (step % 2))
+            nc.gpsimd.tensor_tensor(weighed[:], first[b][:, t, :], wg2_sb[t], MULT)
+            nc.gpsimd.tensor_tensor(second[b][:, t, :], weighed[:], second[b][:, t, :], MULT)
+
+        ahead = 6
+        for step in range(ahead):
+            boundary_product(step)
+        pairs = held([P, 2, T2, 2], BF16, "pairs", tag="w3_ord0")
+        z = [held([P, T2, PACK], BF16, "z%d" % b, tag=("tab_sb", "w2_grouped1")[b]) for b in range(2)]
+        for step, page in enumerate(boundary_order):
+            b, t = page
+            nc.vector.tensor_copy(pages[page][:].indirect(idx4[:]), second[b][:, t, :])
+            if page != last:
+                target = pairs[:, t // 2, :, t % 2] if b == 0 else z[1][:, :, t]
+                nc.scalar.activation(target, pages[page][:], ACT.Identity, bias=bias_sb[b][t])
+            if page == (1, PACK - 2):
+                nc.scalar.copy(
+                    z[0][:].rearrange("p c j -> p (c j)").bitcast(U32).rearrange("p (c i u) -> p c u i", i=4, u=2),
+                    pairs[:].rearrange("p u c e -> p (u c e)").bitcast(U32).rearrange("p (u c i) -> p c u i", i=4, u=2),
                 )
+            if step + ahead < len(boundary_order):
+                boundary_product(step + ahead)
 
-        first = [held([P, PACK, S], F32, "first%d" % b, tag="raw%d" % (2 + b)) for b in range(2)]
-        second = [held([P, PACK, S], F32, "second%d" % b, tag=("raw0", "tab_sb")[b]) for b in range(2)]
-        last = PAGES - 1
-        order = [0, 6, 1, 2, 3, 4, 5, 7]
-        early, late = slice(0, S - 64), slice(S - 64, S)
-        weighed = []
-        for step, i in enumerate(order):
-            b, t = divmod(i, PACK)
-            cols = slice(P * t, P * (t + 1))
-            acc = bank(2 * step, "w2_acc%d" % i)
-            product(acc, [(w2_q[a, b][0][:, cols], w2_q[a, b][1][:, cols]) for a in range(2)])
-            nc.scalar.copy(first[b][:, t, :], acc[:])
-            cols = slice(P * i, P * (i + 1))
-            acc = bank(2 * step + 1, "w3_acc%d" % i)
-            product(acc, [(w3_ord[:, H * a + P * i : H * a + P * (i + 1)], w3_sc[4 * a :, cols]) for a in range(2)])
-            nc.scalar.copy(second[b][:, t, :], acc[:])
-            part = early if step == last else whole
-            h2 = held([P, S], F32, "h2_%d" % i, tag="h2_%d" % (step % 2))
-            nc.gpsimd.tensor_tensor(h2[:, part], first[b][:, t, part], second[b][:, t, part], MULT)
-            ready = held([P, S], F32, "ready%d" % i, tag="left%d" % step)
-            nc.gpsimd.tensor_tensor(ready[:, part], h2[:, part], wg2_sb[t][:, part], MULT)
-            weighed.append(ready)
+        w4_grouped.append(held([P, N, PACK], BF16, "w4_grouped1", tag="weighed0"))
+        nc.gpsimd.tensor_scalar(w4_grouped[1][:], w4_raw[1][:].rearrange("p j c -> p c j"), 1.0, 0.0, MULT, ADD)
+        z0_q = quantize(z[0][:].rearrange("p c j -> p (c j)"), T2, "z0", tag="weighed1")
+        w4_q.append(quantize(w4_grouped[1][:].rearrange("p c j -> p (c j)"), N, "w4_1"))
+        final = held([P, S], F32, "final", tag="w3_ord0")
+        nc.gpsimd.tensor_tensor(final[:], response[last][:], weight[last][:], MULT)
+        nc.vector.tensor_copy(pages[last][:].indirect(idx3[:]), final[:])
 
-        w4_grouped = []
-        for a in range(2):
-            grouped = held([P, PACK * N], BF16, "w4_grouped%d" % a, tag="w2_grouped%d0" % a)
-            nc.scalar.copy(
-                grouped[:].rearrange("p (c i j) -> p c j i", i=4, j=PACK),
-                w4_raw[a][:].rearrange("p j (c i) -> p c j i", i=4),
-            )
-            w4_grouped.append(grouped)
-        w4_q = {}
-
-        pairs = held([P, 2, T2, 2], BF16, "pairs", tag="w3_ord")
-        z0 = [held([P, T2 // 2, PACK], BF16, "z0_%d" % n) for n in range(2)]
-        z1 = held([P, T2, PACK], BF16, "z1", tag="raw1")
         edges = [0, CHUNK // 2] + list(range(CHUNK, T2 + 1, CHUNK))
         chunks = [slice(lo, hi) for lo, hi in zip(edges, edges[1:])]
-        z_q = {}
-
-        def quantize_z0(n, tag):
-            codes = held([P, T2 // 2], U32, "z0_codes%d" % n, tag=tag)
-            scales = held([P, T2 // 2], U8, "z0_scales%d" % n)
-            nc.vector.quantize_mx(
-                out=codes[:].bitcast(FP8X4), scales=scales[:], in_=z0[n][:].rearrange("p c j -> p (c j)"),
-            )
-            for c, cols in enumerate(chunks):
-                if cols.start // (T2 // 2) == n:
-                    own = slice(cols.start - n * T2 // 2, cols.stop - n * T2 // 2)
-                    z_q[0, c] = (codes[:, own], scales[:, own])
-
-        for step, i in enumerate(order[:last]):
-            b, t = divmod(i, PACK)
-            nc.vector.tensor_copy(pages[i][:].indirect(idx4[:]), weighed[step][:])
-            target = pairs[:, t // 2, :, t % 2] if b == 0 else z1[:, :, t]
-            nc.scalar.activation(target, pages[i][:], ACT.Identity, bias=bias_sb[b][t])
-            if i == PACK - 1:
-                words = pairs[:].rearrange("p u c e -> p (u c e)").bitcast(U32).rearrange("p (u n c i) -> p n c u i", i=4, n=2, u=2)
-                for n in range(2):
-                    nc.scalar.copy(
-                        z0[n][:].rearrange("p c j -> p (c j)").bitcast(U32).rearrange("p (c i u) -> p c u i", i=4, u=2),
-                        words[:, n],
-                    )
-            if step == last - 3:
-                w4_q[1] = quantize(w4_grouped[1][:], N, "w4_1", tag="left%d" % step)
-        quantize_z0(0, "left%d" % (last - 2))
-        h2 = held([P, late.stop - late.start], F32, "h2_late", tag="z0_0")
-        nc.vector.tensor_tensor(h2[:], first[1][:, PACK - 1, late], second[1][:, PACK - 1, late], MULT)
-        quantize_z0(1, None)
-        nc.vector.tensor_tensor(weighed[last][:, late], h2[:], wg2_sb[PACK - 1][:, late], MULT)
-        w4_q[0] = quantize(w4_grouped[0][:], 512, "w4_0", tag="left%d" % (last - 1))
-        nc.vector.tensor_copy(pages[last][:].indirect(idx4[:]), weighed[last][:])
-
         accs = {}
 
         def groups(c):
             width = chunks[c].stop - chunks[c].start
-            tiles = 512 // width
+            tiles = BANK // width
             return [range(n, n + tiles) for n in range(0, N // P, tiles)], width
 
-        def reader_pass(b, c, tiles, width):
+        def reader_pass(b, c, tiles, width, z_codes, z_sc):
             if b == 0:
                 accs[c, tiles[0]] = bank(len(accs), "out_acc%d%d" % (c, tiles[0]))
-            w_codes, w_sc = w4_q[b]
-            z_codes, z_sc = z_q[b, c]
             for h, n in enumerate(tiles):
                 n_cols = slice(P * n, P * (n + 1))
                 nc.tensor.matmul_mx(
-                    out=accs[c, tiles[0]][:, width * h : width * (h + 1)], lhsT=w_codes[:, n_cols].bitcast(FP8X4),
-                    lhsT_scale=w_sc[:, n_cols], rhs=z_codes[:, :].bitcast(FP8X4), rhs_scale=z_sc[:, :],
+                    out=accs[c, tiles[0]][:, width * h : width * (h + 1)], lhsT=w4_q[b][0][:, n_cols].bitcast(FP8X4),
+                    lhsT_scale=w4_q[b][1][:, n_cols], rhs=z_codes.bitcast(FP8X4), rhs_scale=z_sc,
                     start=b == 0 and n == tiles[0], stop=b == 1 and n == tiles[-1],
                 )
 
-        for c in range(len(chunks)):
+        for c, cols in enumerate(chunks):
             sets, width = groups(c)
             for tiles in sets:
-                reader_pass(0, c, tiles, width)
+                reader_pass(0, c, tiles, width, z0_q[0][:, cols], z0_q[1][:, cols])
         out_rows = out.rearrange("(n p) t -> p n t", p=P)
-
         last_bias = bias_sb[1][PACK - 1]
 
         def last_z(c):
             cols = chunks[c]
             if c + 1 < len(chunks):
-                nc.vector.tensor_scalar_add(z1[:, cols, PACK - 1], pages[last][:, cols], last_bias)
+                nc.vector.tensor_scalar_add(z[1][:, cols, PACK - 1], pages[last][:, cols], last_bias)
             else:
-                nc.scalar.activation(z1[:, cols, PACK - 1], pages[last][:, cols], ACT.Identity, bias=last_bias)
+                nc.scalar.activation(z[1][:, cols, PACK - 1], pages[last][:, cols], ACT.Identity, bias=last_bias)
 
+        z1_q = []
         last_z(0)
         for c, cols in enumerate(chunks):
             if c + 1 < len(chunks):
                 last_z(c + 1)
-            z_q[1, c] = quantize(z1[:, cols, :].rearrange("p c j -> p (c j)"), cols.stop - cols.start, "z1%d" % c)
+            z1_q.append(quantize(z[1][:, cols, :].rearrange("p c j -> p (c j)"), cols.stop - cols.start, "z1%d" % c))
         stores = 0
         for c in range(len(chunks)):
             sets, width = groups(c)
             for tiles in sets:
-                reader_pass(1, c, tiles, width)
-                result = held([P, len(tiles), width], F32, "result%d" % stores, tag="right%d" % stores)
+                reader_pass(1, c, tiles, width, z1_q[c][0][:], z1_q[c][1][:])
+                result = held([P, len(tiles), width], F32, "result%d" % stores, tag="response%d%d" % bulk_order[stores])
                 flat = result[:].rearrange("p h t -> p (h t)")
                 if stores >= 3 and stores % 2 == 1:
                     nc.vector.tensor_copy(flat, accs[c, tiles[0]][:])

@@ -156,11 +156,10 @@ def tile_list_grain_boundary_segregation_kernel(
             load_words(tab2_words[1], placed([P, T], I32, "tab2_sb1", 32)),
         ]
         idx2 = load_list(offs2, "idx2")
-        w4_raw = [load_w4(0, placed([P, PACK, N], F32, "w4_raw0", 0))]
+        w4_raw = [load_w4(a, placed([P, PACK, N], F32, "w4_raw%d" % a, 8 * a)) for a in range(2)]
         wg2_sb = load_site_slot(wg2, 0, "wg2_0") + load_site_slots(wg2, range(1, PACK), "wg2_rest")
         idx4 = load_list(offs4, "idx4")
         bias_sb = load_row_values(bias, "bias_sb")
-        w4_raw.append(load_w4(1, held([P, PACK, N], F32, "w4_raw1")))
 
         w1_ord = held([P, 2 * H], U8, "w1_ord")
         w1_sc = held([P, H], U8, "w1_sc")
@@ -261,10 +260,14 @@ def tile_list_grain_boundary_segregation_kernel(
             nc.vector.tensor_copy(v2_words[:, S * a : S * (a + 1)], tab2_sb[a][:].bitcast(U32).indirect(idx2[:]))
         w3_ord.append(order_w3(1, "tab2_plane"))
         w2_q.append(quantize_w2(1, kib=32))
-        w4_grouped = [held([P, N, PACK], BF16, "w4_grouped0")]
-        nc.scalar.copy(
-            w4_grouped[0][:].rearrange("p (c i) j -> p c j i", i=4), w4_raw[0][:].rearrange("p j (c i) -> p c j i", i=4),
-        )
+        def round_w4(a):
+            grouped = held([P, N, PACK], BF16, "w4_grouped%d" % a)
+            nc.scalar.copy(
+                grouped[:].rearrange("p (c i) j -> p c j i", i=4), w4_raw[a][:].rearrange("p j (c i) -> p c j i", i=4),
+            )
+            return grouped
+
+        w4_grouped = [round_w4(a) for a in range(2)]
         w4_q = [quantize(w4_grouped[0][:].rearrange("p c j -> p (c j)"), N, "w4_0", kib=36)]
         pages[cover] = held([P, T2], F32, "page_cover", tag="tab2_sb0")
         place_bulk(cover, whole)
@@ -312,10 +315,8 @@ def tile_list_grain_boundary_segregation_kernel(
             if step + ahead < len(boundary_order):
                 boundary_product(step + ahead)
 
-        w4_grouped.append(held([P, N, PACK], BF16, "w4_grouped1", tag="weighed0"))
-        nc.gpsimd.tensor_scalar(w4_grouped[1][:], w4_raw[1][:].rearrange("p j c -> p c j"), 1.0, 0.0, MULT, ADD)
+        w4_q.append(quantize(w4_grouped[1][:].rearrange("p c j -> p (c j)"), N, "w4_1", tag="weighed0"))
         z0_q = quantize(z[0][:].rearrange("p c j -> p (c j)"), T2, "z0", tag="weighed1")
-        w4_q.append(quantize(w4_grouped[1][:].rearrange("p c j -> p (c j)"), N, "w4_1"))
         final = held([P, S], F32, "final", tag="w3_ord0")
         nc.gpsimd.tensor_tensor(final[:], response[last][:], weight[last][:], MULT)
         nc.vector.tensor_copy(pages[last][:].indirect(idx3[:]), final[:])

@@ -309,8 +309,8 @@ def tile_list_grain_boundary_segregation_kernel(
                 nc.scalar.activation(target, pages[page][:], ACT.Identity, bias=bias_sb[b][t])
             if page == (1, PACK - 2):
                 nc.scalar.copy(
-                    z[0][:].rearrange("p c j -> p (c j)").bitcast(U32).rearrange("p (c i u) -> p c u i", i=4, u=2),
-                    pairs[:].rearrange("p u c e -> p (u c e)").bitcast(U32).rearrange("p (u c i) -> p c u i", i=4, u=2),
+                    z[0][:].rearrange("p c j -> p (c j)").bitcast(U32).rearrange("p (c u) -> p c u", u=2),
+                    pairs[:].rearrange("p u c e -> p (u c e)").bitcast(U32).rearrange("p (u c) -> p c u", u=2),
                 )
             if step + ahead < len(boundary_order):
                 boundary_product(step + ahead)

@@ -41,7 +41,7 @@ def tile_list_grain_boundary_segregation_kernel(
             return keep.tile(shape, dtype, name=name, tag=tag or name, align_bytes=64)
 
         def placed(shape, dtype, name, kib):
-            return shared.tile(shape, dtype, name=name, align_bytes=64, offset=1024 * kib)
+            return shared.tile(shape, dtype, name=name, align_bytes=64, offset=int(1024 * kib))
 
         def bank(index, name):
             return psum.tile([P, BANK], F32, name=name, tag="bank%d" % (index % 8))
@@ -87,7 +87,7 @@ def tile_list_grain_boundary_segregation_kernel(
         def load_w2(b):
             tiles = []
             for a in range(2):
-                tile = placed([P, PACK, 512], F32, "w2_raw%d%d" % (a, b), 8 * (2 * b + a))
+                tile = placed([P, PACK, 512], F32, "w2_raw%d%d" % (a, b), 8 * (3 - 2 * b - a))
                 rows = w2[K_PASS * a : K_PASS * (a + 1), 512 * b : 512 * (b + 1)]
                 nc.sync.dma_start(tile[:], rows.rearrange("(p j) c -> p j c", j=PACK))
                 tiles.append(tile)
@@ -121,7 +121,7 @@ def tile_list_grain_boundary_segregation_kernel(
             return codes, scales
 
         tab_plane = held([P, T // 4], I32, "tab_plane")
-        w1_plane = held([P, H // 4], I32, "w1_plane")
+        w1_plane = placed([P, H // 4], I32, "w1_plane", 50.5)
         w3_plane = held([P, H // 4], I32, "w3_plane")
         tab2_plane = held([P, T // 4], I32, "tab2_plane")
         nc.vector.memset(tab_plane[:], 0)
@@ -145,42 +145,41 @@ def tile_list_grain_boundary_segregation_kernel(
         wg1_sb = wg1_sb + load_site_slot(wg1, 1, "wg1_1")
         w2_raw = [load_w2(0)]
         wg1_sb = wg1_sb + load_site_slots(wg1, range(2, PACK), "wg1_rest")
+        w3_sb = [load_w3(b) for b in range(2)]
         w2_raw.append(load_w2(1))
         for q in QUADRANTS:
             load_scale_rows(nc.sync, w3_plane, w3_scales, q)
-        w3_sb = [load_w3(b) for b in range(2)]
         for q in QUADRANTS:
             load_scale_rows(nc.sync, tab2_plane, tab2_scales, q)
         tab2_sb = [
             load_words(tab2_words[0], held([P, T], I32, "tab2_sb0")),
-            load_words(tab2_words[1], placed([P, T], I32, "tab2_sb1", 32)),
+            load_words(tab2_words[1], placed([P, T], I32, "tab2_sb1", 36)),
         ]
         idx2 = load_list(offs2, "idx2")
-        w4_raw = [load_w4(a, placed([P, PACK, N], F32, "w4_raw%d" % a, 8 * a)) for a in range(2)]
+        w4_raw = [load_w4(a, placed([P, PACK, N], F32, "w4_raw%d" % a, (28, 16)[a])) for a in range(2)]
         wg2_sb = load_site_slot(wg2, 0, "wg2_0") + load_site_slots(wg2, range(1, PACK), "wg2_rest")
         idx4 = load_list(offs4, "idx4")
         bias_sb = load_row_values(bias, "bias_sb")
 
         w1_ord = held([P, 2 * H], U8, "w1_ord")
         w1_sc = held([P, H], U8, "w1_sc")
-        v_scales = held([P, S], U8, "v_scales")
-        v_words = held([P, S], U32, "v_words")
         halves = [slice(0, S // 2), slice(S // 2, S)]
         whole = slice(0, S)
 
         def order_w1(b):
             cols = slice(256 * b, 256 * (b + 1))
             reorder_pairs(w1_ord[:].bitcast(U32)[:, cols], w1_sb[:].bitcast(U32)[:, cols], 4)
-            reorder_pairs(w1_sc[:].bitcast(U16)[:, cols], w1_plane[:].bitcast(U16)[:, cols], 8)
 
-        def gather_v(part):
-            nc.vector.tensor_copy(v_words[:, part], tab_sb[:].bitcast(U32).indirect(entries(idx1, part)))
-            nc.vector.tensor_copy(v_scales[:, part], tab_plane[:].bitcast(U8).indirect(entries(idx1, part)))
+        def gather_v(part, words, scales):
+            nc.vector.tensor_copy(words[:], tab_sb[:].bitcast(U32).indirect(entries(idx1, part)))
+            nc.vector.tensor_copy(scales[:], tab_plane[:].bitcast(U8).indirect(entries(idx1, part)))
+            return words, scales
 
-        gather_v(halves[0])
+        v_q = [gather_v(halves[0], held([P, S // 2], U32, "v_words0"), held([P, S // 2], U8, "v_scales0"))]
         order_w1(0)
-        gather_v(halves[1])
+        reorder_pairs(w1_sc[:].bitcast(U16), w1_plane[:].bitcast(U16), 8)
         order_w1(1)
+        v_q.append(gather_v(halves[1], placed([P, S // 2], U32, "v_words1", 50), placed([P, S // 2], U8, "v_scales1", 51)))
 
         bulk_order = [(0, 0), (1, 0), (0, 1), (0, 2), (1, 2), (0, 3), (1, 1), (1, 3)]
         cover, last = bulk_order[-2:]
@@ -190,11 +189,13 @@ def tile_list_grain_boundary_segregation_kernel(
             b, t = page
             i = PACK * b + t
             acc = bank(index, "h1_acc%d_%d" % (i, part.start))
-            nc.tensor.matmul_mx(
-                out=acc[:, part], lhsT=w1_ord[:, 2 * P * i : 2 * P * (i + 1)].bitcast(FP4X4),
-                lhsT_scale=w1_sc[:, P * i : P * (i + 1)],
-                rhs=v_words[:, part].bitcast(FP8X4), rhs_scale=v_scales[:, part], start=True, stop=True,
-            )
+            for half, (words, scales) in zip(halves, v_q):
+                if part.start <= half.start and half.stop <= part.stop:
+                    nc.tensor.matmul_mx(
+                        out=acc[:, half], lhsT=w1_ord[:, 2 * P * i : 2 * P * (i + 1)].bitcast(FP4X4),
+                        lhsT_scale=w1_sc[:, P * i : P * (i + 1)],
+                        rhs=words[:].bitcast(FP8X4), rhs_scale=scales[:], start=True, stop=True,
+                    )
             nc.scalar.activation(response[page][:, part], acc[:, part], ACT.Tanh)
 
         def weigh(page, part):
@@ -240,7 +241,7 @@ def tile_list_grain_boundary_segregation_kernel(
 
         def order_w3(b, tag):
             ordered = held([P, 2 * 512], U32, "w3_ord%d" % b, tag=tag)
-            nc.vector.tensor_copy(
+            nc.gpsimd.tensor_copy(
                 ordered[:].rearrange("p (a t m e) -> p a t m e", t=PACK, m=P // 2, e=2),
                 w3_sb[b][:].bitcast(U32).rearrange("p a (m t e) -> p a t m e", t=PACK, e=2),
             )
@@ -249,17 +250,15 @@ def tile_list_grain_boundary_segregation_kernel(
         def quantize_w2(b, tag=None, kib=None):
             return quantize(w2_grouped[b][:].rearrange("p a c -> p (a c)"), 2 * 512, "w2_%d" % b, tag=tag, kib=kib)
 
+        w3_ord = [order_w3(b, None) for b in range(2)]
         w2_q = [quantize_w2(0, "response%d%d" % bulk_order[-3])]
         w3_sc = held([P, H], U8, "w3_sc")
         reorder_pairs(w3_sc[:].bitcast(U16), w3_plane[:].bitcast(U16), 8)
-        w3_ord = [order_w3(0, None)]
         v2_scales = held([P, S], U8, "v2_scales", tag="response%d%d" % bulk_order[-4])
         nc.vector.tensor_copy(v2_scales[:], tab2_plane[:].bitcast(U8).indirect(idx2[:]))
         v2_words = held([P, 2 * S], U32, "v2_words", tag="w2_grouped0")
         for a in range(2):
             nc.vector.tensor_copy(v2_words[:, S * a : S * (a + 1)], tab2_sb[a][:].bitcast(U32).indirect(idx2[:]))
-        w3_ord.append(order_w3(1, "tab2_plane"))
-        w2_q.append(quantize_w2(1, kib=32))
         def round_w4(a):
             grouped = held([P, N, PACK], BF16, "w4_grouped%d" % a)
             nc.scalar.copy(
@@ -268,8 +267,9 @@ def tile_list_grain_boundary_segregation_kernel(
             return grouped
 
         w4_grouped = [round_w4(a) for a in range(2)]
-        w4_q = [quantize(w4_grouped[0][:].rearrange("p c j -> p (c j)"), N, "w4_0", kib=36)]
-        pages[cover] = held([P, T2], F32, "page_cover", tag="tab2_sb0")
+        w4_q = [quantize(w4_grouped[0][:].rearrange("p c j -> p (c j)"), N, "w4_0")]
+        w2_q.append(quantize_w2(1, kib=32))
+        pages[cover] = held([P, T2], F32, "page_cover", tag="w4_grouped0")
         place_bulk(cover, whole)
 
         sums = placed([P, 4, PACK, S], F32, "sums", 0)
@@ -292,7 +292,7 @@ def tile_list_grain_boundary_segregation_kernel(
                     )
             nc.scalar.copy(first[b][:, t, :], accs[0][:])
             nc.scalar.copy(second[b][:, t, :], accs[1][:])
-            weighed = held([P, S], F32, "weighed%d" % step, tag="weighed%d" % (step % 2))
+            weighed = placed([P, S], F32, "weighed%d" % step, 45)
             nc.gpsimd.tensor_tensor(weighed[:], first[b][:, t, :], wg2_sb[t], MULT)
             nc.gpsimd.tensor_tensor(second[b][:, t, :], weighed[:], second[b][:, t, :], MULT)
 
@@ -315,8 +315,8 @@ def tile_list_grain_boundary_segregation_kernel(
             if step + ahead < len(boundary_order):
                 boundary_product(step + ahead)
 
-        w4_q.append(quantize(w4_grouped[1][:].rearrange("p c j -> p (c j)"), N, "w4_1", tag="weighed0"))
-        z0_q = quantize(z[0][:].rearrange("p c j -> p (c j)"), T2, "z0", tag="weighed1")
+        w4_q.append(quantize(w4_grouped[1][:].rearrange("p c j -> p (c j)"), N, "w4_1", kib=44))
+        z0_q = quantize(z[0][:].rearrange("p c j -> p (c j)"), T2, "z0", kib=46)
         final = held([P, S], F32, "final", tag="w3_ord0")
         nc.gpsimd.tensor_tensor(final[:], response[last][:], weight[last][:], MULT)
         nc.vector.tensor_copy(pages[last][:].indirect(idx3[:]), final[:])

@@ -139,16 +139,16 @@ def tile_list_grain_boundary_segregation_kernel(
             load_scale_rows(nc.gpsimd, w1_plane, w1_scales, q)
         for plane in (tab2_plane, w3_plane):
             nc.gpsimd.memset(plane[:], 0)
-        idx3 = load_list(offs3, "idx3")
         wg1_sb = load_site_slot(wg1, 0, "wg1_0")
         gain_sb = load_row_values(gain, "gain_sb")
+        idx3 = load_list(offs3, "idx3")
         wg1_sb = wg1_sb + load_site_slot(wg1, 1, "wg1_1")
         w2_raw = [load_w2(0)]
         wg1_sb = wg1_sb + load_site_slots(wg1, range(2, PACK), "wg1_rest")
         w3_sb = [load_w3(b) for b in range(2)]
-        w2_raw.append(load_w2(1))
         for q in QUADRANTS:
             load_scale_rows(nc.sync, w3_plane, w3_scales, q)
+        w2_raw.append(load_w2(1))
         for q in QUADRANTS:
             load_scale_rows(nc.sync, tab2_plane, tab2_scales, q)
         tab2_sb = [
@@ -183,6 +183,7 @@ def tile_list_grain_boundary_segregation_kernel(
 
         bulk_order = [(0, 0), (1, 0), (0, 1), (0, 2), (1, 2), (0, 3), (1, 1), (1, 3)]
         cover, last = bulk_order[-2:]
+        early = len(bulk_order) - 2
         pages, response, weight = {}, {}, {}
 
         def respond(step, page, part, index):
@@ -209,7 +210,10 @@ def tile_list_grain_boundary_segregation_kernel(
 
         for step, page in enumerate(bulk_order):
             name = "%d%d" % page
-            response[page] = held([P, S], F32, "response" + name)
+            if step == early - 1:
+                response[page] = placed([P, S], F32, "response" + name, 55)
+            else:
+                response[page] = held([P, S], F32, "response" + name)
             if page != cover:
                 pages[page] = held([P, T2], F32, "page" + name)
             weight[page] = held([P, S], F32, "weight" + name)
@@ -239,8 +243,8 @@ def tile_list_grain_boundary_segregation_kernel(
                 )
             w2_grouped.append(grouped)
 
-        def order_w3(b, tag):
-            ordered = held([P, 2 * 512], U32, "w3_ord%d" % b, tag=tag)
+        def order_w3(b):
+            ordered = placed([P, 2 * 512], U32, "w3_ord%d" % b, (58, 66)[b])
             nc.gpsimd.tensor_copy(
                 ordered[:].rearrange("p (a t m e) -> p a t m e", t=PACK, m=P // 2, e=2),
                 w3_sb[b][:].bitcast(U32).rearrange("p a (m t e) -> p a t m e", t=PACK, e=2),
@@ -250,10 +254,13 @@ def tile_list_grain_boundary_segregation_kernel(
         def quantize_w2(b, tag=None, kib=None):
             return quantize(w2_grouped[b][:].rearrange("p a c -> p (a c)"), 2 * 512, "w2_%d" % b, tag=tag, kib=kib)
 
-        w3_ord = [order_w3(b, None) for b in range(2)]
-        w2_q = [quantize_w2(0, "response%d%d" % bulk_order[-3])]
+        w3_ord = [order_w3(b) for b in range(2)]
         w3_sc = held([P, H], U8, "w3_sc")
-        reorder_pairs(w3_sc[:].bitcast(U16), w3_plane[:].bitcast(U16), 8)
+        nc.gpsimd.tensor_copy(
+            w3_sc[:].rearrange("p (b t m e) -> p b t m e", t=PACK, m=P // 2, e=2),
+            w3_plane[:].bitcast(U8).rearrange("p (b m t e) -> p b t m e", t=PACK, m=P // 2, e=2),
+        )
+        w2_q = [quantize_w2(0, kib=52)]
         v2_scales = held([P, S], U8, "v2_scales", tag="response%d%d" % bulk_order[-4])
         nc.vector.tensor_copy(v2_scales[:], tab2_plane[:].bitcast(U8).indirect(idx2[:]))
         v2_words = held([P, 2 * S], U32, "v2_words", tag="w2_grouped0")
@@ -299,7 +306,7 @@ def tile_list_grain_boundary_segregation_kernel(
         ahead = 6
         for step in range(ahead):
             boundary_product(step)
-        pairs = held([P, 2, T2, 2], BF16, "pairs", tag="w3_ord0")
+        pairs = placed([P, 2, T2, 2], BF16, "pairs", 58)
         z = [held([P, T2, PACK], BF16, "z%d" % b, tag=("tab_sb", "w2_grouped1")[b]) for b in range(2)]
         for step, page in enumerate(boundary_order):
             b, t = page
@@ -315,62 +322,79 @@ def tile_list_grain_boundary_segregation_kernel(
             if step + ahead < len(boundary_order):
                 boundary_product(step + ahead)
 
-        w4_q.append(quantize(w4_grouped[1][:].rearrange("p c j -> p (c j)"), N, "w4_1", kib=44))
         z0_q = quantize(z[0][:].rearrange("p c j -> p (c j)"), T2, "z0", kib=46)
-        final = held([P, S], F32, "final", tag="w3_ord0")
+        final = placed([P, S], F32, "final", 58)
         nc.gpsimd.tensor_tensor(final[:], response[last][:], weight[last][:], MULT)
         nc.vector.tensor_copy(pages[last][:].indirect(idx3[:]), final[:])
 
-        edges = [0, CHUNK // 2] + list(range(CHUNK, T2 + 1, CHUNK))
-        chunks = [slice(lo, hi) for lo, hi in zip(edges, edges[1:])]
+        chunks = [slice(lo, lo + CHUNK) for lo in range(0, T2, CHUNK)]
+        per_bank = BANK // CHUNK
         accs = {}
 
-        def groups(c):
-            width = chunks[c].stop - chunks[c].start
-            tiles = BANK // width
-            return [range(n, n + tiles) for n in range(0, N // P, tiles)], width
-
-        def reader_pass(b, c, tiles, width, z_codes, z_sc):
+        def reader_pass(b, c, pair, w_codes, w_sc, z_codes, z_sc):
             if b == 0:
-                accs[c, tiles[0]] = bank(len(accs), "out_acc%d%d" % (c, tiles[0]))
-            for h, n in enumerate(tiles):
-                n_cols = slice(P * n, P * (n + 1))
+                accs[c, pair] = bank(len(accs), "out_acc%d%d" % (c, pair))
+            for h in range(per_bank):
+                n_cols = slice(P * h, P * (h + 1))
                 nc.tensor.matmul_mx(
-                    out=accs[c, tiles[0]][:, width * h : width * (h + 1)], lhsT=w4_q[b][0][:, n_cols].bitcast(FP8X4),
-                    lhsT_scale=w4_q[b][1][:, n_cols], rhs=z_codes.bitcast(FP8X4), rhs_scale=z_sc,
-                    start=b == 0 and n == tiles[0], stop=b == 1 and n == tiles[-1],
+                    out=accs[c, pair][:, CHUNK * h : CHUNK * (h + 1)], lhsT=w_codes[:, n_cols].bitcast(FP8X4),
+                    lhsT_scale=w_sc[:, n_cols], rhs=z_codes.bitcast(FP8X4), rhs_scale=z_sc,
+                    start=b == 0 and h == 0, stop=b == 1 and h == per_bank - 1,
                 )
 
         for c, cols in enumerate(chunks):
-            sets, width = groups(c)
-            for tiles in sets:
-                reader_pass(0, c, tiles, width, z0_q[0][:, cols], z0_q[1][:, cols])
+            for pair in range(2):
+                own = slice(N // 2 * pair, N // 2 * (pair + 1))
+                reader_pass(0, c, pair, w4_q[0][0][:, own], w4_q[0][1][:, own], z0_q[0][:, cols], z0_q[1][:, cols])
         out_rows = out.rearrange("(n p) t -> p n t", p=P)
         last_bias = bias_sb[1][PACK - 1]
 
         def last_z(c):
             cols = chunks[c]
-            if c + 1 < len(chunks):
-                nc.vector.tensor_scalar_add(z[1][:, cols, PACK - 1], pages[last][:, cols], last_bias)
-            else:
+            if c == 1:
                 nc.scalar.activation(z[1][:, cols, PACK - 1], pages[last][:, cols], ACT.Identity, bias=last_bias)
+            else:
+                nc.vector.tensor_scalar_add(z[1][:, cols, PACK - 1], pages[last][:, cols], last_bias)
 
-        z1_q = []
+        def quantize_w4_late(pair):
+            own = slice(N // 2 * pair, N // 2 * (pair + 1))
+            grouped = w4_grouped[1][:, own, :].rearrange("p c j -> p (c j)")
+            return quantize(grouped, N // 2, "w4_1%d" % pair, kib=58 + pair)
+
+        def quantize_z1(c):
+            return quantize(z[1][:, chunks[c], :].rearrange("p c j -> p (c j)"), CHUNK, "z1%d" % c)
+
         last_z(0)
-        for c, cols in enumerate(chunks):
-            if c + 1 < len(chunks):
-                last_z(c + 1)
-            z1_q.append(quantize(z[1][:, cols, :].rearrange("p c j -> p (c j)"), cols.stop - cols.start, "z1%d" % c))
-        stores = 0
+        last_z(1)
+        w4_late = [quantize_w4_late(0)]
+        z1_q = [quantize_z1(0)]
+        w4_late.append(quantize_w4_late(1))
+        z1_q.append(quantize_z1(1))
+        for c in range(2, len(chunks)):
+            last_z(c)
+        for c in range(2, len(chunks)):
+            z1_q.append(quantize_z1(c))
+        def copy_out(engine_copy, target, c, pair, tiles):
+            acc = accs[c, pair][:].rearrange("p (h t) -> p h t", t=CHUNK)
+            engine_copy(target, acc[:, tiles, :])
+
+        results = [held([P, N // P, CHUNK], F32, "result%d" % c, tag="page%d%d" % bulk_order[c]) for c in range(len(chunks))]
+
+        def store(c, tiles):
+            nc.sync.dma_start(out_rows[:, tiles, chunks[c]], results[c][:, tiles, :])
+
         for c in range(len(chunks)):
-            sets, width = groups(c)
-            for tiles in sets:
-                reader_pass(1, c, tiles, width, z1_q[c][0][:], z1_q[c][1][:])
-                result = held([P, len(tiles), width], F32, "result%d" % stores, tag="response%d%d" % bulk_order[stores])
-                flat = result[:].rearrange("p h t -> p (h t)")
-                if stores >= 3 and stores % 2 == 1:
-                    nc.vector.tensor_copy(flat, accs[c, tiles[0]][:])
-                else:
-                    nc.scalar.copy(flat, accs[c, tiles[0]][:])
-                nc.sync.dma_start(out_rows[:, tiles[0] : tiles[-1] + 1, chunks[c]], result[:])
-                stores = stores + 1
+            for pair in range(2):
+                reader_pass(1, c, pair, w4_late[pair][0][:], w4_late[pair][1][:], z1_q[c][0][:], z1_q[c][1][:])
+                tiles = slice(per_bank * pair, per_bank * (pair + 1))
+                if (c, pair) == (0, 0):
+                    for h in range(per_bank):
+                        copy_out(nc.scalar.copy, results[c][:, h : h + 1, :], c, pair, slice(h, h + 1))
+                        store(c, slice(h, h + 1))
+                    continue
+                on_vector = c >= 2 and pair == 1
+                copy_out(nc.vector.tensor_copy if on_vector else nc.scalar.copy, results[c][:, tiles, :], c, pair, slice(0, per_bank))
+                if c + 1 < len(chunks):
+                    store(c, tiles)
+                elif pair == 1:
+                    store(c, slice(0, N // P))

@@ -146,9 +146,9 @@ def tile_list_grain_boundary_segregation_kernel(
         w2_raw = [load_w2(0)]
         wg1_sb = wg1_sb + load_site_slots(wg1, range(2, PACK), "wg1_rest")
         w3_sb = [load_w3(b) for b in range(2)]
+        w2_raw.append(load_w2(1))
         for q in QUADRANTS:
             load_scale_rows(nc.sync, w3_plane, w3_scales, q)
-        w2_raw.append(load_w2(1))
         for q in QUADRANTS:
             load_scale_rows(nc.sync, tab2_plane, tab2_scales, q)
         tab2_sb = [
@@ -255,12 +255,9 @@ def tile_list_grain_boundary_segregation_kernel(
             return quantize(w2_grouped[b][:].rearrange("p a c -> p (a c)"), 2 * 512, "w2_%d" % b, tag=tag, kib=kib)
 
         w3_ord = [order_w3(b) for b in range(2)]
-        w3_sc = held([P, H], U8, "w3_sc")
-        nc.gpsimd.tensor_copy(
-            w3_sc[:].rearrange("p (b t m e) -> p b t m e", t=PACK, m=P // 2, e=2),
-            w3_plane[:].bitcast(U8).rearrange("p (b m t e) -> p b t m e", t=PACK, m=P // 2, e=2),
-        )
         w2_q = [quantize_w2(0, kib=52)]
+        w3_sc = placed([P, H], U8, "w3_sc", 56)
+        reorder_pairs(w3_sc[:].bitcast(U16), w3_plane[:].bitcast(U16), 8)
         v2_scales = held([P, S], U8, "v2_scales", tag="response%d%d" % bulk_order[-4])
         nc.vector.tensor_copy(v2_scales[:], tab2_plane[:].bitcast(U8).indirect(idx2[:]))
         v2_words = held([P, 2 * S], U32, "v2_words", tag="w2_grouped0")

@@ -143,10 +143,9 @@ def tile_list_grain_boundary_segregation_kernel(
         gain_sb = load_row_values(gain, "gain_sb")
         idx3 = load_list(offs3, "idx3")
         wg1_sb = wg1_sb + load_site_slot(wg1, 1, "wg1_1")
-        w2_raw = [load_w2(0)]
         wg1_sb = wg1_sb + load_site_slots(wg1, range(2, PACK), "wg1_rest")
         w3_sb = [load_w3(b) for b in range(2)]
-        w2_raw.append(load_w2(1))
+        w2_raw = [load_w2(b) for b in range(2)]
         for q in QUADRANTS:
             load_scale_rows(nc.sync, w3_plane, w3_scales, q)
         for q in QUADRANTS:
@@ -183,7 +182,7 @@ def tile_list_grain_boundary_segregation_kernel(
 
         bulk_order = [(0, 0), (1, 0), (0, 1), (0, 2), (1, 2), (0, 3), (1, 1), (1, 3)]
         cover, last = bulk_order[-2:]
-        early = len(bulk_order) - 2
+        response_kib = {3: 66, 4: 57, 5: 55}
         pages, response, weight = {}, {}, {}
 
         def respond(step, page, part, index):
@@ -201,7 +200,10 @@ def tile_list_grain_boundary_segregation_kernel(
 
         def weigh(page, part):
             b, t = page
-            nc.gpsimd.tensor_scalar(weight[page][:, part], wg1_sb[t][:, part], gain_sb[b][t], 0.0, MULT, ADD)
+            if t == 0:
+                nc.gpsimd.tensor_scalar(weight[page][:, part], wg1_sb[t][:, part], gain_sb[b][t], 0.0, MULT, ADD)
+            else:
+                nc.scalar.activation(weight[page][:, part], wg1_sb[t][:, part], ACT.Copy, scale=gain_sb[b][t])
             if page != last:
                 nc.gpsimd.tensor_tensor(weight[page][:, part], response[page][:, part], weight[page][:, part], MULT)
 
@@ -210,8 +212,8 @@ def tile_list_grain_boundary_segregation_kernel(
 
         for step, page in enumerate(bulk_order):
             name = "%d%d" % page
-            if step == early - 1:
-                response[page] = placed([P, S], F32, "response" + name, 55)
+            if step in response_kib:
+                response[page] = placed([P, S], F32, "response" + name, response_kib[step])
             else:
                 response[page] = held([P, S], F32, "response" + name)
             if page != cover:
@@ -258,7 +260,7 @@ def tile_list_grain_boundary_segregation_kernel(
         w2_q = [quantize_w2(0, kib=52)]
         w3_sc = placed([P, H], U8, "w3_sc", 56)
         reorder_pairs(w3_sc[:].bitcast(U16), w3_plane[:].bitcast(U16), 8)
-        v2_scales = held([P, S], U8, "v2_scales", tag="response%d%d" % bulk_order[-4])
+        v2_scales = placed([P, S], U8, "v2_scales", 57)
         nc.vector.tensor_copy(v2_scales[:], tab2_plane[:].bitcast(U8).indirect(idx2[:]))
         v2_words = held([P, 2 * S], U32, "v2_words", tag="w2_grouped0")
         for a in range(2):

@@ -155,10 +155,11 @@ def tile_list_grain_boundary_segregation_kernel(
             load_words(tab2_words[1], placed([P, T], I32, "tab2_sb1", 36)),
         ]
         idx2 = load_list(offs2, "idx2")
-        w4_raw = [load_w4(a, placed([P, PACK, N], F32, "w4_raw%d" % a, (28, 16)[a])) for a in range(2)]
+        w4_raw = [load_w4(0, placed([P, PACK, N], F32, "w4_raw0", 28))]
         wg2_sb = load_site_slot(wg2, 0, "wg2_0") + load_site_slots(wg2, range(1, PACK), "wg2_rest")
         idx4 = load_list(offs4, "idx4")
         bias_sb = load_row_values(bias, "bias_sb")
+        w4_raw.append(load_w4(1, held([P, PACK, N], F32, "w4_raw1")))
 
         w1_ord = held([P, 2 * H], U8, "w1_ord")
         w1_sc = held([P, H], U8, "w1_sc")
@@ -180,9 +181,9 @@ def tile_list_grain_boundary_segregation_kernel(
         order_w1(1)
         v_q.append(gather_v(halves[1], placed([P, S // 2], U32, "v_words1", 50), placed([P, S // 2], U8, "v_scales1", 51)))
 
-        bulk_order = [(0, 0), (1, 0), (0, 1), (0, 2), (1, 2), (0, 3), (1, 1), (1, 3)]
+        bulk_order = [(0, 0), (1, 0), (0, 1), (1, 1), (0, 2), (0, 3), (1, 2), (1, 3)]
         cover, last = bulk_order[-2:]
-        response_kib = {3: 66, 4: 57, 5: 55}
+        response_kib = {2: 64, 3: 61, 5: 55.5}
         pages, response, weight = {}, {}, {}
 
         def respond(step, page, part, index):
@@ -245,34 +246,33 @@ def tile_list_grain_boundary_segregation_kernel(
                 )
             w2_grouped.append(grouped)
 
-        def order_w3(b):
-            ordered = placed([P, 2 * 512], U32, "w3_ord%d" % b, (58, 66)[b])
-            nc.gpsimd.tensor_copy(
-                ordered[:].rearrange("p (a t m e) -> p a t m e", t=PACK, m=P // 2, e=2),
-                w3_sb[b][:].bitcast(U32).rearrange("p a (m t e) -> p a t m e", t=PACK, e=2),
+        w3_ord = {}
+
+        def order_w3(engine, b, a, kib):
+            w3_ord[b, a] = placed([P, 512], U32, "w3_ord%d%d" % (b, a), kib)
+            engine.tensor_copy(
+                w3_ord[b, a][:].rearrange("p (t m e) -> p t m e", t=PACK, e=2),
+                w3_sb[b][:, a, :].bitcast(U32).rearrange("p (m t e) -> p t m e", t=PACK, e=2),
             )
-            return ordered
 
         def quantize_w2(b, tag=None, kib=None):
             return quantize(w2_grouped[b][:].rearrange("p a c -> p (a c)"), 2 * 512, "w2_%d" % b, tag=tag, kib=kib)
 
-        w3_ord = [order_w3(b) for b in range(2)]
+        for n, (b, a) in enumerate(((0, 0), (0, 1), (1, 0))):
+            order_w3(nc.gpsimd, b, a, 60 + 2 * n)
         w2_q = [quantize_w2(0, kib=52)]
         w3_sc = placed([P, H], U8, "w3_sc", 56)
         reorder_pairs(w3_sc[:].bitcast(U16), w3_plane[:].bitcast(U16), 8)
-        v2_scales = placed([P, S], U8, "v2_scales", 57)
+        order_w3(nc.vector, 1, 1, 57)
+        v2_scales = held([P, S], U8, "v2_scales", tag="response%d%d" % bulk_order[4])
         nc.vector.tensor_copy(v2_scales[:], tab2_plane[:].bitcast(U8).indirect(idx2[:]))
         v2_words = held([P, 2 * S], U32, "v2_words", tag="w2_grouped0")
         for a in range(2):
             nc.vector.tensor_copy(v2_words[:, S * a : S * (a + 1)], tab2_sb[a][:].bitcast(U32).indirect(idx2[:]))
-        def round_w4(a):
-            grouped = held([P, N, PACK], BF16, "w4_grouped%d" % a)
-            nc.scalar.copy(
-                grouped[:].rearrange("p (c i) j -> p c j i", i=4), w4_raw[a][:].rearrange("p j (c i) -> p c j i", i=4),
-            )
-            return grouped
-
-        w4_grouped = [round_w4(a) for a in range(2)]
+        w4_grouped = [held([P, N, PACK], BF16, "w4_grouped0")]
+        nc.scalar.copy(
+            w4_grouped[0][:].rearrange("p (c i) j -> p c j i", i=4), w4_raw[0][:].rearrange("p j (c i) -> p c j i", i=4),
+        )
         w4_q = [quantize(w4_grouped[0][:].rearrange("p c j -> p (c j)"), N, "w4_0")]
         w2_q.append(quantize_w2(1, kib=32))
         pages[cover] = held([P, T2], F32, "page_cover", tag="w4_grouped0")
@@ -289,7 +289,7 @@ def tile_list_grain_boundary_segregation_kernel(
             for a in range(2):
                 cols = slice(512 * a + P * t, 512 * a + P * (t + 1))
                 own = slice(512 * b + P * t, 512 * b + P * (t + 1))
-                operands = [(w2_q[b][0][:, cols], w2_q[b][1][:, cols]), (w3_ord[b][:, cols], w3_sc[4 * a :, own])]
+                operands = [(w2_q[b][0][:, cols], w2_q[b][1][:, cols]), (w3_ord[b, a][:, P * t : P * (t + 1)], w3_sc[4 * a :, own])]
                 for acc, (codes, scales) in zip(accs, operands):
                     nc.tensor.matmul_mx(
                         out=acc[:], lhsT=codes.bitcast(FP8X4), lhsT_scale=scales,
@@ -305,7 +305,7 @@ def tile_list_grain_boundary_segregation_kernel(
         ahead = 6
         for step in range(ahead):
             boundary_product(step)
-        pairs = placed([P, 2, T2, 2], BF16, "pairs", 58)
+        pairs = placed([P, 2, T2, 2], BF16, "pairs", 60)
         z = [held([P, T2, PACK], BF16, "z%d" % b, tag=("tab_sb", "w2_grouped1")[b]) for b in range(2)]
         for step, page in enumerate(boundary_order):
             b, t = page
@@ -321,8 +321,10 @@ def tile_list_grain_boundary_segregation_kernel(
             if step + ahead < len(boundary_order):
                 boundary_product(step + ahead)
 
+        w4_grouped.append(placed([P, N, PACK], BF16, "w4_grouped1", 41.5))
+        nc.gpsimd.tensor_scalar(w4_grouped[1][:], w4_raw[1][:].rearrange("p j c -> p c j"), 1.0, 0.0, MULT, ADD)
         z0_q = quantize(z[0][:].rearrange("p c j -> p (c j)"), T2, "z0", kib=46)
-        final = placed([P, S], F32, "final", 58)
+        final = placed([P, S], F32, "final", 60)
         nc.gpsimd.tensor_tensor(final[:], response[last][:], weight[last][:], MULT)
         nc.vector.tensor_copy(pages[last][:].indirect(idx3[:]), final[:])
 
@@ -358,7 +360,7 @@ def tile_list_grain_boundary_segregation_kernel(
         def quantize_w4_late(pair):
             own = slice(N // 2 * pair, N // 2 * (pair + 1))
             grouped = w4_grouped[1][:, own, :].rearrange("p c j -> p (c j)")
-            return quantize(grouped, N // 2, "w4_1%d" % pair, kib=58 + pair)
+            return quantize(grouped, N // 2, "w4_1%d" % pair, kib=60 + pair)
 
         def quantize_z1(c):
             return quantize(z[1][:, chunks[c], :].rearrange("p c j -> p (c j)"), CHUNK, "z1%d" % c)
@@ -377,7 +379,7 @@ def tile_list_grain_boundary_segregation_kernel(
             acc = accs[c, pair][:].rearrange("p (h t) -> p h t", t=CHUNK)
             engine_copy(target, acc[:, tiles, :])
 
-        results = [held([P, N // P, CHUNK], F32, "result%d" % c, tag="page%d%d" % bulk_order[c]) for c in range(len(chunks))]
+        results = [held([P, N // P, CHUNK], F32, "result%d" % c, tag="page0%d" % c) for c in range(len(chunks))]
 
         def store(c, tiles):
             nc.sync.dma_start(out_rows[:, tiles, chunks[c]], results[c][:, tiles, :])

@@ -124,7 +124,8 @@ def tile_list_grain_boundary_segregation_kernel(
         w1_plane = placed([P, H // 4], I32, "w1_plane", 50.5)
         w3_plane = held([P, H // 4], I32, "w3_plane")
         tab2_plane = held([P, T // 4], I32, "tab2_plane")
-        nc.vector.memset(tab_plane[:], 0)
+        for cols in (slice(0, T // 8 + 1), slice(T // 8 + 1, T // 4)):
+            nc.vector.memset(tab_plane[:, cols], 0)
         nc.gpsimd.memset(w1_plane[:], 0)
 
         idx1 = load_list(offs, "idx1")
@@ -328,74 +329,66 @@ def tile_list_grain_boundary_segregation_kernel(
         nc.gpsimd.tensor_tensor(final[:], response[last][:], weight[last][:], MULT)
         nc.vector.tensor_copy(pages[last][:].indirect(idx3[:]), final[:])
 
-        chunks = [slice(lo, lo + CHUNK) for lo in range(0, T2, CHUNK)]
-        per_bank = BANK // CHUNK
-        accs = {}
+        half = T2 // 2
+        banks = [(slice(CHUNK * c, CHUNK * (c + 1)), range(2 * pair, 2 * pair + 2)) for c in range(2) for pair in range(2)]
+        banks = banks + [(slice(half, T2), range(n, n + 1)) for n in range(N // P)]
+        accs = [bank(index, "out_acc%d" % index) for index in range(len(banks))]
 
-        def reader_pass(b, c, pair, w_codes, w_sc, z_codes, z_sc):
-            if b == 0:
-                accs[c, pair] = bank(len(accs), "out_acc%d%d" % (c, pair))
-            for h in range(per_bank):
-                n_cols = slice(P * h, P * (h + 1))
+        def reader_pass(b, index, weights, z_codes, z_sc):
+            cols, tiles = banks[index]
+            width = cols.stop - cols.start
+            for h, n in enumerate(tiles):
+                w_codes, w_sc = weights(n)
                 nc.tensor.matmul_mx(
-                    out=accs[c, pair][:, CHUNK * h : CHUNK * (h + 1)], lhsT=w_codes[:, n_cols].bitcast(FP8X4),
-                    lhsT_scale=w_sc[:, n_cols], rhs=z_codes.bitcast(FP8X4), rhs_scale=z_sc,
-                    start=b == 0 and h == 0, stop=b == 1 and h == per_bank - 1,
+                    out=accs[index][:, width * h : width * (h + 1)], lhsT=w_codes.bitcast(FP8X4), lhsT_scale=w_sc,
+                    rhs=z_codes.bitcast(FP8X4), rhs_scale=z_sc,
+                    start=b == 0 and h == 0, stop=b == 1 and n == tiles[-1],
                 )
 
-        for c, cols in enumerate(chunks):
-            for pair in range(2):
-                own = slice(N // 2 * pair, N // 2 * (pair + 1))
-                reader_pass(0, c, pair, w4_q[0][0][:, own], w4_q[0][1][:, own], z0_q[0][:, cols], z0_q[1][:, cols])
+        def early_weights(n):
+            return [part[:, P * n : P * (n + 1)] for part in w4_q[0]]
+
+        def late_weights(n):
+            return [part[:, P * (n % 2) : P * (n % 2 + 1)] for part in w4_late[n // 2]]
+
+        for index, (cols, tiles) in enumerate(banks):
+            reader_pass(0, index, early_weights, z0_q[0][:, cols], z0_q[1][:, cols])
         out_rows = out.rearrange("(n p) t -> p n t", p=P)
         last_bias = bias_sb[1][PACK - 1]
 
-        def last_z(c):
-            cols = chunks[c]
-            if c == 1:
-                nc.scalar.activation(z[1][:, cols, PACK - 1], pages[last][:, cols], ACT.Identity, bias=last_bias)
-            else:
-                nc.vector.tensor_scalar_add(z[1][:, cols, PACK - 1], pages[last][:, cols], last_bias)
+        def bias_on_vector(cols):
+            nc.vector.tensor_scalar_add(z[1][:, cols, PACK - 1], pages[last][:, cols], last_bias)
+
+        def bias_on_scalar(cols):
+            nc.scalar.activation(z[1][:, cols, PACK - 1], pages[last][:, cols], ACT.Identity, bias=last_bias)
 
         def quantize_w4_late(pair):
             own = slice(N // 2 * pair, N // 2 * (pair + 1))
             grouped = w4_grouped[1][:, own, :].rearrange("p c j -> p (c j)")
             return quantize(grouped, N // 2, "w4_1%d" % pair, kib=60 + pair)
 
-        def quantize_z1(c):
-            return quantize(z[1][:, chunks[c], :].rearrange("p c j -> p (c j)"), CHUNK, "z1%d" % c)
+        def quantize_z1(cols):
+            grouped = z[1][:, cols, :].rearrange("p c j -> p (c j)")
+            return quantize(grouped, cols.stop - cols.start, "z1_%d" % cols.start)
 
-        last_z(0)
-        last_z(1)
+        bias_on_vector(slice(0, CHUNK // 2))
+        bias_on_scalar(slice(CHUNK // 2, CHUNK))
+        bias_on_scalar(slice(CHUNK, half))
         w4_late = [quantize_w4_late(0)]
-        z1_q = [quantize_z1(0)]
+        z1_q = {0: quantize_z1(slice(0, CHUNK))}
         w4_late.append(quantize_w4_late(1))
-        z1_q.append(quantize_z1(1))
-        for c in range(2, len(chunks)):
-            last_z(c)
-        for c in range(2, len(chunks)):
-            z1_q.append(quantize_z1(c))
-        def copy_out(engine_copy, target, c, pair, tiles):
-            acc = accs[c, pair][:].rearrange("p (h t) -> p h t", t=CHUNK)
-            engine_copy(target, acc[:, tiles, :])
-
-        results = [held([P, N // P, CHUNK], F32, "result%d" % c, tag="page0%d" % c) for c in range(len(chunks))]
-
-        def store(c, tiles):
-            nc.sync.dma_start(out_rows[:, tiles, chunks[c]], results[c][:, tiles, :])
-
-        for c in range(len(chunks)):
-            for pair in range(2):
-                reader_pass(1, c, pair, w4_late[pair][0][:], w4_late[pair][1][:], z1_q[c][0][:], z1_q[c][1][:])
-                tiles = slice(per_bank * pair, per_bank * (pair + 1))
-                if (c, pair) == (0, 0):
-                    for h in range(per_bank):
-                        copy_out(nc.scalar.copy, results[c][:, h : h + 1, :], c, pair, slice(h, h + 1))
-                        store(c, slice(h, h + 1))
-                    continue
-                on_vector = c >= 2 and pair == 1
-                copy_out(nc.vector.tensor_copy if on_vector else nc.scalar.copy, results[c][:, tiles, :], c, pair, slice(0, per_bank))
-                if c + 1 < len(chunks):
-                    store(c, tiles)
-                elif pair == 1:
-                    store(c, slice(0, N // P))
+        bias_on_vector(slice(half, T2))
+        z1_q[CHUNK] = quantize_z1(slice(CHUNK, half))
+        z1_q[half] = quantize_z1(slice(half, T2))
+        for index, (cols, tiles) in enumerate(banks):
+            reader_pass(1, index, late_weights, z1_q[cols.start][0][:], z1_q[cols.start][1][:])
+            width = cols.stop - cols.start
+            result = held([P, len(tiles), width], F32, "result%d" % index, tag="weight%d%d" % bulk_order[index])
+            acc = accs[index][:].rearrange("p (h t) -> p h t", t=width)
+            pieces = [slice(h, h + 1) for h in range(len(tiles))] if index == 0 else [slice(0, len(tiles))]
+            for own in pieces:
+                if index in (4, 6):
+                    nc.vector.tensor_copy(result[:, own, :], acc[:, own, :])
+                else:
+                    nc.scalar.copy(result[:, own, :], acc[:, own, :])
+                nc.sync.dma_start(out_rows[:, tiles[0] + own.start : tiles[0] + own.stop, cols], result[:, own, :])

@@ -69,6 +69,7 @@ def tile_list_grain_boundary_segregation_kernel(
                 nc.sync.dma_start(tile[QUAD * q : QUAD * (q + 1)], rows)
             return [tile[:]]
 
+
         def load_site_slots(source, slots, name):
             tile = held([P, len(slots), S], F32, name)
             rows = source.rearrange("(m t e) j -> e m t j", t=PACK, e=2)
@@ -105,8 +106,8 @@ def tile_list_grain_boundary_segregation_kernel(
                 nc.sync.dma_start(tile[e:P:2], rows[e])
             return tile
 
-        def reorder_pairs(dst, src, line):
-            nc.vector.tensor_copy(
+        def reorder_pairs(copy, dst, src, line):
+            copy(
                 dst.rearrange("p (b t m i) -> p b m t i", t=PACK, m=P // 2 // line, i=line),
                 src.rearrange("p (b m i t) -> p b m t i", t=PACK, m=P // 2 // line, i=line),
             )
@@ -129,11 +130,13 @@ def tile_list_grain_boundary_segregation_kernel(
         nc.gpsimd.memset(w1_plane[:], 0)
 
         idx1 = load_list(offs, "idx1")
+        idx3 = load_list(offs3, "idx3")
+        gain_sb = load_row_values(gain, "gain_sb")
         tab_sb = load_words(tab_words[0], held([P, T], I32, "tab_sb"))
-        w1_sb = held([P, H // 2], I32, "w1_sb")
-        nc.sync.dma_start(w1_sb[:], w1_words[0].bitcast(I32))
         for q in QUADRANTS:
             load_scale_rows(nc.sync, tab_plane, tab_scales, q)
+        w1_sb = held([P, H // 2], I32, "w1_sb")
+        nc.sync.dma_start(w1_sb[:], w1_words[0].bitcast(I32))
         for q in QUADRANTS[:2]:
             load_scale_rows(nc.sync, w1_plane, w1_scales, q)
         for q in QUADRANTS[2:]:
@@ -141,20 +144,19 @@ def tile_list_grain_boundary_segregation_kernel(
         for plane in (tab2_plane, w3_plane):
             nc.gpsimd.memset(plane[:], 0)
         wg1_sb = load_site_slot(wg1, 0, "wg1_0")
-        gain_sb = load_row_values(gain, "gain_sb")
-        idx3 = load_list(offs3, "idx3")
         wg1_sb = wg1_sb + load_site_slot(wg1, 1, "wg1_1")
-        wg1_sb = wg1_sb + load_site_slots(wg1, range(2, PACK), "wg1_rest")
-        w3_sb = [load_w3(b) for b in range(2)]
-        w2_raw = [load_w2(b) for b in range(2)]
+        w2_raw = [load_w2(0)]
+        wg1_sb = wg1_sb + load_site_slot(wg1, 2, "wg1_2")
+        w3_sb = [load_w3(0)]
+        wg1_sb = wg1_sb + load_site_slot(wg1, 3, "wg1_3")
+        w3_sb.append(load_w3(1))
+        w2_raw.append(load_w2(1))
         for q in QUADRANTS:
             load_scale_rows(nc.sync, w3_plane, w3_scales, q)
+        tab2_sb = [load_words(tab2_words[0], held([P, T], I32, "tab2_sb0"))]
         for q in QUADRANTS:
             load_scale_rows(nc.sync, tab2_plane, tab2_scales, q)
-        tab2_sb = [
-            load_words(tab2_words[0], held([P, T], I32, "tab2_sb0")),
-            load_words(tab2_words[1], placed([P, T], I32, "tab2_sb1", 36)),
-        ]
+        tab2_sb.append(load_words(tab2_words[1], placed([P, T], I32, "tab2_sb1", 36)))
         idx2 = load_list(offs2, "idx2")
         w4_raw = [load_w4(0, placed([P, PACK, N], F32, "w4_raw0", 28))]
         wg2_sb = load_site_slot(wg2, 0, "wg2_0") + load_site_slots(wg2, range(1, PACK), "wg2_rest")
@@ -162,112 +164,111 @@ def tile_list_grain_boundary_segregation_kernel(
         bias_sb = load_row_values(bias, "bias_sb")
         w4_raw.append(load_w4(1, held([P, PACK, N], F32, "w4_raw1")))
 
-        w1_ord = held([P, 2 * H], U8, "w1_ord")
-        w1_sc = held([P, H], U8, "w1_sc")
         halves = [slice(0, S // 2), slice(S // 2, S)]
         whole = slice(0, S)
+        w1_first = placed([P, 2, P // 2], U32, "w1_first", 70)
+        w1_rest = placed([P, 2, PACK - 1, P // 2], U32, "w1_rest", 70)
+        w1_pairs = w1_sb[:].bitcast(U32).rearrange("p (b m t) -> p b m t", b=2, t=PACK)
+        w1_sc = held([P, H], U8, "w1_sc")
 
-        def order_w1(b):
-            cols = slice(256 * b, 256 * (b + 1))
-            reorder_pairs(w1_ord[:].bitcast(U32)[:, cols], w1_sb[:].bitcast(U32)[:, cols], 4)
+        def w1_operand(b, t):
+            i = PACK * b + t
+            words = w1_first[:, b, :] if t == 0 else w1_rest[:, b, t - 1, :]
+            return words.bitcast(U8).bitcast(FP4X4), w1_sc[:, P * i : P * (i + 1)]
 
         def gather_v(part, words, scales):
             nc.vector.tensor_copy(words[:], tab_sb[:].bitcast(U32).indirect(entries(idx1, part)))
             nc.vector.tensor_copy(scales[:], tab_plane[:].bitcast(U8).indirect(entries(idx1, part)))
             return words, scales
 
-        v_q = [gather_v(halves[0], held([P, S // 2], U32, "v_words0"), held([P, S // 2], U8, "v_scales0"))]
-        order_w1(0)
-        reorder_pairs(w1_sc[:].bitcast(U16), w1_plane[:].bitcast(U16), 8)
-        order_w1(1)
+        bulk_order = [(b, t) for t in range(PACK) for b in range(2)]
+        cover, last = bulk_order[-2:]
+        pages = {page: held([P, T2], F32, "page%d%d" % page) for page in bulk_order if page != cover}
+
+        v_q = [gather_v(halves[0], placed([P, S // 2], U32, "v_words0", 76), placed([P, S // 2], U8, "v_scales0", 80))]
+        nc.vector.tensor_copy(w1_first[:], w1_pairs[:, :, :, 0])
+        reorder_pairs(nc.vector.tensor_copy, w1_sc[:].bitcast(U16), w1_plane[:].bitcast(U16), 8)
         v_q.append(gather_v(halves[1], placed([P, S // 2], U32, "v_words1", 50), placed([P, S // 2], U8, "v_scales1", 51)))
 
-        bulk_order = [(0, 0), (1, 0), (0, 1), (1, 1), (0, 2), (0, 3), (1, 2), (1, 3)]
-        cover, last = bulk_order[-2:]
-        response_kib = {2: 64, 3: 61, 5: 55.5}
-        pages, response, weight = {}, {}, {}
-
-        def respond(step, page, part, index):
-            b, t = page
-            i = PACK * b + t
-            acc = bank(index, "h1_acc%d_%d" % (i, part.start))
+        def multiply(page, part, index):
+            codes, code_scales = w1_operand(*page)
+            acc = bank(index, "h1_acc%d%d_%d" % (*page, part.start))
             for half, (words, scales) in zip(halves, v_q):
                 if part.start <= half.start and half.stop <= part.stop:
                     nc.tensor.matmul_mx(
-                        out=acc[:, half], lhsT=w1_ord[:, 2 * P * i : 2 * P * (i + 1)].bitcast(FP4X4),
-                        lhsT_scale=w1_sc[:, P * i : P * (i + 1)],
+                        out=acc[:, half], lhsT=codes, lhsT_scale=code_scales,
                         rhs=words[:].bitcast(FP8X4), rhs_scale=scales[:], start=True, stop=True,
                     )
-            nc.scalar.activation(response[page][:, part], acc[:, part], ACT.Tanh)
+            return acc
 
-        def weigh(page, part):
+        def apply_gain(weight, site, row_gain):
+            nc.gpsimd.tensor_scalar(weight, site, row_gain, 0.0, MULT, ADD)
+
+        def weigh(weight, response):
+            nc.gpsimd.tensor_tensor(weight, response, weight, MULT)
+
+        def place_bulk(page, part, values):
+            nc.vector.tensor_copy(pages[page][:].indirect(entries(idx3, part)), values)
+
+        for n, half in enumerate(halves):
+            for b in range(2):
+                acc = multiply((b, 0), half, (b, 6 + b)[n])
+                response = held([P, S // 2], F32, "response0%d%d" % (b, n), tag="slot2" if n and b else None)
+                values = held([P, S // 2], F32, "values0%d%d" % (b, n), tag="slot%d" % b if n else None)
+                nc.scalar.activation(response[:], acc[:, half], ACT.Tanh)
+                if n == 0 and b == 0:
+                    nc.vector.scalar_tensor_tensor(values[:], response[:], gain_sb[0][0], wg1_sb[0][:, half], MULT, MULT)
+                else:
+                    apply_gain(values[:], wg1_sb[0][:, half], gain_sb[b][0])
+                    weigh(values[:], response[:])
+                place_bulk((b, 0), half, values[:])
+        nc.scalar.copy(w1_rest[:].rearrange("p b t m -> p b m t"), w1_pairs[:, :, :, 1:])
+
+        for step, page in enumerate(bulk_order[2:], start=2):
             b, t = page
-            if t == 0:
-                nc.gpsimd.tensor_scalar(weight[page][:, part], wg1_sb[t][:, part], gain_sb[b][t], 0.0, MULT, ADD)
+            weight = held([P, S], F32, "weight%d" % step, tag="slot%d" % step)
+            apply_gain(weight[:], wg1_sb[t], gain_sb[b][t])
+            acc = multiply(page, whole, step)
+            response = held([P, S], F32, "response%d" % step, tag="slot%d" % (step + 1))
+            nc.scalar.activation(response[:], acc[:], ACT.Tanh)
+            if page == last:
+                last_weight, last_response = weight, response
             else:
-                nc.scalar.activation(weight[page][:, part], wg1_sb[t][:, part], ACT.Copy, scale=gain_sb[b][t])
-            if page != last:
-                nc.gpsimd.tensor_tensor(weight[page][:, part], response[page][:, part], weight[page][:, part], MULT)
+                weigh(weight[:], response[:])
+            if page == cover:
+                cover_values = weight
+            elif page != last:
+                place_bulk(page, whole, weight[:])
 
-        def place_bulk(page, part):
-            nc.vector.tensor_copy(pages[page][:].indirect(entries(idx3, part)), weight[page][:, part])
-
-        for step, page in enumerate(bulk_order):
-            name = "%d%d" % page
-            if step in response_kib:
-                response[page] = placed([P, S], F32, "response" + name, response_kib[step])
-            else:
-                response[page] = held([P, S], F32, "response" + name)
-            if page != cover:
-                pages[page] = held([P, T2], F32, "page" + name)
-            weight[page] = held([P, S], F32, "weight" + name)
-            if step == 0:
-                respond(step, page, halves[0], 0)
-                nc.vector.scalar_tensor_tensor(
-                    weight[page][:, halves[0]], response[page][:, halves[0]], gain_sb[0][0], wg1_sb[0][:, halves[0]],
-                    MULT, MULT,
-                )
-                place_bulk(page, halves[0])
-                respond(step, page, halves[1], 7)
-                weigh(page, halves[1])
-                place_bulk(page, halves[1])
-            else:
-                respond(step, page, whole, step)
-                weigh(page, whole)
-                if page not in (cover, last):
-                    place_bulk(page, whole)
-
-        w2_grouped = []
+        w2_grouped, w3_ord = [], []
         for b in range(2):
-            grouped = held([P, 2, PACK * 512], BF16, "w2_grouped%d" % b)
+            if b == 0:
+                grouped = placed([P, 2, PACK * 512], BF16, "w2_grouped0", 68)
+            else:
+                grouped = held([P, 2, PACK * 512], BF16, "w2_grouped1")
+            w3_ord.append(placed([P, 2, 512], U32, "w3_ord%d" % b, 76 + 4 * b))
+            if b == 1:
+                for n in range(2):
+                    nc.scalar.copy(
+                        w3_ord[n][:].rearrange("p a (t m e) -> p a t m e", t=PACK, e=2),
+                        w3_sb[n][:].bitcast(U32).rearrange("p a (m t e) -> p a t m e", t=PACK, e=2),
+                    )
             for a in range(2):
                 nc.scalar.copy(
                     grouped[:, a, :].rearrange("p (t m e j) -> p m t e j", t=PACK, e=2, j=PACK),
                     w2_raw[b][a][:].rearrange("p j (m t e) -> p m t e j", t=PACK, e=2),
                 )
             w2_grouped.append(grouped)
-
-        w3_ord = {}
-
-        def order_w3(engine, b, a, kib):
-            w3_ord[b, a] = placed([P, 512], U32, "w3_ord%d%d" % (b, a), kib)
-            engine.tensor_copy(
-                w3_ord[b, a][:].rearrange("p (t m e) -> p t m e", t=PACK, e=2),
-                w3_sb[b][:, a, :].bitcast(U32).rearrange("p (m t e) -> p t m e", t=PACK, e=2),
-            )
+        w3_sc = held([P, H], U8, "w3_sc")
+        reorder_pairs(nc.scalar.copy, w3_sc[:].bitcast(U16), w3_plane[:].bitcast(U16), 8)
 
         def quantize_w2(b, tag=None, kib=None):
             return quantize(w2_grouped[b][:].rearrange("p a c -> p (a c)"), 2 * 512, "w2_%d" % b, tag=tag, kib=kib)
 
-        for n, (b, a) in enumerate(((0, 0), (0, 1), (1, 0))):
-            order_w3(nc.gpsimd, b, a, 60 + 2 * n)
-        w2_q = [quantize_w2(0, kib=52)]
-        w3_sc = placed([P, H], U8, "w3_sc", 56)
-        reorder_pairs(w3_sc[:].bitcast(U16), w3_plane[:].bitcast(U16), 8)
-        order_w3(nc.vector, 1, 1, 57)
-        v2_scales = held([P, S], U8, "v2_scales", tag="response%d%d" % bulk_order[4])
+        w2_q = [quantize_w2(0, tag="wg1_3")]
+        v2_scales = held([P, S], U8, "v2_scales", tag="slot4")
         nc.vector.tensor_copy(v2_scales[:], tab2_plane[:].bitcast(U8).indirect(idx2[:]))
-        v2_words = held([P, 2 * S], U32, "v2_words", tag="w2_grouped0")
+        v2_words = placed([P, 2 * S], U32, "v2_words", 68)
         for a in range(2):
             nc.vector.tensor_copy(v2_words[:, S * a : S * (a + 1)], tab2_sb[a][:].bitcast(U32).indirect(idx2[:]))
         w4_grouped = [held([P, N, PACK], BF16, "w4_grouped0")]
@@ -277,7 +278,7 @@ def tile_list_grain_boundary_segregation_kernel(
         w4_q = [quantize(w4_grouped[0][:].rearrange("p c j -> p (c j)"), N, "w4_0")]
         w2_q.append(quantize_w2(1, kib=32))
         pages[cover] = held([P, T2], F32, "page_cover", tag="w4_grouped0")
-        place_bulk(cover, whole)
+        place_bulk(cover, whole, cover_values[:])
 
         sums = placed([P, 4, PACK, S], F32, "sums", 0)
         first = [sums[:, b] for b in range(2)]
@@ -290,7 +291,7 @@ def tile_list_grain_boundary_segregation_kernel(
             for a in range(2):
                 cols = slice(512 * a + P * t, 512 * a + P * (t + 1))
                 own = slice(512 * b + P * t, 512 * b + P * (t + 1))
-                operands = [(w2_q[b][0][:, cols], w2_q[b][1][:, cols]), (w3_ord[b, a][:, P * t : P * (t + 1)], w3_sc[4 * a :, own])]
+                operands = [(w2_q[b][0][:, cols], w2_q[b][1][:, cols]), (w3_ord[b][:, a, P * t : P * (t + 1)], w3_sc[4 * a :, own])]
                 for acc, (codes, scales) in zip(accs, operands):
                     nc.tensor.matmul_mx(
                         out=acc[:], lhsT=codes.bitcast(FP8X4), lhsT_scale=scales,
@@ -326,7 +327,7 @@ def tile_list_grain_boundary_segregation_kernel(
         nc.gpsimd.tensor_scalar(w4_grouped[1][:], w4_raw[1][:].rearrange("p j c -> p c j"), 1.0, 0.0, MULT, ADD)
         z0_q = quantize(z[0][:].rearrange("p c j -> p (c j)"), T2, "z0", kib=46)
         final = placed([P, S], F32, "final", 60)
-        nc.gpsimd.tensor_tensor(final[:], response[last][:], weight[last][:], MULT)
+        nc.gpsimd.tensor_tensor(final[:], last_response[:], last_weight[:], MULT)
         nc.vector.tensor_copy(pages[last][:].indirect(idx3[:]), final[:])
 
         half = T2 // 2
@@ -383,7 +384,7 @@ def tile_list_grain_boundary_segregation_kernel(
         for index, (cols, tiles) in enumerate(banks):
             reader_pass(1, index, late_weights, z1_q[cols.start][0][:], z1_q[cols.start][1][:])
             width = cols.stop - cols.start
-            result = held([P, len(tiles), width], F32, "result%d" % index, tag="weight%d%d" % bulk_order[index])
+            result = held([P, len(tiles), width], F32, "result%d" % index, tag="slot%d" % (index + 1))
             acc = accs[index][:].rearrange("p (h t) -> p h t", t=width)
             pieces = [slice(h, h + 1) for h in range(len(tiles))] if index == 0 else [slice(0, len(tiles))]
             for own in pieces:

@@ -85,14 +85,10 @@ def tile_list_grain_boundary_segregation_kernel(
                 nc.sync.dma_start(tile[e:P:2, :, 0:7], runs[:, :, e : e + 7])
             return [[tile[:, b, 2 * t : 2 * t + 1] for t in range(PACK)] for b in range(2)]
 
-        def load_w2(b):
-            tiles = []
-            for a in range(2):
-                tile = placed([P, PACK, 512], F32, "w2_raw%d%d" % (a, b), 8 * (3 - 2 * b - a))
-                rows = w2[K_PASS * a : K_PASS * (a + 1), 512 * b : 512 * (b + 1)]
-                nc.sync.dma_start(tile[:], rows.rearrange("(p j) c -> p j c", j=PACK))
-                tiles.append(tile)
-            return tiles
+        def load_w2(a):
+            tile = placed([P, PACK, H], F32, "w2_raw%d" % a, 16 * (1 - a))
+            nc.sync.dma_start(tile[:], w2[K_PASS * a : K_PASS * (a + 1), :].rearrange("(p j) c -> p j c", j=PACK))
+            return tile
 
         def load_w3(b):
             tile = held([P, 2, 512], I32, "w3_sb%d" % b)
@@ -149,7 +145,6 @@ def tile_list_grain_boundary_segregation_kernel(
         wg1_sb = wg1_sb + load_site_slot(wg1, 2, "wg1_2")
         w3_sb = [load_w3(0)]
         wg1_sb = wg1_sb + load_site_slot(wg1, 3, "wg1_3")
-        w3_sb.append(load_w3(1))
         w2_raw.append(load_w2(1))
         for q in QUADRANTS:
             load_scale_rows(nc.sync, w3_plane, w3_scales, q)
@@ -159,8 +154,9 @@ def tile_list_grain_boundary_segregation_kernel(
         tab2_sb.append(load_words(tab2_words[1], placed([P, T], I32, "tab2_sb1", 36)))
         idx2 = load_list(offs2, "idx2")
         w4_raw = [load_w4(0, placed([P, PACK, N], F32, "w4_raw0", 28))]
-        wg2_sb = load_site_slot(wg2, 0, "wg2_0") + load_site_slots(wg2, range(1, PACK), "wg2_rest")
+        w3_sb.append(load_w3(1))
         idx4 = load_list(offs4, "idx4")
+        wg2_sb = load_site_slot(wg2, 0, "wg2_0") + load_site_slots(wg2, range(1, PACK), "wg2_rest")
         bias_sb = load_row_values(bias, "bias_sb")
         w4_raw.append(load_w4(1, held([P, PACK, N], F32, "w4_raw1")))
 
@@ -240,25 +236,23 @@ def tile_list_grain_boundary_segregation_kernel(
             elif page != last:
                 place_bulk(page, whole, weight[:])
 
-        w2_grouped, w3_ord = [], []
-        for b in range(2):
-            if b == 0:
-                grouped = placed([P, 2, PACK * 512], BF16, "w2_grouped0", 68)
-            else:
-                grouped = held([P, 2, PACK * 512], BF16, "w2_grouped1")
-            w3_ord.append(placed([P, 2, 512], U32, "w3_ord%d" % b, 76 + 4 * b))
-            if b == 1:
-                for n in range(2):
-                    nc.scalar.copy(
-                        w3_ord[n][:].rearrange("p a (t m e) -> p a t m e", t=PACK, e=2),
-                        w3_sb[n][:].bitcast(U32).rearrange("p a (m t e) -> p a t m e", t=PACK, e=2),
-                    )
-            for a in range(2):
+        w2_grouped = [placed([P, 2, PACK * 512], BF16, "w2_grouped%d" % b, 68 + 12 * b) for b in range(2)]
+        w3_ord = [placed([P, 2, 512], U32, "w3_ord0", 76), held([P, 2, 512], U32, "w3_ord1")]
+
+        def order_w3(b):
+            nc.scalar.copy(
+                w3_ord[b][:].rearrange("p a (t m e) -> p a t m e", t=PACK, e=2),
+                w3_sb[b][:].bitcast(U32).rearrange("p a (m t e) -> p a t m e", t=PACK, e=2),
+            )
+
+        for a in range(2):
+            for b in range(2):
                 nc.scalar.copy(
-                    grouped[:, a, :].rearrange("p (t m e j) -> p m t e j", t=PACK, e=2, j=PACK),
-                    w2_raw[b][a][:].rearrange("p j (m t e) -> p m t e j", t=PACK, e=2),
+                    w2_grouped[b][:, a, :].rearrange("p (t m e j) -> p m t e j", t=PACK, e=2, j=PACK),
+                    w2_raw[a][:, :, 512 * b : 512 * (b + 1)].rearrange("p j (m t e) -> p m t e j", t=PACK, e=2),
                 )
-            w2_grouped.append(grouped)
+            if a == 0:
+                order_w3(0)
         w3_sc = held([P, H], U8, "w3_sc")
         reorder_pairs(nc.scalar.copy, w3_sc[:].bitcast(U16), w3_plane[:].bitcast(U16), 8)
 
@@ -275,6 +269,7 @@ def tile_list_grain_boundary_segregation_kernel(
         nc.scalar.copy(
             w4_grouped[0][:].rearrange("p (c i) j -> p c j i", i=4), w4_raw[0][:].rearrange("p j (c i) -> p c j i", i=4),
         )
+        order_w3(1)
         w4_q = [quantize(w4_grouped[0][:].rearrange("p c j -> p (c j)"), N, "w4_0")]
         w2_q.append(quantize_w2(1, kib=32))
         pages[cover] = held([P, T2], F32, "page_cover", tag="w4_grouped0")
@@ -308,7 +303,7 @@ def tile_list_grain_boundary_segregation_kernel(
         for step in range(ahead):
             boundary_product(step)
         pairs = placed([P, 2, T2, 2], BF16, "pairs", 60)
-        z = [held([P, T2, PACK], BF16, "z%d" % b, tag=("tab_sb", "w2_grouped1")[b]) for b in range(2)]
+        z = [held([P, T2, PACK], BF16, "z0", tag="tab_sb"), placed([P, T2, PACK], BF16, "z1", 80)]
         for step, page in enumerate(boundary_order):
             b, t = page
             nc.vector.tensor_copy(pages[page][:].indirect(idx4[:]), second[b][:, t, :])

@@ -62,9 +62,9 @@ def tile_list_grain_boundary_segregation_kernel(
             rows = 4 * source.shape[0]
             queue.dma_start(plane[QUAD * q : QUAD * q + rows, :], source[:, 4 * q : 4 * q + 4, :].bitcast(I32))
 
-        def load_site_slot(source, t, name):
-            tile = held([P, S], F32, name)
-            rows = source.rearrange("(m t e) j -> t m e j", t=PACK, e=2)[t]
+        def load_site_slot(source, t, name, part=slice(0, S)):
+            tile = held([P, part.stop - part.start], F32, name)
+            rows = source.rearrange("(m t e) j -> t m e j", t=PACK, e=2)[t][:, :, part]
             for q in QUADRANTS:
                 nc.sync.dma_start(tile[QUAD * q : QUAD * (q + 1)], rows)
             return [tile[:]]
@@ -126,7 +126,6 @@ def tile_list_grain_boundary_segregation_kernel(
         nc.gpsimd.memset(w1_plane[:], 0)
 
         idx1 = load_list(offs, "idx1")
-        idx3 = load_list(offs3, "idx3")
         gain_sb = load_row_values(gain, "gain_sb")
         tab_sb = load_words(tab_words[0], held([P, T], I32, "tab_sb"))
         for q in QUADRANTS:
@@ -139,12 +138,14 @@ def tile_list_grain_boundary_segregation_kernel(
             load_scale_rows(nc.gpsimd, w1_plane, w1_scales, q)
         for plane in (tab2_plane, w3_plane):
             nc.gpsimd.memset(plane[:], 0)
-        wg1_sb = load_site_slot(wg1, 0, "wg1_0")
-        wg1_sb = wg1_sb + load_site_slot(wg1, 1, "wg1_1")
+        halves = [slice(0, S // 2), slice(S // 2, S)]
+        wg1_first = load_site_slot(wg1, 0, "wg1_0a", halves[0])
+        idx3 = load_list(offs3, "idx3")
+        wg1_first = wg1_first + load_site_slot(wg1, 0, "wg1_0b", halves[1])
+        w3_sb = [load_w3(0)]
+        wg1_sb = [None] + load_site_slot(wg1, 1, "wg1_1")
         w2_raw = [load_w2(0)]
         wg1_sb = wg1_sb + load_site_slot(wg1, 2, "wg1_2")
-        w3_sb = [load_w3(0)]
-        wg1_sb = wg1_sb + load_site_slot(wg1, 3, "wg1_3")
         w2_raw.append(load_w2(1))
         for q in QUADRANTS:
             load_scale_rows(nc.sync, w3_plane, w3_scales, q)
@@ -154,13 +155,13 @@ def tile_list_grain_boundary_segregation_kernel(
         tab2_sb.append(load_words(tab2_words[1], placed([P, T], I32, "tab2_sb1", 36)))
         idx2 = load_list(offs2, "idx2")
         w4_raw = [load_w4(0, placed([P, PACK, N], F32, "w4_raw0", 28))]
+        wg1_sb = wg1_sb + load_site_slot(wg1, 3, "wg1_3")
         w3_sb.append(load_w3(1))
         idx4 = load_list(offs4, "idx4")
         wg2_sb = load_site_slot(wg2, 0, "wg2_0") + load_site_slots(wg2, range(1, PACK), "wg2_rest")
         bias_sb = load_row_values(bias, "bias_sb")
         w4_raw.append(load_w4(1, held([P, PACK, N], F32, "w4_raw1")))
 
-        halves = [slice(0, S // 2), slice(S // 2, S)]
         whole = slice(0, S)
         w1_first = placed([P, 2, P // 2], U32, "w1_first", 70)
         w1_rest = placed([P, 2, PACK - 1, P // 2], U32, "w1_rest", 70)
@@ -209,31 +210,29 @@ def tile_list_grain_boundary_segregation_kernel(
         for n, half in enumerate(halves):
             for b in range(2):
                 acc = multiply((b, 0), half, (b, 6 + b)[n])
-                response = held([P, S // 2], F32, "response0%d%d" % (b, n), tag="slot2" if n and b else None)
-                values = held([P, S // 2], F32, "values0%d%d" % (b, n), tag="slot%d" % b if n else None)
+                response = held([P, S // 2], F32, "response0%d%d" % (b, n), tag=(None, "slot0", "slot1", "slot2")[2 * n + b])
+                values = held([P, S // 2], F32, "values0%d%d" % (b, n), tag=("slot0", "slot1")[b] if n else None)
                 nc.scalar.activation(response[:], acc[:, half], ACT.Tanh)
                 if n == 0 and b == 0:
-                    nc.vector.scalar_tensor_tensor(values[:], response[:], gain_sb[0][0], wg1_sb[0][:, half], MULT, MULT)
+                    nc.vector.scalar_tensor_tensor(values[:], response[:], gain_sb[0][0], wg1_first[n], MULT, MULT)
                 else:
-                    apply_gain(values[:], wg1_sb[0][:, half], gain_sb[b][0])
+                    apply_gain(values[:], wg1_first[n], gain_sb[b][0])
                     weigh(values[:], response[:])
                 place_bulk((b, 0), half, values[:])
         nc.scalar.copy(w1_rest[:].rearrange("p b t m -> p b m t"), w1_pairs[:, :, :, 1:])
 
+        responses = {}
         for step, page in enumerate(bulk_order[2:], start=2):
             b, t = page
-            weight = held([P, S], F32, "weight%d" % step, tag="slot%d" % step)
-            apply_gain(weight[:], wg1_sb[t], gain_sb[b][t])
+            if page not in (cover, last):
+                weight = held([P, S], F32, "weight%d" % step, tag="slot%d" % step)
+                apply_gain(weight[:], wg1_sb[t], gain_sb[b][t])
             acc = multiply(page, whole, step)
-            response = held([P, S], F32, "response%d" % step, tag="slot%d" % (step + 1))
-            nc.scalar.activation(response[:], acc[:], ACT.Tanh)
-            if page == last:
-                last_weight, last_response = weight, response
-            else:
-                weigh(weight[:], response[:])
-            if page == cover:
-                cover_values = weight
-            elif page != last:
+            tag = "early" if step == 5 else "slot%d" % (step + 1)
+            responses[page] = held([P, S], F32, "response%d" % step, tag=tag)
+            nc.scalar.activation(responses[page][:], acc[:], ACT.Tanh)
+            if page not in (cover, last):
+                weigh(weight[:], responses[page][:])
                 place_bulk(page, whole, weight[:])
 
         w2_grouped = [placed([P, 2, PACK * 512], BF16, "w2_grouped%d" % b, 68 + 12 * b) for b in range(2)]
@@ -256,10 +255,14 @@ def tile_list_grain_boundary_segregation_kernel(
         w3_sc = held([P, H], U8, "w3_sc")
         reorder_pairs(nc.scalar.copy, w3_sc[:].bitcast(U16), w3_plane[:].bitcast(U16), 8)
 
-        def quantize_w2(b, tag=None, kib=None):
-            return quantize(w2_grouped[b][:].rearrange("p a c -> p (a c)"), 2 * 512, "w2_%d" % b, tag=tag, kib=kib)
 
-        w2_q = [quantize_w2(0, tag="wg1_3")]
+        w2_low = quantize(w2_grouped[0][:].rearrange("p a c -> p (a c)"), 2 * 512, "w2_0", tag="early")
+        w2_q = {(0, a): [part[:, 512 * a : 512 * (a + 1)] for part in w2_low] for a in range(2)}
+        cover_values = placed([P, S], F32, "weight_cover", 72)
+        apply_gain(cover_values[:], wg1_sb[cover[1]], gain_sb[cover[0]][cover[1]])
+        weigh(cover_values[:], responses[cover][:])
+        last_weight = held([P, S], F32, "weight_last", tag="slot7")
+        apply_gain(last_weight[:], wg1_sb[last[1]], gain_sb[last[0]][last[1]])
         v2_scales = held([P, S], U8, "v2_scales", tag="slot4")
         nc.vector.tensor_copy(v2_scales[:], tab2_plane[:].bitcast(U8).indirect(idx2[:]))
         v2_words = placed([P, 2 * S], U32, "v2_words", 68)
@@ -270,8 +273,9 @@ def tile_list_grain_boundary_segregation_kernel(
             w4_grouped[0][:].rearrange("p (c i) j -> p c j i", i=4), w4_raw[0][:].rearrange("p j (c i) -> p c j i", i=4),
         )
         order_w3(1)
+        w2_q[1, 0] = quantize(w2_grouped[1][:, 0, :], 512, "w2_10", tag="tab2_sb0")
         w4_q = [quantize(w4_grouped[0][:].rearrange("p c j -> p (c j)"), N, "w4_0")]
-        w2_q.append(quantize_w2(1, kib=32))
+        w2_q[1, 1] = quantize(w2_grouped[1][:, 1, :], 512, "w2_11", kib=32)
         pages[cover] = held([P, T2], F32, "page_cover", tag="w4_grouped0")
         place_bulk(cover, whole, cover_values[:])
 
@@ -284,9 +288,9 @@ def tile_list_grain_boundary_segregation_kernel(
             b, t = boundary_order[step]
             accs = [bank(2 * step + n, "bnd_acc%d%d%d" % (b, t, n)) for n in range(2)]
             for a in range(2):
-                cols = slice(512 * a + P * t, 512 * a + P * (t + 1))
+                cols = slice(P * t, P * (t + 1))
                 own = slice(512 * b + P * t, 512 * b + P * (t + 1))
-                operands = [(w2_q[b][0][:, cols], w2_q[b][1][:, cols]), (w3_ord[b][:, a, P * t : P * (t + 1)], w3_sc[4 * a :, own])]
+                operands = [(w2_q[b, a][0][:, cols], w2_q[b, a][1][:, cols]), (w3_ord[b][:, a, cols], w3_sc[4 * a :, own])]
                 for acc, (codes, scales) in zip(accs, operands):
                     nc.tensor.matmul_mx(
                         out=acc[:], lhsT=codes.bitcast(FP8X4), lhsT_scale=scales,
@@ -322,7 +326,7 @@ def tile_list_grain_boundary_segregation_kernel(
         nc.gpsimd.tensor_scalar(w4_grouped[1][:], w4_raw[1][:].rearrange("p j c -> p c j"), 1.0, 0.0, MULT, ADD)
         z0_q = quantize(z[0][:].rearrange("p c j -> p (c j)"), T2, "z0", kib=46)
         final = placed([P, S], F32, "final", 60)
-        nc.gpsimd.tensor_tensor(final[:], last_response[:], last_weight[:], MULT)
+        nc.gpsimd.tensor_tensor(final[:], responses[last][:], last_weight[:], MULT)
         nc.vector.tensor_copy(pages[last][:].indirect(idx3[:]), final[:])
 
         half = T2 // 2

@@ -23,6 +23,7 @@ K_PASS = P * PACK
 QUAD = 32
 BANK = 512
 CHUNK = 256
+FIRST_ON_VECTOR = 176
 QUADRANTS = (0, 2, 1, 3)
 
 
@@ -282,7 +283,7 @@ def tile_list_grain_boundary_segregation_kernel(
         sums = placed([P, 4, PACK, S], F32, "sums", 0)
         first = [sums[:, b] for b in range(2)]
         second = [sums[:, 2 + b] for b in range(2)]
-        boundary_order = [(0, 0), (0, 1), (0, 2), (0, 3), (1, 2), (1, 0), (1, 1), (1, 3)]
+        boundary_order = [(0, 0), (0, 1), (0, 2), (0, 3), (1, 2), (1, 0), (1, 3), (1, 1)]
 
         def boundary_product(step):
             b, t = boundary_order[step]
@@ -299,7 +300,7 @@ def tile_list_grain_boundary_segregation_kernel(
                     )
             nc.scalar.copy(first[b][:, t, :], accs[0][:])
             nc.scalar.copy(second[b][:, t, :], accs[1][:])
-            weighed = placed([P, S], F32, "weighed%d" % step, 45)
+            weighed = placed([P, S], F32, "weighed%d" % step, 58)
             nc.gpsimd.tensor_tensor(weighed[:], first[b][:, t, :], wg2_sb[t], MULT)
             nc.gpsimd.tensor_tensor(second[b][:, t, :], weighed[:], second[b][:, t, :], MULT)
 
@@ -322,21 +323,31 @@ def tile_list_grain_boundary_segregation_kernel(
             if step + ahead < len(boundary_order):
                 boundary_product(step + ahead)
 
-        w4_grouped.append(placed([P, N, PACK], BF16, "w4_grouped1", 41.5))
+        w4_grouped.append(placed([P, N, PACK], BF16, "w4_grouped1", 54.5))
         nc.gpsimd.tensor_scalar(w4_grouped[1][:], w4_raw[1][:].rearrange("p j c -> p c j"), 1.0, 0.0, MULT, ADD)
-        z0_q = quantize(z[0][:].rearrange("p c j -> p (c j)"), T2, "z0", kib=46)
-        final = placed([P, S], F32, "final", 60)
-        nc.gpsimd.tensor_tensor(final[:], responses[last][:], last_weight[:], MULT)
-        nc.vector.tensor_copy(pages[last][:].indirect(idx3[:]), final[:])
-
         half = T2 // 2
-        banks = [(slice(CHUNK * c, CHUNK * (c + 1)), range(2 * pair, 2 * pair + 2)) for c in range(2) for pair in range(2)]
+
+        def quantize_z0(cols, tag=None, kib=None):
+            return quantize(z[0][:, cols, :].rearrange("p c j -> p (c j)"), half, "z0_%d" % cols.start, tag=tag, kib=kib)
+
+        final = placed([P, S], F32, "final", 59)
+        for part in halves:
+            nc.gpsimd.tensor_tensor(final[:, part], responses[last][:, part], last_weight[:, part], MULT)
+        place_bulk(last, halves[0], final[:, halves[0]])
+        z0_low = quantize_z0(slice(0, half), tag="slot7")
+        place_bulk(last, halves[1], final[:, halves[1]])
+
+        banks = [(slice(0, CHUNK), tiles) for tiles in (range(0, 1), range(1, 2), range(2, 4))]
+        banks = banks + [(slice(CHUNK, half), range(2 * pair, 2 * pair + 2)) for pair in range(2)]
+        early = len(banks)
         banks = banks + [(slice(half, T2), range(n, n + 1)) for n in range(N // P)]
-        accs = [bank(index, "out_acc%d" % index) for index in range(len(banks))]
+        accs = {}
 
         def reader_pass(b, index, weights, z_codes, z_sc):
             cols, tiles = banks[index]
             width = cols.stop - cols.start
+            if b == 0:
+                accs[index] = bank(index, "out_acc%d" % index)
             for h, n in enumerate(tiles):
                 w_codes, w_sc = weights(n)
                 nc.tensor.matmul_mx(
@@ -351,8 +362,8 @@ def tile_list_grain_boundary_segregation_kernel(
         def late_weights(n):
             return [part[:, P * (n % 2) : P * (n % 2 + 1)] for part in w4_late[n // 2]]
 
-        for index, (cols, tiles) in enumerate(banks):
-            reader_pass(0, index, early_weights, z0_q[0][:, cols], z0_q[1][:, cols])
+        for index, (cols, tiles) in enumerate(banks[:early]):
+            reader_pass(0, index, early_weights, z0_low[0][:, cols], z0_low[1][:, cols])
         out_rows = out.rearrange("(n p) t -> p n t", p=P)
         last_bias = bias_sb[1][PACK - 1]
 
@@ -365,30 +376,40 @@ def tile_list_grain_boundary_segregation_kernel(
         def quantize_w4_late(pair):
             own = slice(N // 2 * pair, N // 2 * (pair + 1))
             grouped = w4_grouped[1][:, own, :].rearrange("p c j -> p (c j)")
-            return quantize(grouped, N // 2, "w4_1%d" % pair, kib=60 + pair)
+            return quantize(grouped, N // 2, "w4_1%d" % pair, tag=("slot8", None)[pair], kib=(None, 60)[pair])
 
         def quantize_z1(cols):
             grouped = z[1][:, cols, :].rearrange("p c j -> p (c j)")
             return quantize(grouped, cols.stop - cols.start, "z1_%d" % cols.start)
 
-        bias_on_vector(slice(0, CHUNK // 2))
-        bias_on_scalar(slice(CHUNK // 2, CHUNK))
+        bias_on_vector(slice(0, FIRST_ON_VECTOR))
+        bias_on_scalar(slice(FIRST_ON_VECTOR, CHUNK))
         bias_on_scalar(slice(CHUNK, half))
         w4_late = [quantize_w4_late(0)]
         z1_q = {0: quantize_z1(slice(0, CHUNK))}
         w4_late.append(quantize_w4_late(1))
-        bias_on_vector(slice(half, T2))
         z1_q[CHUNK] = quantize_z1(slice(CHUNK, half))
-        z1_q[half] = quantize_z1(slice(half, T2))
+        z0_high = quantize_z0(slice(half, T2), kib=56)
+        late = [slice(half, half + CHUNK), slice(half + CHUNK, T2)]
+        for cols in late:
+            bias_on_vector(cols)
+        z1_q[half] = held([P, half], U32, "z1_late_codes"), held([P, half], U8, "z1_late_scales")
+        for cols in late:
+            own = slice(cols.start - half, cols.stop - half)
+            nc.vector.quantize_mx(
+                out=z1_q[half][0][:, own].bitcast(FP8X4), scales=z1_q[half][1][:, own],
+                in_=z[1][:, cols, :].rearrange("p c j -> p (c j)"),
+            )
         for index, (cols, tiles) in enumerate(banks):
+            if index == early:
+                for later in range(early, len(banks)):
+                    reader_pass(0, later, early_weights, z0_high[0][:], z0_high[1][:])
             reader_pass(1, index, late_weights, z1_q[cols.start][0][:], z1_q[cols.start][1][:])
             width = cols.stop - cols.start
-            result = held([P, len(tiles), width], F32, "result%d" % index, tag="slot%d" % (index + 1))
-            acc = accs[index][:].rearrange("p (h t) -> p h t", t=width)
-            pieces = [slice(h, h + 1) for h in range(len(tiles))] if index == 0 else [slice(0, len(tiles))]
-            for own in pieces:
-                if index in (4, 6):
-                    nc.vector.tensor_copy(result[:, own, :], acc[:, own, :])
-                else:
-                    nc.scalar.copy(result[:, own, :], acc[:, own, :])
-                nc.sync.dma_start(out_rows[:, tiles[0] + own.start : tiles[0] + own.stop, cols], result[:, own, :])
+            result = held([P, len(tiles), width], F32, "result%d" % index, tag="slot%d" % index)
+            acc = accs[index][:, : width * len(tiles)].rearrange("p (h t) -> p h t", t=width)
+            if index in (early, early + 2):
+                nc.vector.tensor_copy(result[:], acc)
+            else:
+                nc.scalar.copy(result[:], acc)
+            nc.sync.dma_start(out_rows[:, tiles[0] : tiles[-1] + 1, cols], result[:])

@@ -119,12 +119,16 @@ def tile_list_grain_boundary_segregation_kernel(
             return codes, scales
 
         tab_plane = held([P, T // 4], I32, "tab_plane")
-        w1_plane = placed([P, H // 4], I32, "w1_plane", 50.5)
+        w1_plane = held([P, H // 4], I32, "w1_plane")
         w3_plane = held([P, H // 4], I32, "w3_plane")
         tab2_plane = held([P, T // 4], I32, "tab2_plane")
         for cols in (slice(0, T // 8 + 1), slice(T // 8 + 1, T // 4)):
             nc.vector.memset(tab_plane[:, cols], 0)
         nc.gpsimd.memset(w1_plane[:], 0)
+
+        warm = held([P, 2], F32, "warm")
+        nc.vector.memset(warm[:, 0:1], 0.0)
+        nc.scalar.activation(warm[:, 1:2], warm[:, 0:1], ACT.Tanh)
 
         idx1 = load_list(offs, "idx1")
         gain_sb = load_row_values(gain, "gain_sb")
@@ -167,12 +171,14 @@ def tile_list_grain_boundary_segregation_kernel(
         w1_first = placed([P, 2, P // 2], U32, "w1_first", 70)
         w1_rest = placed([P, 2, PACK - 1, P // 2], U32, "w1_rest", 70)
         w1_pairs = w1_sb[:].bitcast(U32).rearrange("p (b m t) -> p b m t", b=2, t=PACK)
-        w1_sc = held([P, H], U8, "w1_sc")
+        sc_first = placed([P, 2, P // 2], U16, "sc_first", 72)
+        sc_rest = placed([P, 2, PACK - 1, P // 2], U16, "sc_rest", 72)
+        sc_pairs = w1_plane[:].bitcast(U16).rearrange("p (b m t) -> p b m t", b=2, t=PACK)
 
         def w1_operand(b, t):
-            i = PACK * b + t
             words = w1_first[:, b, :] if t == 0 else w1_rest[:, b, t - 1, :]
-            return words.bitcast(U8).bitcast(FP4X4), w1_sc[:, P * i : P * (i + 1)]
+            scales = sc_first[:, b, :] if t == 0 else sc_rest[:, b, t - 1, :]
+            return words.bitcast(U8).bitcast(FP4X4), scales.bitcast(U8)
 
         def gather_v(part, words, scales):
             nc.vector.tensor_copy(words[:], tab_sb[:].bitcast(U32).indirect(entries(idx1, part)))
@@ -184,9 +190,9 @@ def tile_list_grain_boundary_segregation_kernel(
         pages = {page: held([P, T2], F32, "page%d%d" % page) for page in bulk_order if page != cover}
 
         v_q = [gather_v(halves[0], placed([P, S // 2], U32, "v_words0", 76), placed([P, S // 2], U8, "v_scales0", 80))]
-        nc.vector.tensor_copy(w1_first[:], w1_pairs[:, :, :, 0])
-        reorder_pairs(nc.vector.tensor_copy, w1_sc[:].bitcast(U16), w1_plane[:].bitcast(U16), 8)
-        v_q.append(gather_v(halves[1], placed([P, S // 2], U32, "v_words1", 50), placed([P, S // 2], U8, "v_scales1", 51)))
+        v_q.append(gather_v(halves[1], held([P, S // 2], U32, "v_words1"), held([P, S // 2], U8, "v_scales1")))
+        nc.scalar.copy(w1_first[:], w1_pairs[:, :, :, 0])
+        nc.scalar.copy(sc_first[:], sc_pairs[:, :, :, 0])
 
         def multiply(page, part, index):
             codes, code_scales = w1_operand(*page)
@@ -221,6 +227,7 @@ def tile_list_grain_boundary_segregation_kernel(
                     weigh(values[:], response[:])
                 place_bulk((b, 0), half, values[:])
         nc.scalar.copy(w1_rest[:].rearrange("p b t m -> p b m t"), w1_pairs[:, :, :, 1:])
+        nc.scalar.copy(sc_rest[:].rearrange("p b t m -> p b m t"), sc_pairs[:, :, :, 1:])
 
         responses = {}
         for step, page in enumerate(bulk_order[2:], start=2):

@@ -151,6 +151,7 @@ def tile_list_grain_boundary_segregation_kernel(
         wg1_sb = [None] + load_site_slot(wg1, 1, "wg1_1")
         w2_raw = [load_w2(0)]
         wg1_sb = wg1_sb + load_site_slot(wg1, 2, "wg1_2")
+        wg1_sb = wg1_sb + load_site_slot(wg1, 3, "wg1_3")
         w2_raw.append(load_w2(1))
         for q in QUADRANTS:
             load_scale_rows(nc.sync, w3_plane, w3_scales, q)
@@ -160,10 +161,9 @@ def tile_list_grain_boundary_segregation_kernel(
         tab2_sb.append(load_words(tab2_words[1], placed([P, T], I32, "tab2_sb1", 36)))
         idx2 = load_list(offs2, "idx2")
         w4_raw = [load_w4(0, placed([P, PACK, N], F32, "w4_raw0", 28))]
-        wg1_sb = wg1_sb + load_site_slot(wg1, 3, "wg1_3")
-        w3_sb.append(load_w3(1))
         idx4 = load_list(offs4, "idx4")
         wg2_sb = load_site_slot(wg2, 0, "wg2_0") + load_site_slots(wg2, range(1, PACK), "wg2_rest")
+        w3_sb.append(load_w3(1))
         bias_sb = load_row_values(bias, "bias_sb")
         w4_raw.append(load_w4(1, held([P, PACK, N], F32, "w4_raw1")))
 
@@ -215,17 +215,20 @@ def tile_list_grain_boundary_segregation_kernel(
             nc.vector.tensor_copy(pages[page][:].indirect(entries(idx3, part)), values)
 
         for n, half in enumerate(halves):
+            made = []
             for b in range(2):
                 acc = multiply((b, 0), half, (b, 6 + b)[n])
                 response = held([P, S // 2], F32, "response0%d%d" % (b, n), tag=(None, "slot0", "slot1", "slot2")[2 * n + b])
                 values = held([P, S // 2], F32, "values0%d%d" % (b, n), tag=("slot0", "slot1")[b] if n else None)
                 nc.scalar.activation(response[:], acc[:, half], ACT.Tanh)
-                if n == 0 and b == 0:
-                    nc.vector.scalar_tensor_tensor(values[:], response[:], gain_sb[0][0], wg1_first[n], MULT, MULT)
+                if n == 0:
+                    nc.vector.scalar_tensor_tensor(values[:], response[:], gain_sb[b][0], wg1_first[n], MULT, MULT)
                 else:
                     apply_gain(values[:], wg1_first[n], gain_sb[b][0])
                     weigh(values[:], response[:])
-                place_bulk((b, 0), half, values[:])
+                made.append(values)
+            for b in range(2):
+                place_bulk((b, 0), half, made[b][:])
         nc.scalar.copy(w1_rest[:].rearrange("p b t m -> p b m t"), w1_pairs[:, :, :, 1:])
         nc.scalar.copy(sc_rest[:].rearrange("p b t m -> p b m t"), sc_pairs[:, :, :, 1:])
 
@@ -244,9 +247,10 @@ def tile_list_grain_boundary_segregation_kernel(
                 place_bulk(page, whole, weight[:])
 
         w2_grouped = [placed([P, 2, PACK * 512], BF16, "w2_grouped%d" % b, 68 + 12 * b) for b in range(2)]
-        w3_ord = [placed([P, 2, 512], U32, "w3_ord0", 76), held([P, 2, 512], U32, "w3_ord1")]
+        w3_ord = []
 
         def order_w3(b):
+            w3_ord.append(placed([P, 2, 512], U32, "w3_ord%d" % b, 76 - 4 * b))
             nc.scalar.copy(
                 w3_ord[b][:].rearrange("p a (t m e) -> p a t m e", t=PACK, e=2),
                 w3_sb[b][:].bitcast(U32).rearrange("p a (m t e) -> p a t m e", t=PACK, e=2),
@@ -269,22 +273,23 @@ def tile_list_grain_boundary_segregation_kernel(
         cover_values = placed([P, S], F32, "weight_cover", 72)
         apply_gain(cover_values[:], wg1_sb[cover[1]], gain_sb[cover[0]][cover[1]])
         weigh(cover_values[:], responses[cover][:])
-        last_weight = held([P, S], F32, "weight_last", tag="slot7")
+        last_weight = placed([P, S], F32, "weight_last", 48)
         apply_gain(last_weight[:], wg1_sb[last[1]], gain_sb[last[0]][last[1]])
         v2_scales = held([P, S], U8, "v2_scales", tag="slot4")
         nc.vector.tensor_copy(v2_scales[:], tab2_plane[:].bitcast(U8).indirect(idx2[:]))
         v2_words = placed([P, 2 * S], U32, "v2_words", 68)
-        for a in range(2):
-            nc.vector.tensor_copy(v2_words[:, S * a : S * (a + 1)], tab2_sb[a][:].bitcast(U32).indirect(idx2[:]))
+        for a, part in ((0, whole), (1, halves[0]), (1, halves[1])):
+            nc.vector.tensor_copy(
+                v2_words[:, S * a + part.start : S * a + part.stop], tab2_sb[a][:].bitcast(U32).indirect(entries(idx2, part)),
+            )
         w4_grouped = [held([P, N, PACK], BF16, "w4_grouped0")]
         nc.scalar.copy(
             w4_grouped[0][:].rearrange("p (c i) j -> p c j i", i=4), w4_raw[0][:].rearrange("p j (c i) -> p c j i", i=4),
         )
-        order_w3(1)
-        w2_q[1, 0] = quantize(w2_grouped[1][:, 0, :], 512, "w2_10", tag="tab2_sb0")
-        w4_q = [quantize(w4_grouped[0][:].rearrange("p c j -> p (c j)"), N, "w4_0")]
-        w2_q[1, 1] = quantize(w2_grouped[1][:, 1, :], 512, "w2_11", kib=32)
-        pages[cover] = held([P, T2], F32, "page_cover", tag="w4_grouped0")
+        w2_high = quantize(w2_grouped[1][:].rearrange("p a c -> p (a c)"), 2 * 512, "w2_1", tag="tab2_sb0")
+        for a in range(2):
+            w2_q[1, a] = [part[:, 512 * a : 512 * (a + 1)] for part in w2_high]
+        pages[cover] = held([P, T2], F32, "page_cover", tag="tab2_plane")
         place_bulk(cover, whole, cover_values[:])
 
         sums = placed([P, 4, PACK, S], F32, "sums", 0)
@@ -294,25 +299,29 @@ def tile_list_grain_boundary_segregation_kernel(
 
         def boundary_product(step):
             b, t = boundary_order[step]
-            accs = [bank(2 * step + n, "bnd_acc%d%d%d" % (b, t, n)) for n in range(2)]
-            for a in range(2):
-                cols = slice(P * t, P * (t + 1))
-                own = slice(512 * b + P * t, 512 * b + P * (t + 1))
-                operands = [(w2_q[b, a][0][:, cols], w2_q[b, a][1][:, cols]), (w3_ord[b][:, a, cols], w3_sc[4 * a :, own])]
-                for acc, (codes, scales) in zip(accs, operands):
-                    nc.tensor.matmul_mx(
-                        out=acc[:], lhsT=codes.bitcast(FP8X4), lhsT_scale=scales,
-                        rhs=v2_words[:, S * a : S * (a + 1)].bitcast(FP8X4), rhs_scale=v2_scales[4 * a :, :],
-                        start=a == 0, stop=a == 1,
-                    )
-            nc.scalar.copy(first[b][:, t, :], accs[0][:])
-            nc.scalar.copy(second[b][:, t, :], accs[1][:])
+            cols = slice(P * t, P * (t + 1))
+            own = slice(512 * b + P * t, 512 * b + P * (t + 1))
             weighed = placed([P, S], F32, "weighed%d" % step, 58)
-            nc.gpsimd.tensor_tensor(weighed[:], first[b][:, t, :], wg2_sb[t], MULT)
-            nc.gpsimd.tensor_tensor(second[b][:, t, :], weighed[:], second[b][:, t, :], MULT)
+            for n, part in enumerate(halves if step == 0 else [whole]):
+                accs = [bank(2 * (min(step, 1) + step + n) + k, "bnd_acc%d%d%d" % (step, n, k)) for k in range(2)]
+                for a in range(2):
+                    atoms = slice(S * a + part.start, S * a + part.stop)
+                    operands = [(w2_q[b, a][0][:, cols], w2_q[b, a][1][:, cols]), (w3_ord[b][:, a, cols], w3_sc[4 * a :, own])]
+                    for acc, (codes, scales) in zip(accs, operands):
+                        nc.tensor.matmul_mx(
+                            out=acc[:, part], lhsT=codes.bitcast(FP8X4), lhsT_scale=scales,
+                            rhs=v2_words[:, atoms].bitcast(FP8X4), rhs_scale=v2_scales[4 * a :, part],
+                            start=a == 0, stop=a == 1,
+                        )
+                nc.scalar.copy(first[b][:, t, part], accs[0][:, part])
+                nc.scalar.copy(second[b][:, t, part], accs[1][:, part])
+                nc.gpsimd.tensor_tensor(weighed[:, part], first[b][:, t, part], wg2_sb[t][:, part], MULT)
+                nc.gpsimd.tensor_tensor(second[b][:, t, part], weighed[:, part], second[b][:, t, part], MULT)
 
         ahead = 6
         for step in range(ahead):
+            if step == PACK:
+                order_w3(1)
             boundary_product(step)
         pairs = placed([P, 2, T2, 2], BF16, "pairs", 60)
         z = [held([P, T2, PACK], BF16, "z0", tag="tab_sb"), placed([P, T2, PACK], BF16, "z1", 80)]
@@ -341,7 +350,8 @@ def tile_list_grain_boundary_segregation_kernel(
         for part in halves:
             nc.gpsimd.tensor_tensor(final[:, part], responses[last][:, part], last_weight[:, part], MULT)
         place_bulk(last, halves[0], final[:, halves[0]])
-        z0_low = quantize_z0(slice(0, half), tag="slot7")
+        w4_q = [quantize(w4_grouped[0][:].rearrange("p c j -> p (c j)"), N, "w4_0", kib=46.5)]
+        z0_low = quantize_z0(slice(0, half), kib=48.5)
         place_bulk(last, halves[1], final[:, halves[1]])
 
         banks = [(slice(0, CHUNK), tiles) for tiles in (range(0, 1), range(1, 2), range(2, 4))]

@@ -63,8 +63,9 @@ def tile_list_grain_boundary_segregation_kernel(
             rows = 4 * source.shape[0]
             queue.dma_start(plane[QUAD * q : QUAD * q + rows, :], source[:, 4 * q : 4 * q + 4, :].bitcast(I32))
 
-        def load_site_slot(source, t, name, part=slice(0, S)):
-            tile = held([P, part.stop - part.start], F32, name)
+        def load_site_slot(source, t, name, part=slice(0, S), kib=None):
+            shape = [P, part.stop - part.start]
+            tile = held(shape, F32, name) if kib is None else placed(shape, F32, name, kib)
             rows = source.rearrange("(m t e) j -> t m e j", t=PACK, e=2)[t][:, :, part]
             for q in QUADRANTS:
                 nc.sync.dma_start(tile[QUAD * q : QUAD * (q + 1)], rows)
@@ -86,13 +87,11 @@ def tile_list_grain_boundary_segregation_kernel(
                 nc.sync.dma_start(tile[e:P:2, :, 0:7], runs[:, :, e : e + 7])
             return [[tile[:, b, 2 * t : 2 * t + 1] for t in range(PACK)] for b in range(2)]
 
-        def load_w2(a):
-            tile = placed([P, PACK, H], F32, "w2_raw%d" % a, 16 * (1 - a))
-            nc.sync.dma_start(tile[:], w2[K_PASS * a : K_PASS * (a + 1), :].rearrange("(p j) c -> p j c", j=PACK))
-            return tile
+        def load_w2(a, own):
+            rows = w2[K_PASS * a : K_PASS * (a + 1), :].rearrange("(p j) c -> p j c", j=PACK)
+            nc.sync.dma_start(w2_raw[a][:, own, :], rows[:, own, :])
 
-        def load_w3(b):
-            tile = held([P, 2, 512], I32, "w3_sb%d" % b)
+        def load_w3(b, tile):
             words = w3_words[:, :, 512 * b : 512 * (b + 1), :].rearrange("a p c i -> p a (c i)")
             nc.sync.dma_start(tile[:], words.bitcast(I32))
             return tile
@@ -147,23 +146,24 @@ def tile_list_grain_boundary_segregation_kernel(
         wg1_first = load_site_slot(wg1, 0, "wg1_0a", halves[0])
         idx3 = load_list(offs3, "idx3")
         wg1_first = wg1_first + load_site_slot(wg1, 0, "wg1_0b", halves[1])
-        w3_sb = [load_w3(0)]
+        w2_raw = [placed([P, PACK, H], F32, "w2_raw%d" % a, 16 * (1 - a)) for a in range(2)]
+        w3_sb = [load_w3(0, held([P, 2, 512], I32, "w3_sb0"))]
         wg1_sb = [None] + load_site_slot(wg1, 1, "wg1_1")
-        w2_raw = [load_w2(0)]
+        load_w2(0, slice(0, PACK))
         wg1_sb = wg1_sb + load_site_slot(wg1, 2, "wg1_2")
-        wg1_sb = wg1_sb + load_site_slot(wg1, 3, "wg1_3")
-        w2_raw.append(load_w2(1))
+        wg1_sb = wg1_sb + load_site_slot(wg1, 3, "wg1_3", kib=106)
+        load_w2(1, slice(0, PACK))
         for q in QUADRANTS:
             load_scale_rows(nc.sync, w3_plane, w3_scales, q)
-        tab2_sb = [load_words(tab2_words[0], held([P, T], I32, "tab2_sb0"))]
+        tab2_sb = [load_words(tab2_words[0], placed([P, T], I32, "tab2_sb0", 96))]
         for q in QUADRANTS:
             load_scale_rows(nc.sync, tab2_plane, tab2_scales, q)
-        tab2_sb.append(load_words(tab2_words[1], placed([P, T], I32, "tab2_sb1", 36)))
+        tab2_sb.append(load_words(tab2_words[1], placed([P, T], I32, "tab2_sb1", 40)))
         idx2 = load_list(offs2, "idx2")
         w4_raw = [load_w4(0, placed([P, PACK, N], F32, "w4_raw0", 28))]
         idx4 = load_list(offs4, "idx4")
         wg2_sb = load_site_slot(wg2, 0, "wg2_0") + load_site_slots(wg2, range(1, PACK), "wg2_rest")
-        w3_sb.append(load_w3(1))
+        w3_sb.append(load_w3(1, held([P, 2, 512], I32, "w3_sb1")))
         bias_sb = load_row_values(bias, "bias_sb")
         w4_raw.append(load_w4(1, held([P, PACK, N], F32, "w4_raw1")))
 
@@ -232,25 +232,29 @@ def tile_list_grain_boundary_segregation_kernel(
         nc.scalar.copy(w1_rest[:].rearrange("p b t m -> p b m t"), w1_pairs[:, :, :, 1:])
         nc.scalar.copy(sc_rest[:].rearrange("p b t m -> p b m t"), sc_pairs[:, :, :, 1:])
 
-        responses = {}
+        def slot(n, name):
+            if n == 7:
+                return placed([P, S], F32, name, 90)
+            return held([P, S], F32, name, tag="slot%d" % n)
+
+        weights, responses = {}, {}
         for step, page in enumerate(bulk_order[2:], start=2):
             b, t = page
-            if page not in (cover, last):
-                weight = held([P, S], F32, "weight%d" % step, tag="slot%d" % step)
-                apply_gain(weight[:], wg1_sb[t], gain_sb[b][t])
+            weights[page] = slot(step, "weight%d" % step)
+            apply_gain(weights[page][:], wg1_sb[t], gain_sb[b][t])
             acc = multiply(page, whole, step)
-            tag = "early" if step == 5 else "slot%d" % (step + 1)
-            responses[page] = held([P, S], F32, "response%d" % step, tag=tag)
+            responses[page] = slot(step + 1, "response%d" % step)
             nc.scalar.activation(responses[page][:], acc[:], ACT.Tanh)
+            if page != last:
+                weigh(weights[page][:], responses[page][:])
             if page not in (cover, last):
-                weigh(weight[:], responses[page][:])
-                place_bulk(page, whole, weight[:])
+                place_bulk(page, whole, weights[page][:])
 
         w2_grouped = [placed([P, 2, PACK * 512], BF16, "w2_grouped%d" % b, 68 + 12 * b) for b in range(2)]
         w3_ord = []
 
         def order_w3(b):
-            w3_ord.append(placed([P, 2, 512], U32, "w3_ord%d" % b, 76 - 4 * b))
+            w3_ord.append(placed([P, 2, 512], U32, "w3_ord%d" % b, (76, 107)[b]))
             nc.scalar.copy(
                 w3_ord[b][:].rearrange("p a (t m e) -> p a t m e", t=PACK, e=2),
                 w3_sb[b][:].bitcast(U32).rearrange("p a (m t e) -> p a t m e", t=PACK, e=2),
@@ -268,29 +272,24 @@ def tile_list_grain_boundary_segregation_kernel(
         reorder_pairs(nc.scalar.copy, w3_sc[:].bitcast(U16), w3_plane[:].bitcast(U16), 8)
 
 
-        w2_low = quantize(w2_grouped[0][:].rearrange("p a c -> p (a c)"), 2 * 512, "w2_0", tag="early")
+        w2_low = quantize(w2_grouped[0][:].rearrange("p a c -> p (a c)"), 2 * 512, "w2_0", kib=107)
         w2_q = {(0, a): [part[:, 512 * a : 512 * (a + 1)] for part in w2_low] for a in range(2)}
-        cover_values = placed([P, S], F32, "weight_cover", 72)
-        apply_gain(cover_values[:], wg1_sb[cover[1]], gain_sb[cover[0]][cover[1]])
-        weigh(cover_values[:], responses[cover][:])
-        last_weight = placed([P, S], F32, "weight_last", 48)
-        apply_gain(last_weight[:], wg1_sb[last[1]], gain_sb[last[0]][last[1]])
-        v2_scales = held([P, S], U8, "v2_scales", tag="slot4")
+        v2_scales = placed([P, S], U8, "v2_scales", 106)
         nc.vector.tensor_copy(v2_scales[:], tab2_plane[:].bitcast(U8).indirect(idx2[:]))
         v2_words = placed([P, 2 * S], U32, "v2_words", 68)
         for a, part in ((0, whole), (1, halves[0]), (1, halves[1])):
             nc.vector.tensor_copy(
                 v2_words[:, S * a + part.start : S * a + part.stop], tab2_sb[a][:].bitcast(U32).indirect(entries(idx2, part)),
             )
-        w4_grouped = [held([P, N, PACK], BF16, "w4_grouped0")]
+        w4_early = held([P, N, PACK], BF16, "w4_early")
         nc.scalar.copy(
-            w4_grouped[0][:].rearrange("p (c i) j -> p c j i", i=4), w4_raw[0][:].rearrange("p j (c i) -> p c j i", i=4),
+            w4_early[:].rearrange("p (c i) j -> p c j i", i=4), w4_raw[0][:].rearrange("p j (c i) -> p c j i", i=4),
         )
-        w2_high = quantize(w2_grouped[1][:].rearrange("p a c -> p (a c)"), 2 * 512, "w2_1", tag="tab2_sb0")
+        w2_high = quantize(w2_grouped[1][:].rearrange("p a c -> p (a c)"), 2 * 512, "w2_1", kib=100)
         for a in range(2):
             w2_q[1, a] = [part[:, 512 * a : 512 * (a + 1)] for part in w2_high]
-        pages[cover] = held([P, T2], F32, "page_cover", tag="tab2_plane")
-        place_bulk(cover, whole, cover_values[:])
+        pages[cover] = placed([P, T2], F32, "page_cover", 96)
+        place_bulk(cover, whole, weights[cover][:])
 
         sums = placed([P, 4, PACK, S], F32, "sums", 0)
         first = [sums[:, b] for b in range(2)]
@@ -339,8 +338,8 @@ def tile_list_grain_boundary_segregation_kernel(
             if step + ahead < len(boundary_order):
                 boundary_product(step + ahead)
 
-        w4_grouped.append(placed([P, N, PACK], BF16, "w4_grouped1", 54.5))
-        nc.gpsimd.tensor_scalar(w4_grouped[1][:], w4_raw[1][:].rearrange("p j c -> p c j"), 1.0, 0.0, MULT, ADD)
+        w4_late_grouped = placed([P, N, PACK], BF16, "w4_grouped1", 54.5)
+        nc.gpsimd.tensor_scalar(w4_late_grouped[:], w4_raw[1][:].rearrange("p j c -> p c j"), 1.0, 0.0, MULT, ADD)
         half = T2 // 2
 
         def quantize_z0(cols, tag=None, kib=None):
@@ -348,10 +347,10 @@ def tile_list_grain_boundary_segregation_kernel(
 
         final = placed([P, S], F32, "final", 59)
         for part in halves:
-            nc.gpsimd.tensor_tensor(final[:, part], responses[last][:, part], last_weight[:, part], MULT)
+            nc.gpsimd.tensor_tensor(final[:, part], responses[last][:, part], weights[last][:, part], MULT)
         place_bulk(last, halves[0], final[:, halves[0]])
-        w4_q = [quantize(w4_grouped[0][:].rearrange("p c j -> p (c j)"), N, "w4_0", kib=46.5)]
-        z0_low = quantize_z0(slice(0, half), kib=48.5)
+        w4_q = quantize(w4_early[:].rearrange("p c j -> p (c j)"), N, "w4_0", kib=88.5)
+        z0_low = quantize_z0(slice(0, half), kib=90.5)
         place_bulk(last, halves[1], final[:, halves[1]])
 
         banks = [(slice(0, CHUNK), tiles) for tiles in (range(0, 1), range(1, 2), range(2, 4))]
@@ -374,7 +373,7 @@ def tile_list_grain_boundary_segregation_kernel(
                 )
 
         def early_weights(n):
-            return [part[:, P * n : P * (n + 1)] for part in w4_q[0]]
+            return [part[:, P * n : P * (n + 1)] for part in w4_q]
 
         def late_weights(n):
             return [part[:, P * (n % 2) : P * (n % 2 + 1)] for part in w4_late[n // 2]]
@@ -392,7 +391,7 @@ def tile_list_grain_boundary_segregation_kernel(
 
         def quantize_w4_late(pair):
             own = slice(N // 2 * pair, N // 2 * (pair + 1))
-            grouped = w4_grouped[1][:, own, :].rearrange("p c j -> p (c j)")
+            grouped = w4_late_grouped[:, own, :].rearrange("p c j -> p (c j)")
             return quantize(grouped, N // 2, "w4_1%d" % pair, tag=("slot8", None)[pair], kib=(None, 60)[pair])
 
         def quantize_z1(cols):

@@ -353,8 +353,8 @@ def tile_list_grain_boundary_segregation_kernel(
         z0_low = quantize_z0(slice(0, half), kib=90.5)
         place_bulk(last, halves[1], final[:, halves[1]])
 
-        banks = [(slice(0, CHUNK), tiles) for tiles in (range(0, 1), range(1, 2), range(2, 4))]
-        banks = banks + [(slice(CHUNK, half), range(2 * pair, 2 * pair + 2)) for pair in range(2)]
+        banks = [(slice(0, CHUNK if n < 2 else half), range(n, n + 1)) for n in range(N // P)]
+        banks = banks + [(slice(CHUNK, half), range(0, 2))]
         early = len(banks)
         banks = banks + [(slice(half, T2), range(n, n + 1)) for n in range(N // P)]
         accs = {}
@@ -394,33 +394,36 @@ def tile_list_grain_boundary_segregation_kernel(
             grouped = w4_late_grouped[:, own, :].rearrange("p c j -> p (c j)")
             return quantize(grouped, N // 2, "w4_1%d" % pair, tag=("slot8", None)[pair], kib=(None, 60)[pair])
 
+        z1_q = [(held([P, half], U32, "z1_codes%d" % n), held([P, half], U8, "z1_scales%d" % n)) for n in range(2)]
+
+        def z1_operand(cols):
+            side = cols.start // half
+            return [part[:, cols.start - side * half : cols.stop - side * half] for part in z1_q[side]]
+
         def quantize_z1(cols):
-            grouped = z[1][:, cols, :].rearrange("p c j -> p (c j)")
-            return quantize(grouped, cols.stop - cols.start, "z1_%d" % cols.start)
+            codes, scales = z1_operand(cols)
+            nc.vector.quantize_mx(
+                out=codes.bitcast(FP8X4), scales=scales, in_=z[1][:, cols, :].rearrange("p c j -> p (c j)"),
+            )
 
         bias_on_vector(slice(0, FIRST_ON_VECTOR))
         bias_on_scalar(slice(FIRST_ON_VECTOR, CHUNK))
         bias_on_scalar(slice(CHUNK, half))
         w4_late = [quantize_w4_late(0)]
-        z1_q = {0: quantize_z1(slice(0, CHUNK))}
+        quantize_z1(slice(0, CHUNK))
         w4_late.append(quantize_w4_late(1))
-        z1_q[CHUNK] = quantize_z1(slice(CHUNK, half))
+        quantize_z1(slice(CHUNK, half))
         z0_high = quantize_z0(slice(half, T2), kib=56)
         late = [slice(half, half + CHUNK), slice(half + CHUNK, T2)]
         for cols in late:
             bias_on_vector(cols)
-        z1_q[half] = held([P, half], U32, "z1_late_codes"), held([P, half], U8, "z1_late_scales")
         for cols in late:
-            own = slice(cols.start - half, cols.stop - half)
-            nc.vector.quantize_mx(
-                out=z1_q[half][0][:, own].bitcast(FP8X4), scales=z1_q[half][1][:, own],
-                in_=z[1][:, cols, :].rearrange("p c j -> p (c j)"),
-            )
+            quantize_z1(cols)
         for index, (cols, tiles) in enumerate(banks):
             if index == early:
                 for later in range(early, len(banks)):
                     reader_pass(0, later, early_weights, z0_high[0][:], z0_high[1][:])
-            reader_pass(1, index, late_weights, z1_q[cols.start][0][:], z1_q[cols.start][1][:])
+            reader_pass(1, index, late_weights, *z1_operand(cols))
             width = cols.stop - cols.start
             result = held([P, len(tiles), width], F32, "result%d" % index, tag="slot%d" % index)
             acc = accs[index][:, : width * len(tiles)].rearrange("p (h t) -> p h t", t=width)

@@ -125,10 +125,6 @@ def tile_list_grain_boundary_segregation_kernel(
             nc.vector.memset(tab_plane[:, cols], 0)
         nc.gpsimd.memset(w1_plane[:], 0)
 
-        warm = held([P, 2], F32, "warm")
-        nc.vector.memset(warm[:, 0:1], 0.0)
-        nc.scalar.activation(warm[:, 1:2], warm[:, 0:1], ACT.Tanh)
-
         idx1 = load_list(offs, "idx1")
         gain_sb = load_row_values(gain, "gain_sb")
         tab_sb = load_words(tab_words[0], held([P, T], I32, "tab_sb"))

from contextlib import ExitStack

import concourse.mybir as mybir

K, K2, T, S, H, N, T2 = 512, 1024, 2048, 512, 1024, 512, 1024
FLOPS = 2 * (K * H * S + 2 * K2 * H * S + H * N * T2)

F32 = mybir.dt.float32
BF16 = mybir.dt.bfloat16
I32 = mybir.dt.int32
U32 = mybir.dt.uint32
U16 = mybir.dt.uint16
U8 = mybir.dt.uint8
FP8X4 = mybir.dt.float8_e4m3fn_x4
FP4X4 = mybir.dt.float4_e2m1fn_x4
ACT = mybir.ActivationFunctionType
MULT = mybir.AluOpType.mult
ADD = mybir.AluOpType.add

P = 128
PACK = 4
K_PASS = P * PACK
QUAD = 32
BANK = 512
CHUNK = 256
FIRST_ON_VECTOR = 176
QUADRANTS = (0, 2, 1, 3)


def tile_list_grain_boundary_segregation_kernel(
    tc, tab_words, tab_scales, tab2_words, tab2_scales, offs, offs2, offs3, offs4,
    w1_words, w1_scales, w2, w3_words, w3_scales, gain, wg1, wg2, bias, w4, out,
):
    nc = tc.nc
    with ExitStack() as ctx:
        lists = ctx.enter_context(tc.tile_pool(name="lists", bufs=1))
        keep = ctx.enter_context(tc.tile_pool(name="keep", bufs=1))
        shared = ctx.enter_context(tc.tile_pool(name="shared", bufs=1))
        psum = ctx.enter_context(tc.psum_pool(name="psum", bufs=1))

        def held(shape, dtype, name, tag=None):
            return keep.tile(shape, dtype, name=name, tag=tag or name, align_bytes=64)

        def placed(shape, dtype, name, kib):
            return shared.tile(shape, dtype, name=name, align_bytes=64, offset=int(1024 * kib))

        def bank(index, name):
            return psum.tile([P, BANK], F32, name=name, tag="bank%d" % (index % 8))

        def load_list(source, name):
            tile = lists.tile([P, S // 16], U16, name=name)
            nc.sync.dma_start(tile[:], source)
            return tile

        def entries(idx, part):
            return idx[:, part.start // 16 : part.stop // 16]

        def load_words(source, tile):
            nc.sync.dma_start(tile[:], source.rearrange("p c i -> p (c i)").bitcast(I32))
            return tile

        def load_scale_rows(queue, plane, source, q):
            rows = 4 * source.shape[0]
            queue.dma_start(plane[QUAD * q : QUAD * q + rows, :], source[:, 4 * q : 4 * q + 4, :].bitcast(I32))

        def load_site_slot(source, t, name, part=slice(0, S), kib=None):
            shape = [P, part.stop - part.start]
            tile = held(shape, F32, name) if kib is None else placed(shape, F32, name, kib)
            rows = source.rearrange("(m t e) j -> t m e j", t=PACK, e=2)[t][:, :, part]
            for q in QUADRANTS:
                nc.sync.dma_start(tile[QUAD * q : QUAD * (q + 1)], rows)
            return [tile[:]]


        def load_site_slots(source, slots, name):
            tile = held([P, len(slots), S], F32, name)
            rows = source.rearrange("(m t e) j -> e m t j", t=PACK, e=2)
            for e in range(2):
                for q in QUADRANTS:
                    nc.sync.dma_start(tile[QUAD * q + e : QUAD * (q + 1) : 2], rows[e][:, slots.start : slots.stop, :])
            return [tile[:, n, :] for n in range(len(slots))]

        def load_row_values(source, name):
            tile = held([P, 2, 8], F32, name)
            runs = source.rearrange("(b m x) -> m b x", b=2, x=8)
            for e in range(2):
                nc.sync.dma_start(tile[e:P:2, :, 0:7], runs[:, :, e : e + 7])
            return [[tile[:, b, 2 * t : 2 * t + 1] for t in range(PACK)] for b in range(2)]

        def load_w2(a, own):
            rows = w2[K_PASS * a : K_PASS * (a + 1), :].rearrange("(p j) c -> p j c", j=PACK)
            nc.sync.dma_start(w2_raw[a][:, own, :], rows[:, own, :])

        def load_w3(b, tile):
            words = w3_words[:, :, 512 * b : 512 * (b + 1), :].rearrange("a p c i -> p a (c i)")
            nc.sync.dma_start(tile[:], words.bitcast(I32))
            return tile

        def load_w4(a, tile):
            rows = w4[K_PASS * a : K_PASS * (a + 1), :].rearrange("(m t e) c -> e m t c", t=PACK, e=2)
            for e in range(2):
                nc.sync.dma_start(tile[e:P:2], rows[e])
            return tile

        def reorder_pairs(copy, dst, src, line):
            copy(
                dst.rearrange("p (b t m i) -> p b m t i", t=PACK, m=P // 2 // line, i=line),
                src.rearrange("p (b m i t) -> p b m t i", t=PACK, m=P // 2 // line, i=line),
            )

        def quantize(grouped, columns, name, tag=None, kib=None):
            if kib is None:
                codes = held([P, columns], U32, name + "_codes", tag=tag)
            else:
                codes = placed([P, columns], U32, name + "_codes", kib)
            scales = held([P, columns], U8, name + "_scales")
            nc.vector.quantize_mx(out=codes[:].bitcast(FP8X4), scales=scales[:], in_=grouped)
            return codes, scales

        tab_plane = held([P, T // 4], I32, "tab_plane")
        w1_plane = held([P, H // 4], I32, "w1_plane")
        w3_plane = held([P, H // 4], I32, "w3_plane")
        tab2_plane = held([P, T // 4], I32, "tab2_plane")
        for cols in (slice(0, T // 8 + 1), slice(T // 8 + 1, T // 4)):
            nc.vector.memset(tab_plane[:, cols], 0)
        nc.gpsimd.memset(w1_plane[:], 0)

        idx1 = load_list(offs, "idx1")
        gain_sb = load_row_values(gain, "gain_sb")
        tab_sb = load_words(tab_words[0], held([P, T], I32, "tab_sb"))
        for q in QUADRANTS:
            load_scale_rows(nc.sync, tab_plane, tab_scales, q)
        w1_sb = held([P, H // 2], I32, "w1_sb")
        nc.sync.dma_start(w1_sb[:], w1_words[0].bitcast(I32))
        for q in QUADRANTS[:2]:
            load_scale_rows(nc.sync, w1_plane, w1_scales, q)
        for q in QUADRANTS[2:]:
            load_scale_rows(nc.gpsimd, w1_plane, w1_scales, q)
        for plane in (tab2_plane, w3_plane):
            nc.gpsimd.memset(plane[:], 0)
        halves = [slice(0, S // 2), slice(S // 2, S)]
        wg1_first = load_site_slot(wg1, 0, "wg1_0a", halves[0])
        idx3 = load_list(offs3, "idx3")
        wg1_first = wg1_first + load_site_slot(wg1, 0, "wg1_0b", halves[1])
        w2_raw = [placed([P, PACK, H], F32, "w2_raw%d" % a, 16 * (1 - a)) for a in range(2)]
        w3_sb = [load_w3(0, held([P, 2, 512], I32, "w3_sb0"))]
        wg1_sb = [None] + load_site_slot(wg1, 1, "wg1_1")
        load_w2(0, slice(0, PACK))
        wg1_sb = wg1_sb + load_site_slot(wg1, 2, "wg1_2")
        wg1_sb = wg1_sb + load_site_slot(wg1, 3, "wg1_3", kib=106)
        load_w2(1, slice(0, PACK))
        for q in QUADRANTS:
            load_scale_rows(nc.sync, w3_plane, w3_scales, q)
        tab2_sb = [load_words(tab2_words[0], placed([P, T], I32, "tab2_sb0", 96))]
        for q in QUADRANTS:
            load_scale_rows(nc.sync, tab2_plane, tab2_scales, q)
        tab2_sb.append(load_words(tab2_words[1], placed([P, T], I32, "tab2_sb1", 40)))
        idx2 = load_list(offs2, "idx2")
        w4_raw = [load_w4(0, placed([P, PACK, N], F32, "w4_raw0", 28))]
        idx4 = load_list(offs4, "idx4")
        wg2_sb = load_site_slot(wg2, 0, "wg2_0") + load_site_slots(wg2, range(1, PACK), "wg2_rest")
        w3_sb.append(load_w3(1, held([P, 2, 512], I32, "w3_sb1")))
        bias_sb = load_row_values(bias, "bias_sb")
        w4_raw.append(load_w4(1, held([P, PACK, N], F32, "w4_raw1")))

        whole = slice(0, S)
        w1_first = placed([P, 2, P // 2], U32, "w1_first", 70)
        w1_rest = placed([P, 2, PACK - 1, P // 2], U32, "w1_rest", 70)
        w1_pairs = w1_sb[:].bitcast(U32).rearrange("p (b m t) -> p b m t", b=2, t=PACK)
        sc_first = placed([P, 2, P // 2], U16, "sc_first", 72)
        sc_rest = placed([P, 2, PACK - 1, P // 2], U16, "sc_rest", 72)
        sc_pairs = w1_plane[:].bitcast(U16).rearrange("p (b m t) -> p b m t", b=2, t=PACK)

        def w1_operand(b, t):
            words = w1_first[:, b, :] if t == 0 else w1_rest[:, b, t - 1, :]
            scales = sc_first[:, b, :] if t == 0 else sc_rest[:, b, t - 1, :]
            return words.bitcast(U8).bitcast(FP4X4), scales.bitcast(U8)

        def gather_v(part, words, scales):
            nc.vector.tensor_copy(words[:], tab_sb[:].bitcast(U32).indirect(entries(idx1, part)))
            nc.vector.tensor_copy(scales[:], tab_plane[:].bitcast(U8).indirect(entries(idx1, part)))
            return words, scales

        bulk_order = [(b, t) for t in range(PACK) for b in range(2)]
        cover, last = bulk_order[-2:]
        pages = {page: held([P, T2], F32, "page%d%d" % page) for page in bulk_order if page != cover}

        v_q = [gather_v(halves[0], placed([P, S // 2], U32, "v_words0", 76), placed([P, S // 2], U8, "v_scales0", 80))]
        v_q.append(gather_v(halves[1], held([P, S // 2], U32, "v_words1"), held([P, S // 2], U8, "v_scales1")))
        nc.scalar.copy(w1_first[:], w1_pairs[:, :, :, 0])
        nc.scalar.copy(sc_first[:], sc_pairs[:, :, :, 0])

        def multiply(page, part, index):
            codes, code_scales = w1_operand(*page)
            acc = bank(index, "h1_acc%d%d_%d" % (*page, part.start))
            for half, (words, scales) in zip(halves, v_q):
                if part.start <= half.start and half.stop <= part.stop:
                    nc.tensor.matmul_mx(
                        out=acc[:, half], lhsT=codes, lhsT_scale=code_scales,
                        rhs=words[:].bitcast(FP8X4), rhs_scale=scales[:], start=True, stop=True,
                    )
            return acc

        def apply_gain(weight, site, row_gain):
            nc.gpsimd.tensor_scalar(weight, site, row_gain, 0.0, MULT, ADD)

        def weigh(weight, response):
            nc.gpsimd.tensor_tensor(weight, response, weight, MULT)

        def place_bulk(page, part, values):
            nc.vector.tensor_copy(pages[page][:].indirect(entries(idx3, part)), values)

        for n, half in enumerate(halves):
            made = []
            for b in range(2):
                acc = multiply((b, 0), half, (b, 6 + b)[n])
                response = held([P, S // 2], F32, "response0%d%d" % (b, n), tag=(None, "slot0", "slot1", "slot2")[2 * n + b])
                values = held([P, S // 2], F32, "values0%d%d" % (b, n), tag=("slot0", "slot1")[b] if n else None)
                nc.scalar.activation(response[:], acc[:, half], ACT.Tanh)
                if n == 0:
                    nc.vector.scalar_tensor_tensor(values[:], response[:], gain_sb[b][0], wg1_first[n], MULT, MULT)
                else:
                    apply_gain(values[:], wg1_first[n], gain_sb[b][0])
                    weigh(values[:], response[:])
                made.append(values)
            for b in range(2):
                place_bulk((b, 0), half, made[b][:])
        nc.scalar.copy(w1_rest[:].rearrange("p b t m -> p b m t"), w1_pairs[:, :, :, 1:])
        nc.scalar.copy(sc_rest[:].rearrange("p b t m -> p b m t"), sc_pairs[:, :, :, 1:])

        def slot(n, name):
            if n == 7:
                return placed([P, S], F32, name, 90)
            return held([P, S], F32, name, tag="slot%d" % n)

        weights, responses = {}, {}
        for step, page in enumerate(bulk_order[2:], start=2):
            b, t = page
            weights[page] = slot(step, "weight%d" % step)
            apply_gain(weights[page][:], wg1_sb[t], gain_sb[b][t])
            acc = multiply(page, whole, step)
            responses[page] = slot(step + 1, "response%d" % step)
            nc.scalar.activation(responses[page][:], acc[:], ACT.Tanh)
            if page != last:
                weigh(weights[page][:], responses[page][:])
            if page not in (cover, last):
                place_bulk(page, whole, weights[page][:])

        w2_grouped = [placed([P, 2, PACK * 512], BF16, "w2_grouped%d" % b, 68 + 12 * b) for b in range(2)]
        w3_ord = []

        def order_w3(b):
            w3_ord.append(placed([P, 2, 512], U32, "w3_ord%d" % b, (76, 107)[b]))
            nc.scalar.copy(
                w3_ord[b][:].rearrange("p a (t m e) -> p a t m e", t=PACK, e=2),
                w3_sb[b][:].bitcast(U32).rearrange("p a (m t e) -> p a t m e", t=PACK, e=2),
            )

        for a in range(2):
            for b in range(2):
                nc.scalar.copy(
                    w2_grouped[b][:, a, :].rearrange("p (t m e j) -> p m t e j", t=PACK, e=2, j=PACK),
                    w2_raw[a][:, :, 512 * b : 512 * (b + 1)].rearrange("p j (m t e) -> p m t e j", t=PACK, e=2),
                )
            if a == 0:
                order_w3(0)
        w3_sc = held([P, H], U8, "w3_sc")
        reorder_pairs(nc.scalar.copy, w3_sc[:].bitcast(U16), w3_plane[:].bitcast(U16), 8)


        w2_low = quantize(w2_grouped[0][:].rearrange("p a c -> p (a c)"), 2 * 512, "w2_0", kib=107)
        w2_q = {(0, a): [part[:, 512 * a : 512 * (a + 1)] for part in w2_low] for a in range(2)}
        v2_scales = placed([P, S], U8, "v2_scales", 106)
        nc.vector.tensor_copy(v2_scales[:], tab2_plane[:].bitcast(U8).indirect(idx2[:]))
        v2_words = placed([P, 2 * S], U32, "v2_words", 68)
        for a, part in ((0, whole), (1, halves[0]), (1, halves[1])):
            nc.vector.tensor_copy(
                v2_words[:, S * a + part.start : S * a + part.stop], tab2_sb[a][:].bitcast(U32).indirect(entries(idx2, part)),
            )
        w4_early = held([P, N, PACK], BF16, "w4_early")
        nc.scalar.copy(
            w4_early[:].rearrange("p (c i) j -> p c j i", i=4), w4_raw[0][:].rearrange("p j (c i) -> p c j i", i=4),
        )
        w2_high = quantize(w2_grouped[1][:].rearrange("p a c -> p (a c)"), 2 * 512, "w2_1", kib=100)
        for a in range(2):
            w2_q[1, a] = [part[:, 512 * a : 512 * (a + 1)] for part in w2_high]
        pages[cover] = placed([P, T2], F32, "page_cover", 96)
        place_bulk(cover, whole, weights[cover][:])

        sums = placed([P, 4, PACK, S], F32, "sums", 0)
        first = [sums[:, b] for b in range(2)]
        second = [sums[:, 2 + b] for b in range(2)]
        boundary_order = [(0, 0), (0, 1), (0, 2), (0, 3), (1, 2), (1, 0), (1, 3), (1, 1)]

        def boundary_product(step):
            b, t = boundary_order[step]
            cols = slice(P * t, P * (t + 1))
            own = slice(512 * b + P * t, 512 * b + P * (t + 1))
            weighed = placed([P, S], F32, "weighed%d" % step, 58)
            for n, part in enumerate(halves if step == 0 else [whole]):
                accs = [bank(2 * (min(step, 1) + step + n) + k, "bnd_acc%d%d%d" % (step, n, k)) for k in range(2)]
                for a in range(2):
                    atoms = slice(S * a + part.start, S * a + part.stop)
                    operands = [(w2_q[b, a][0][:, cols], w2_q[b, a][1][:, cols]), (w3_ord[b][:, a, cols], w3_sc[4 * a :, own])]
                    for acc, (codes, scales) in zip(accs, operands):
                        nc.tensor.matmul_mx(
                            out=acc[:, part], lhsT=codes.bitcast(FP8X4), lhsT_scale=scales,
                            rhs=v2_words[:, atoms].bitcast(FP8X4), rhs_scale=v2_scales[4 * a :, part],
                            start=a == 0, stop=a == 1,
                        )
                nc.scalar.copy(first[b][:, t, part], accs[0][:, part])
                nc.scalar.copy(second[b][:, t, part], accs[1][:, part])
                nc.gpsimd.tensor_tensor(weighed[:, part], first[b][:, t, part], wg2_sb[t][:, part], MULT)
                nc.gpsimd.tensor_tensor(second[b][:, t, part], weighed[:, part], second[b][:, t, part], MULT)

        ahead = 6
        for step in range(ahead):
            if step == PACK:
                order_w3(1)
            boundary_product(step)
        pairs = placed([P, 2, T2, 2], BF16, "pairs", 60)
        z = [held([P, T2, PACK], BF16, "z0", tag="tab_sb"), placed([P, T2, PACK], BF16, "z1", 80)]
        for step, page in enumerate(boundary_order):
            b, t = page
            nc.vector.tensor_copy(pages[page][:].indirect(idx4[:]), second[b][:, t, :])
            if page != last:
                target = pairs[:, t // 2, :, t % 2] if b == 0 else z[1][:, :, t]
                nc.scalar.activation(target, pages[page][:], ACT.Identity, bias=bias_sb[b][t])
            if page == (1, PACK - 2):
                nc.scalar.copy(
                    z[0][:].rearrange("p c j -> p (c j)").bitcast(U32).rearrange("p (c u) -> p c u", u=2),
                    pairs[:].rearrange("p u c e -> p (u c e)").bitcast(U32).rearrange("p (u c) -> p c u", u=2),
                )
            if step + ahead < len(boundary_order):
                boundary_product(step + ahead)

        w4_late_grouped = placed([P, N, PACK], BF16, "w4_grouped1", 54.5)
        nc.gpsimd.tensor_scalar(w4_late_grouped[:], w4_raw[1][:].rearrange("p j c -> p c j"), 1.0, 0.0, MULT, ADD)
        half = T2 // 2

        def quantize_z0(cols, tag=None, kib=None):
            return quantize(z[0][:, cols, :].rearrange("p c j -> p (c j)"), half, "z0_%d" % cols.start, tag=tag, kib=kib)

        final = placed([P, S], F32, "final", 59)
        for part in halves:
            nc.gpsimd.tensor_tensor(final[:, part], responses[last][:, part], weights[last][:, part], MULT)
        place_bulk(last, halves[0], final[:, halves[0]])
        w4_q = quantize(w4_early[:].rearrange("p c j -> p (c j)"), N, "w4_0", kib=88.5)
        z0_low = quantize_z0(slice(0, half), kib=90.5)
        place_bulk(last, halves[1], final[:, halves[1]])

        banks = [(slice(0, CHUNK if n < 2 else half), range(n, n + 1)) for n in range(N // P)]
        banks = banks + [(slice(CHUNK, half), range(0, 2))]
        early = len(banks)
        banks = banks + [(slice(half, T2), range(n, n + 1)) for n in range(N // P)]
        accs = {}

        def reader_pass(b, index, weights, z_codes, z_sc):
            cols, tiles = banks[index]
            width = cols.stop - cols.start
            if b == 0:
                accs[index] = bank(index, "out_acc%d" % index)
            for h, n in enumerate(tiles):
                w_codes, w_sc = weights(n)
                nc.tensor.matmul_mx(
                    out=accs[index][:, width * h : width * (h + 1)], lhsT=w_codes.bitcast(FP8X4), lhsT_scale=w_sc,
                    rhs=z_codes.bitcast(FP8X4), rhs_scale=z_sc,
                    start=b == 0 and h == 0, stop=b == 1 and n == tiles[-1],
                )

        def early_weights(n):
            return [part[:, P * n : P * (n + 1)] for part in w4_q]

        def late_weights(n):
            return [part[:, P * (n % 2) : P * (n % 2 + 1)] for part in w4_late[n // 2]]

        for index, (cols, tiles) in enumerate(banks[:early]):
            reader_pass(0, index, early_weights, z0_low[0][:, cols], z0_low[1][:, cols])
        out_rows = out.rearrange("(n p) t -> p n t", p=P)
        last_bias = bias_sb[1][PACK - 1]

        def bias_on_vector(cols):
            nc.vector.tensor_scalar_add(z[1][:, cols, PACK - 1], pages[last][:, cols], last_bias)

        def bias_on_scalar(cols):
            nc.scalar.activation(z[1][:, cols, PACK - 1], pages[last][:, cols], ACT.Identity, bias=last_bias)

        def quantize_w4_late(pair):
            own = slice(N // 2 * pair, N // 2 * (pair + 1))
            grouped = w4_late_grouped[:, own, :].rearrange("p c j -> p (c j)")
            return quantize(grouped, N // 2, "w4_1%d" % pair, tag=("slot8", None)[pair], kib=(None, 60)[pair])

        z1_q = [(held([P, half], U32, "z1_codes%d" % n), held([P, half], U8, "z1_scales%d" % n)) for n in range(2)]

        def z1_operand(cols):
            side = cols.start // half
            return [part[:, cols.start - side * half : cols.stop - side * half] for part in z1_q[side]]

        def quantize_z1(cols):
            codes, scales = z1_operand(cols)
            nc.vector.quantize_mx(
                out=codes.bitcast(FP8X4), scales=scales, in_=z[1][:, cols, :].rearrange("p c j -> p (c j)"),
            )

        bias_on_vector(slice(0, FIRST_ON_VECTOR))
        bias_on_scalar(slice(FIRST_ON_VECTOR, CHUNK))
        bias_on_scalar(slice(CHUNK, half))
        w4_late = [quantize_w4_late(0)]
        quantize_z1(slice(0, CHUNK))
        w4_late.append(quantize_w4_late(1))
        quantize_z1(slice(CHUNK, half))
        z0_high = quantize_z0(slice(half, T2), kib=56)
        late = [slice(half, half + CHUNK), slice(half + CHUNK, T2)]
        for cols in late:
            bias_on_vector(cols)
        for cols in late:
            quantize_z1(cols)
        for index, (cols, tiles) in enumerate(banks):
            if index == early:
                for later in range(early, len(banks)):
                    reader_pass(0, later, early_weights, z0_high[0][:], z0_high[1][:])
            reader_pass(1, index, late_weights, *z1_operand(cols))
            width = cols.stop - cols.start
            result = held([P, len(tiles), width], F32, "result%d" % index, tag="slot%d" % index)
            acc = accs[index][:, : width * len(tiles)].rearrange("p (h t) -> p h t", t=width)
            if index in (early, early + 2):
                nc.vector.tensor_copy(result[:], acc)
            else:
                nc.scalar.copy(result[:], acc)
            nc.sync.dma_start(out_rows[:, tiles[0] : tiles[-1] + 1, cols], result[:])
